import numpy as np
import ml_dtypes


def mxq(x, axis, fmt="e4m3"):
    dtype, down = {"e4m3": (ml_dtypes.float8_e4m3fn, 7), "e5m2": (ml_dtypes.float8_e5m2, 14)}[fmt]
    v = np.moveaxis(np.asarray(x, np.float32).astype(ml_dtypes.bfloat16).astype(np.float64), axis, -1)
    blocks = v.reshape(v.shape[:-1] + (-1, 32))
    amax = np.abs(blocks).max(-1, keepdims=True)
    byte = np.maximum(np.where(amax > 0, np.frexp(amax)[1] - 1 + 127, 0) - down, 1)
    scale = np.exp2(byte - 127.0)
    codes = (blocks / scale).astype(np.float32).astype(dtype).astype(np.float64)
    return np.moveaxis((codes * scale).reshape(v.shape), -1, axis)


WIDE = False


def mx_kscale(k):
    if not WIDE:
        return np.ones(k)
    levels = np.array([10, -10, 5, -5, 0])
    if k % 512:
        return np.exp2(np.random.permutation(np.resize(levels, k // 32))).repeat(32)
    a = np.empty((k // 512, 16))
    for p in range(k // 512):
        a[p, :8] = np.random.permutation(np.resize(levels, 8))
        for g in range(8):
            far = levels[np.abs(levels - a[p, g]) >= 10]
            a[p, g + 8] = far[np.random.randint(len(far))]
    return np.exp2(a.ravel()).repeat(32)


def f64(x):
    return np.asarray(x).astype(np.float64)


def striped(idx):
    return np.tile(idx.reshape(-1, 16).T, (8, 1)).astype(np.uint16)


def unstriped(offs):
    return offs[:16].T.reshape(-1).astype(np.int64)


E2M1 = np.array([0.0, 0.5, 1.0, 1.5, 2.0, 3.0, 4.0, 6.0, -0.0, -0.5, -1.0, -1.5, -2.0, -3.0, -4.0, -6.0])


def pack_weight(w, fmt):
    k, n = w.shape
    w = f64(np.asarray(w, np.float32).astype(ml_dtypes.bfloat16)).reshape(k // 32, 32, n)
    amax = np.abs(w).max(1)
    if fmt == "e4m3":
        byte = np.frexp(amax)[1] - 1 + 127 - 7
    else:
        mant, ex = np.frexp(amax / 6.0)
        byte = np.where(mant > 0.5, ex, ex - 1) + 127
    byte = np.clip(np.where(amax > 0, byte, 1), 1, 254)
    scaled = (w * np.exp2(127.0 - byte)[:, None, :]).reshape(k, n).astype(np.float32)
    by_word = np.ascontiguousarray(scaled.reshape(k // 512, 128, 4, n).transpose(0, 1, 3, 2))
    if fmt == "e4m3":
        words = by_word.astype(ml_dtypes.float8_e4m3fn).view(np.uint8)
    else:
        c = by_word.astype(ml_dtypes.float4_e2m1fn).view(np.uint8) & 0xF
        words = (c[..., 0::2] | (c[..., 1::2] << 4)).reshape(k // 512, 128, 2 * n)
    return np.ascontiguousarray(words), np.ascontiguousarray(byte.astype(np.uint8).reshape(k // 512, 16, n))


def unpack_weight(words, scales, fmt):
    g, _, n = scales.shape
    words = np.ascontiguousarray(words).reshape(g, 128, n, -1)
    if fmt == "e4m3":
        vals = words.view(ml_dtypes.float8_e4m3fn).astype(np.float64)
    else:
        nib = np.empty((g, 128, n, 4), np.uint8)
        nib[..., 0::2] = words & 0xF
        nib[..., 1::2] = words >> 4
        vals = E2M1[nib]
    vals = vals * np.repeat(np.exp2(scales.astype(np.float64) - 127.0), 8, axis=1)[..., None]
    return vals.transpose(0, 1, 3, 2).reshape(g * 512, n)


def gelu(v):
    return 0.5 * v * (1.0 + np.tanh(np.sqrt(2.0 / np.pi) * (v + 0.044715 * v**3)))


K, K2, K3, H, N, T, T2, T3, S = 1024, 512, 1024, 1024, 512, 2048, 1024, 1024, 512

def setup_inputs():
    n = np.random.standard_normal
    s, s2, s3 = mx_kscale(K)[:, None], mx_kscale(K2)[:, None], mx_kscale(K3)[:, None]
    u = mx_kscale(H)[:, None]
    tab_words, tab_scales = pack_weight(n((K, T)) * s, "e4m3")
    tab2_words, tab2_scales = pack_weight(n((K2, T2)) * s2, "e4m3")
    tab3_words, tab3_scales = pack_weight(n((K3, T3)) * s3, "e2m1")
    w1_words, w1_scales = pack_weight(n((K, H)) / np.sqrt(K) / s * u.T, "e2m1")
    w3_words, w3_scales = pack_weight(n((K3, H)) / np.sqrt(K3) / s3, "e4m3")
    return {
        "tab_words": tab_words, "tab_scales": tab_scales,
        "tab2_words": tab2_words, "tab2_scales": tab2_scales,
        "tab3_words": tab3_words, "tab3_scales": tab3_scales,
        "offs": striped(np.random.permutation(T)[:S]),
        "offs2": striped(np.random.permutation(T2)[:S]),
        "offs3": striped(np.random.permutation(T3)[:S]),
        "w1_words": w1_words, "w1_scales": w1_scales,
        "w2": (n((K2, H)) / np.sqrt(K2) / s2 * u.T).astype(np.float32),
        "w3_words": w3_words, "w3_scales": w3_scales,
        "curv": (0.6 * n(H) * u[:, 0]).astype(np.float32),
        "wo": (n((H, N)) / np.sqrt(H) / u).astype(np.float32),
    }

def reference(tab_words, tab_scales, tab2_words, tab2_scales, tab3_words, tab3_scales, offs, offs2, offs3, w1_words, w1_scales, w2, w3_words, w3_scales, curv, wo):
    v = unpack_weight(tab_words, tab_scales, "e4m3")[:, unstriped(offs)]
    v2 = unpack_weight(tab2_words, tab2_scales, "e4m3")[:, unstriped(offs2)]
    v3 = unpack_weight(tab3_words, tab3_scales, "e2m1")[:, unstriped(offs3)]
    line = unpack_weight(w1_words, w1_scales, "e2m1").T @ v
    soil = mxq(f64(w2), 0, "e4m3").T @ v2
    weather = unpack_weight(w3_words, w3_scales, "e4m3").T @ v3
    h = line + soil * weather + f64(curv)[:, None] * np.square(weather)
    return mxq(f64(wo), 0, "e4m3").T @ mxq(h, 0, "e4m3")

@@ -1,0 +1,268 @@
+from contextlib import ExitStack
+
+import concourse.mybir as mybir
+from concourse.masks import make_identity
+
+K, K2, K3, H, N, T, T2, T3, S = 1024, 512, 1024, 1024, 512, 2048, 1024, 1024, 512
+FLOPS = 2 * S * (H * (K + K2 + K3) + N * H)
+
+F32 = mybir.dt.float32
+BF16 = mybir.dt.bfloat16
+I32 = mybir.dt.int32
+U32 = mybir.dt.uint32
+U16 = mybir.dt.uint16
+U8 = mybir.dt.uint8
+FP8X4 = mybir.dt.float8_e4m3fn_x4
+FP4X4 = mybir.dt.float4_e2m1fn_x4
+MULT = mybir.AluOpType.mult
+ADD = mybir.AluOpType.add
+
+P = 128
+GP_UNITS = ()
+
+
+def tile_list_wheat_reaction_norm_kernel(
+    tc, tab_words, tab_scales, tab2_words, tab2_scales, tab3_words, tab3_scales, offs, offs2, offs3,
+    w1_words, w1_scales, w2, w3_words, w3_scales, curv, wo, out,
+):
+    nc = tc.nc
+    with ExitStack() as ctx:
+        keep = ctx.enter_context(tc.tile_pool(name="keep", bufs=1))
+        psum = ctx.enter_context(tc.psum_pool(name="psum", bufs=2))
+
+        def sb(name, shape, dtype):
+            return keep.tile(shape, dtype, name=name, align_bytes=64)
+
+        list1 = sb("list1", [P, S // 16], U16)
+        list2 = sb("list2", [P, S // 16], U16)
+        list3 = sb("list3", [P, S // 16], U16)
+        t1w = [sb(f"t1w{a}", [P, T], I32) for a in range(2)]
+        t2w = sb("t2w", [P, T2], I32)
+        t3w = [sb(f"t3w{a}", [P, T3], U16) for a in range(2)]
+        t1s = sb("t1s", [P, T], U8)
+        t2s = sb("t2s", [P, T2], U8)
+        t3s = sb("t3s", [P, T3], U8)
+        g1w = [sb(f"g1w{a}", [P, S], U32) for a in range(2)]
+        g2w = sb("g2w", [P, S], U32)
+        g3w = [sb(f"g3w{a}", [P, S], U16) for a in range(2)]
+        g1s = [sb(f"g1s{a}", [P, S], U8) for a in range(2)]
+        g2s = sb("g2s", [P, S], U8)
+        g3s = [sb(f"g3s{a}", [P, S], U8) for a in range(2)]
+        w1raw = sb("w1raw", [P, 2, H // 2], I32)
+        w1p = sb("w1p", [P, 2, H // 2], I32)
+        w1sraw = sb("w1sraw", [P, 2, H // 4], I32)
+        w1sp = sb("w1sp", [P, 2, H], U8)
+        w3raw = [sb(f"w3raw{b}", [P, 2, 512], I32) for b in range(2)]
+        w3p = [sb(f"w3p{b}", [P, 2, 512], I32) for b in range(2)]
+        w3sraw = sb("w3sraw", [P, 2, H // 4], I32)
+        w3sp = sb("w3sp", [P, 2, H], U8)
+        w2raw = [sb(f"w2raw{b}", [P, 4, 512], F32) for b in range(2)]
+        w2h = [sb(f"w2h{b}", [P, 2048], BF16) for b in range(2)]
+        w2c = [sb(f"w2c{b}", [P, 512], U32) for b in range(2)]
+        w2s = [sb(f"w2s{b}", [P, 512], U8) for b in range(2)]
+        woraw = [sb(f"woraw{b}", [P, 4, N], F32) for b in range(2)]
+        woh = [keep.tile([P, 4 * N], BF16, name=f"woh{b}", tag=f"half{b}", align_bytes=64) for b in range(2)]
+        woc = [sb(f"woc{b}", [P, N], U32) for b in range(2)]
+        wos = [sb(f"wos{b}", [P, N], U8) for b in range(2)]
+        cvrows = sb("cvrows", [P, P], F32)
+        ident = sb("ident", [P, P], F32)
+        cv = sb("cv", [P, 8], F32)
+
+        for t in (t3s, t2s):
+            nc.vector.memset(t[:].bitcast(I32), 0)
+        nc.vector.memset(w3sraw[:], 0)
+        nc.vector.memset(t1s[:].bitcast(I32), 0)
+        nc.vector.memset(g3s[1][:].bitcast(I32), 0)
+        nc.vector.memset(g1s[1][:].bitcast(I32), 0)
+        nc.gpsimd.memset(cvrows[:], 0.0)
+        nc.gpsimd.memset(w1sraw[:], 0)
+
+        def words(dram, a):
+            return dram[a].rearrange("p c i -> p (c i)").bitcast(I32)
+
+        def load_table_scales(tile, dram):
+            passes = dram.shape[0]
+            rows = dram.bitcast(I32).rearrange("a (q r) c -> r q a c", r=4)
+            for r in range(4):
+                nc.sync.dma_start(out=tile[r : P : 32 // passes, :].bitcast(I32), in_=rows[r])
+
+        def load_weight_scales(eng, tile, dram):
+            rows = dram.bitcast(I32).rearrange("a (q r) c -> q r a c", r=4)
+            for q in range(4):
+                eng.dma_start(out=tile[32 * q : 32 * q + 4, :, :], in_=rows[q])
+
+        def load_w2(b):
+            nc.sync.dma_start(out=w2raw[b][:], in_=w2[:, 512 * b : 512 * (b + 1)].rearrange("(p j) c -> p j c", j=4))
+
+        def load_w3(b):
+            src = w3_words.rearrange("a p c i -> p a (c i)")[:, :, 2048 * b : 2048 * (b + 1)].bitcast(I32)
+            nc.sync.dma_start(out=w3raw[b][:], in_=src)
+
+        def load_wo(b):
+            rows = wo[512 * b : 512 * (b + 1), :].rearrange("(g t i) n -> t g i n", t=4, i=8)
+            for t in range(4):
+                nc.sync.dma_start(out=woraw[b][:, t, :], in_=rows[t])
+
+        nc.sync.dma_start(list3[:], offs3)
+        for a in range(2):
+            nc.sync.dma_start(out=t3w[a][:].bitcast(I32), in_=tab3_words[a].bitcast(I32))
+        load_table_scales(t3s, tab3_scales)
+        nc.sync.dma_start(out=t2w[:], in_=words(tab2_words, 0))
+        nc.sync.dma_start(list2[:], offs2)
+        load_w2(0)
+        load_table_scales(t2s, tab2_scales)
+        load_w3(0)
+        nc.sync.dma_start(out=t1w[0][:], in_=words(tab_words, 0))
+        load_weight_scales(nc.sync, w3sraw, w3_scales)
+        nc.sync.dma_start(list1[:], offs)
+        load_w2(1)
+        load_table_scales(t1s, tab_scales)
+        nc.sync.dma_start(out=w1raw[:], in_=w1_words.rearrange("a p c -> p a c").bitcast(I32))
+        load_weight_scales(nc.sync, w1sraw, w1_scales)
+        load_w3(1)
+        nc.sync.dma_start(out=t1w[1][:], in_=words(tab_words, 1))
+        load_wo(0)
+        load_wo(1)
+
+        crows = curv.rearrange("(b g t i) -> b t g i", b=2, t=4, i=8)
+        for b in range(2):
+            nc.gpsimd.dma_start(out=cvrows[4 * b : 4 * b + 4, :].rearrange("t (g i) -> t g i", i=8), in_=crows[b])
+        make_identity(nc, ident[:])
+        cvt = psum.tile([P, P], F32, name="cvt", tag="outb")
+        nc.tensor.transpose(cvt[:], cvrows[:], ident[:])
+        nc.scalar.copy(out=cv[:], in_=cvt[:, 0:8])
+
+        def gather(dst, window, lst):
+            nc.vector.tensor_copy(dst[:], window.indirect(lst[:]))
+
+        def shift(g):
+            nc.gpsimd.dma_start(out=g[1][0:112, :].bitcast(I32), in_=g[0][16:128, :].bitcast(I32))
+
+        def permute(dst, src, run):
+            nc.vector.tensor_copy(
+                out=dst.rearrange("p a (b t g i) -> p (a b) t g i", t=4, g=16, i=run),
+                in_=src.rearrange("p a (b g t i) -> p (a b) t g i", t=4, g=16, i=run),
+            )
+
+        def cast_w2(b):
+            dst = w2h[b][:].rearrange("p (t g u i j) -> p t g u j i", t=4, g=16, u=2, i=4)
+            src = w2raw[b][:].rearrange("p j (g t u i) -> p t g u j i", t=4, u=2, i=4)
+            for t in range(4):
+                nc.scalar.copy(out=dst[:, t], in_=src[:, t])
+
+        def cast_wo(b):
+            nc.scalar.copy(
+                out=woh[b][:].rearrange("p (c i t) -> p c t i", i=4, t=4),
+                in_=woraw[b][:].rearrange("p t (c i) -> p c t i", i=4),
+            )
+
+        def quantize(codes, scales, values):
+            nc.vector.quantize_mx(out=codes[:].bitcast(FP8X4), scales=scales[:], in_=values)
+
+        curved = [sb(f"curved{b}", [P, 4, S], F32) for b in range(2)]
+
+        def slope_unit(b, t):
+            cols = slice(P * t, P * (t + 1))
+            hcols = slice(512 * b + P * t, 512 * b + P * (t + 1))
+            weather = psum.tile([P, S], F32, name="weather")
+            for a in range(2):
+                nc.tensor.matmul_mx(
+                    out=weather[:], lhsT=w3p[b][:, a, cols].bitcast(FP8X4), lhsT_scale=w3sp[:, a, hcols],
+                    rhs=g3w[a][:].bitcast(FP4X4), rhs_scale=g3s[a][:], start=(a == 0), stop=(a == 1),
+                )
+            soil = psum.tile([P, S], F32, name="soil")
+            nc.tensor.matmul_mx(
+                out=soil[:], lhsT=w2c[b][:, cols].bitcast(FP8X4), lhsT_scale=w2s[b][:, cols],
+                rhs=g2w[:].bitcast(FP8X4), rhs_scale=g2s[:], start=True, stop=True,
+            )
+            u = 4 * b + t
+            wsb = sb(f"wsb{u}", [P, S], F32)
+            nc.scalar.copy(out=wsb[:], in_=weather[:])
+            slope = sb(f"slope{u}", [P, S], F32)
+            nc.vector.scalar_tensor_tensor(slope[:], wsb[:], cv[:, u : u + 1], soil[:], MULT, ADD)
+            eng = nc.gpsimd if u in GP_UNITS else nc.vector
+            eng.tensor_tensor(curved[b][:, t, :], slope[:], wsb[:], MULT)
+
+        hc = {}
+        hs = {}
+
+        def level_unit(b, q, hh):
+            toks = slice(P * q, P * (q + 1))
+            line = psum.tile([P, 4, P], F32, name="line")
+            for t in range(4):
+                c0 = 512 * b + P * t
+                for a in range(2):
+                    nc.tensor.matmul_mx(
+                        out=line[:, t, :], lhsT=w1p[:, a, c0 // 2 : (c0 + P) // 2].bitcast(FP4X4),
+                        lhsT_scale=w1sp[:, a, c0 : c0 + P],
+                        rhs=g1w[a][:, toks].bitcast(FP8X4), rhs_scale=g1s[a][:, toks], start=(a == 0), stop=(a == 1),
+                    )
+            nc.vector.tensor_tensor(
+                hh.rearrange("p (c i t) -> p c t i", i=4, t=4),
+                line[:].rearrange("p t (c i) -> p c t i", i=4),
+                curved[b][:, :, toks].rearrange("p t (c i) -> p c t i", i=4),
+                ADD,
+            )
+            hc[b, q] = sb(f"hc{b}{q}", [P, P], U32)
+            hs[b, q] = sb(f"hs{b}{q}", [P, P], U8)
+
+        accs = {}
+
+        def out_pass(b, q):
+            if b == 0:
+                accs[q] = psum.tile([P, 4, P], F32, name=f"acc{q}", tag=("outb", "outb", "weather", "soil")[q])
+            acc = accs[q]
+            for m in range(4):
+                cols = slice(P * m, P * (m + 1))
+                nc.tensor.matmul_mx(
+                    out=acc[:, m, :], lhsT=woc[b][:, cols].bitcast(FP8X4), lhsT_scale=wos[b][:, cols],
+                    rhs=hc[b, q][:].bitcast(FP8X4), rhs_scale=hs[b, q][:],
+                    start=(b == 0 and m == 0), stop=(b == 1 and m == 3),
+                )
+
+        def store(q):
+            res = sb(f"res{q}", [P, 4, P], F32)
+            nc.scalar.copy(out=res[:], in_=accs[q][:])
+            nc.sync.dma_start(out=out[:, P * q : P * (q + 1)].rearrange("(m p) j -> p m j", p=P), in_=res[:])
+
+        gather(g3w[0], t3w[0][:], list3)
+        gather(g3s[0], t3s[:], list3)
+        shift(g3s)
+        gather(g3w[1], t3w[1][:], list3)
+        gather(g2w, t2w[:].bitcast(U32), list2)
+        gather(g2s, t2s[:], list2)
+        cast_w2(0)
+        permute(w3p[0][:], w3raw[0][:], 8)
+        quantize(w2c[0], w2s[0], w2h[0][:])
+        permute(w3sp[:].bitcast(I32), w3sraw[:], 2)
+        gather(g1w[0], t1w[0][:].bitcast(U32), list1)
+        gather(g1s[0], t1s[:], list1)
+        shift(g1s)
+        for t in range(4):
+            slope_unit(0, t)
+        cast_w2(1)
+        quantize(w2c[1], w2s[1], w2h[1][:])
+        permute(w1p[:], w1raw[:], 4)
+        permute(w1sp[:].bitcast(I32), w1sraw[:], 2)
+        permute(w3p[1][:], w3raw[1][:], 8)
+        gather(g1w[1], t1w[1][:].bitcast(U32), list1)
+        h0 = sb("h0", [P, 4, 4 * P], BF16)
+        for t in range(4):
+            slope_unit(1, t)
+            level_unit(0, t, h0[:, t, :])
+        for b in range(2):
+            cast_wo(b)
+        for q in range(4):
+            quantize(hc[0, q], hs[0, q], h0[:, q, :])
+        for b in range(2):
+            quantize(woc[b], wos[b], woh[b][:])
+        for q in range(4):
+            out_pass(0, q)
+        h1 = keep.tile([P, 4, 4 * P], BF16, name="h1", tag="half1", align_bytes=64)
+        level_unit(1, 0, h1[:, 0, :])
+        for q in range(4):
+            if q < 3:
+                level_unit(1, q + 1, h1[:, q + 1, :])
+            quantize(hc[1, q], hs[1, q], h1[:, q, :])
+            out_pass(1, q)
+            store(q)

@@ -18,7 +18,6 @@ MULT = mybir.AluOpType.mult
 ADD = mybir.AluOpType.add
 
 P = 128
-GP_UNITS = ()
 
 
 def tile_list_wheat_reaction_norm_kernel(
@@ -28,7 +27,7 @@ def tile_list_wheat_reaction_norm_kernel(
     nc = tc.nc
     with ExitStack() as ctx:
         keep = ctx.enter_context(tc.tile_pool(name="keep", bufs=1))
-        psum = ctx.enter_context(tc.psum_pool(name="psum", bufs=2))
+        psum = ctx.enter_context(tc.psum_pool(name="psum", bufs=4))
 
         def sb(name, shape, dtype):
             return keep.tile(shape, dtype, name=name, align_bytes=64)
@@ -41,7 +40,7 @@ def tile_list_wheat_reaction_norm_kernel(
         t3w = [sb(f"t3w{a}", [P, T3], U16) for a in range(2)]
         t1s = sb("t1s", [P, T], U8)
         t2s = sb("t2s", [P, T2], U8)
-        t3s = sb("t3s", [P, T3], U8)
+        t3s = sb("t3s", [P, 2, T3], U8)
         g1w = [sb(f"g1w{a}", [P, S], U32) for a in range(2)]
         g2w = sb("g2w", [P, S], U32)
         g3w = [sb(f"g3w{a}", [P, S], U16) for a in range(2)]
@@ -51,7 +50,6 @@ def tile_list_wheat_reaction_norm_kernel(
         w1raw = sb("w1raw", [P, 2, H // 2], I32)
         w1p = sb("w1p", [P, 2, H // 2], I32)
         w1sraw = sb("w1sraw", [P, 2, H // 4], I32)
-        w1sp = sb("w1sp", [P, 2, H], U8)
         w3raw = [sb(f"w3raw{b}", [P, 2, 512], I32) for b in range(2)]
         w3p = [sb(f"w3p{b}", [P, 2, 512], I32) for b in range(2)]
         w3sraw = sb("w3sraw", [P, 2, H // 4], I32)
@@ -67,15 +65,14 @@ def tile_list_wheat_reaction_norm_kernel(
         cvrows = sb("cvrows", [P, P], F32)
         ident = sb("ident", [P, P], F32)
         cv = sb("cv", [P, 8], F32)
-
-        for t in (t3s, t2s):
-            nc.vector.memset(t[:].bitcast(I32), 0)
-        nc.vector.memset(w3sraw[:], 0)
-        nc.vector.memset(t1s[:].bitcast(I32), 0)
-        nc.vector.memset(g3s[1][:].bitcast(I32), 0)
-        nc.vector.memset(g1s[1][:].bitcast(I32), 0)
         nc.gpsimd.memset(cvrows[:], 0.0)
-        nc.gpsimd.memset(w1sraw[:], 0)
+
+        nc.vector.memset(t3s[:].bitcast(I32), 0)
+        nc.vector.memset(w3sraw[:], 0)
+        nc.vector.memset(t2s[:].bitcast(I32), 0)
+        nc.vector.memset(t1s[:].bitcast(I32), 0)
+        nc.vector.memset(g1s[1][:].bitcast(I32), 0)
+        nc.vector.memset(w1sraw[:], 0)
 
         def words(dram, a):
             return dram[a].rearrange("p c i -> p (c i)").bitcast(I32)
@@ -84,7 +81,7 @@ def tile_list_wheat_reaction_norm_kernel(
             passes = dram.shape[0]
             rows = dram.bitcast(I32).rearrange("a (q r) c -> r q a c", r=4)
             for r in range(4):
-                nc.sync.dma_start(out=tile[r : P : 32 // passes, :].bitcast(I32), in_=rows[r])
+                nc.scalar.dma_start(out=tile[r : P : 32 // passes, :].bitcast(I32), in_=rows[r])
 
         def load_weight_scales(eng, tile, dram):
             rows = dram.bitcast(I32).rearrange("a (q r) c -> q r a c", r=4)
@@ -106,29 +103,28 @@ def tile_list_wheat_reaction_norm_kernel(
         nc.sync.dma_start(list3[:], offs3)
         for a in range(2):
             nc.sync.dma_start(out=t3w[a][:].bitcast(I32), in_=tab3_words[a].bitcast(I32))
-        load_table_scales(t3s, tab3_scales)
-        nc.sync.dma_start(out=t2w[:], in_=words(tab2_words, 0))
-        nc.sync.dma_start(list2[:], offs2)
         load_w2(0)
-        load_table_scales(t2s, tab2_scales)
         load_w3(0)
-        nc.sync.dma_start(out=t1w[0][:], in_=words(tab_words, 0))
-        load_weight_scales(nc.sync, w3sraw, w3_scales)
+        nc.sync.dma_start(list2[:], offs2)
+        nc.sync.dma_start(out=t2w[:], in_=words(tab2_words, 0))
         nc.sync.dma_start(list1[:], offs)
-        load_w2(1)
-        load_table_scales(t1s, tab_scales)
-        nc.sync.dma_start(out=w1raw[:], in_=w1_words.rearrange("a p c -> p a c").bitcast(I32))
-        load_weight_scales(nc.sync, w1sraw, w1_scales)
         load_w3(1)
+        nc.sync.dma_start(out=t1w[0][:], in_=words(tab_words, 0))
+        load_w2(1)
+        nc.sync.dma_start(out=w1raw[:], in_=w1_words.rearrange("a p c -> p a c").bitcast(I32))
         nc.sync.dma_start(out=t1w[1][:], in_=words(tab_words, 1))
         load_wo(0)
         load_wo(1)
+        load_weight_scales(nc.scalar, t3s[:].bitcast(I32), tab3_scales)
+        load_weight_scales(nc.scalar, w3sraw, w3_scales)
+        load_table_scales(t2s, tab2_scales)
 
         crows = curv.rearrange("(b g t i) -> b t g i", b=2, t=4, i=8)
         for b in range(2):
             nc.gpsimd.dma_start(out=cvrows[4 * b : 4 * b + 4, :].rearrange("t (g i) -> t g i", i=8), in_=crows[b])
         make_identity(nc, ident[:])
-        cvt = psum.tile([P, P], F32, name="cvt", tag="outb")
+        load_weight_scales(nc.gpsimd, w1sraw, w1_scales)
+        cvt = psum.tile([P, P], F32, name="cvt", tag="wl")
         nc.tensor.transpose(cvt[:], cvrows[:], ident[:])
         nc.scalar.copy(out=cv[:], in_=cvt[:, 0:8])
 
@@ -157,38 +153,38 @@ def tile_list_wheat_reaction_norm_kernel(
             )
 
         def quantize(codes, scales, values):
-            nc.vector.quantize_mx(out=codes[:].bitcast(FP8X4), scales=scales[:], in_=values)
+            nc.vector.quantize_mx(out=codes.bitcast(FP8X4), scales=scales, in_=values)
 
+        wsb = [sb(f"wsb{b}", [P, 4, S], F32) for b in range(2)]
+        slope = [keep.tile([P, 4, S], F32, name=f"slope{b}", tag=f"slope{b}", align_bytes=64) for b in range(2)]
         curved = [sb(f"curved{b}", [P, 4, S], F32) for b in range(2)]
 
         def slope_unit(b, t):
             cols = slice(P * t, P * (t + 1))
             hcols = slice(512 * b + P * t, 512 * b + P * (t + 1))
-            weather = psum.tile([P, S], F32, name="weather")
+            weather = psum.tile([P, S], F32, name="weather", tag="wl")
             for a in range(2):
                 nc.tensor.matmul_mx(
                     out=weather[:], lhsT=w3p[b][:, a, cols].bitcast(FP8X4), lhsT_scale=w3sp[:, a, hcols],
                     rhs=g3w[a][:].bitcast(FP4X4), rhs_scale=g3s[a][:], start=(a == 0), stop=(a == 1),
                 )
-            soil = psum.tile([P, S], F32, name="soil")
+            soil = psum.tile([P, S], F32, name="soil", tag="soil")
             nc.tensor.matmul_mx(
                 out=soil[:], lhsT=w2c[b][:, cols].bitcast(FP8X4), lhsT_scale=w2s[b][:, cols],
                 rhs=g2w[:].bitcast(FP8X4), rhs_scale=g2s[:], start=True, stop=True,
             )
-            u = 4 * b + t
-            wsb = sb(f"wsb{u}", [P, S], F32)
-            nc.scalar.copy(out=wsb[:], in_=weather[:])
-            slope = sb(f"slope{u}", [P, S], F32)
-            nc.vector.scalar_tensor_tensor(slope[:], wsb[:], cv[:, u : u + 1], soil[:], MULT, ADD)
-            eng = nc.gpsimd if u in GP_UNITS else nc.vector
-            eng.tensor_tensor(curved[b][:, t, :], slope[:], wsb[:], MULT)
+            nc.scalar.copy(out=wsb[b][:, t, :], in_=weather[:])
+            nc.vector.scalar_tensor_tensor(slope[b][:, t, :], wsb[b][:, t, :], cv[:, 4 * b + t : 4 * b + t + 1], soil[:], MULT, ADD)
 
-        hc = {}
-        hs = {}
+        def curve(b):
+            nc.vector.tensor_tensor(curved[b][:], slope[b][:], wsb[b][:], MULT)
 
-        def level_unit(b, q, hh):
+        hc = [sb(f"hc{b}", [P, S], U32) for b in range(2)]
+        hs = [sb(f"hs{b}", [P, S], U8) for b in range(2)]
+
+        def level_unit(b, q, hh, w1sp):
             toks = slice(P * q, P * (q + 1))
-            line = psum.tile([P, 4, P], F32, name="line")
+            line = psum.tile([P, 4, P], F32, name="line", tag="wl")
             for t in range(4):
                 c0 = 512 * b + P * t
                 for a in range(2):
@@ -203,66 +199,72 @@ def tile_list_wheat_reaction_norm_kernel(
                 curved[b][:, :, toks].rearrange("p t (c i) -> p c t i", i=4),
                 ADD,
             )
-            hc[b, q] = sb(f"hc{b}{q}", [P, P], U32)
-            hs[b, q] = sb(f"hs{b}{q}", [P, P], U8)
 
-        accs = {}
-
-        def out_pass(b, q):
-            if b == 0:
-                accs[q] = psum.tile([P, 4, P], F32, name=f"acc{q}", tag=("outb", "outb", "weather", "soil")[q])
-            acc = accs[q]
-            for m in range(4):
-                cols = slice(P * m, P * (m + 1))
+        def out_pass(b, q, acc, m0):
+            count = acc.shape[1]
+            for m in range(count):
+                cols = slice(P * (m0 + m), P * (m0 + m + 1))
                 nc.tensor.matmul_mx(
                     out=acc[:, m, :], lhsT=woc[b][:, cols].bitcast(FP8X4), lhsT_scale=wos[b][:, cols],
-                    rhs=hc[b, q][:].bitcast(FP8X4), rhs_scale=hs[b, q][:],
-                    start=(b == 0 and m == 0), stop=(b == 1 and m == 3),
+                    rhs=hc[b][:, P * q : P * (q + 1)].bitcast(FP8X4), rhs_scale=hs[b][:, P * q : P * (q + 1)],
+                    start=(b == 0 and m == 0), stop=(b == 1 and m == count - 1),
                 )
 
-        def store(q):
-            res = sb(f"res{q}", [P, 4, P], F32)
-            nc.scalar.copy(out=res[:], in_=accs[q][:])
-            nc.sync.dma_start(out=out[:, P * q : P * (q + 1)].rearrange("(m p) j -> p m j", p=P), in_=res[:])
+        out_rows = out.rearrange("(m p) j -> p m j", p=P)
+
+        def store(q, acc, m0, copy):
+            count = acc.shape[1]
+            res = sb(f"res{q}{m0}", [P, count, P], F32)
+            copy(out=res[:], in_=acc[:])
+            nc.sync.dma_start(out=out_rows[:, m0 : m0 + count, P * q : P * (q + 1)], in_=res[:])
 
         gather(g3w[0], t3w[0][:], list3)
-        gather(g3s[0], t3s[:], list3)
-        shift(g3s)
+        gather(g3s[0], t3s[:, 0, :], list3)
         gather(g3w[1], t3w[1][:], list3)
-        gather(g2w, t2w[:].bitcast(U32), list2)
-        gather(g2s, t2s[:], list2)
-        cast_w2(0)
-        permute(w3p[0][:], w3raw[0][:], 8)
-        quantize(w2c[0], w2s[0], w2h[0][:])
+        gather(g3s[1], t3s[:, 1, :], list3)
         permute(w3sp[:].bitcast(I32), w3sraw[:], 2)
-        gather(g1w[0], t1w[0][:].bitcast(U32), list1)
+        permute(w3p[0][:], w3raw[0][:], 8)
+        cast_w2(0)
+        load_table_scales(t1s, tab_scales)
+        gather(g2s, t2s[:], list2)
+        quantize(w2c[0][:], w2s[0][:], w2h[0][:])
+        gather(g2w, t2w[:].bitcast(U32), list2)
         gather(g1s[0], t1s[:], list1)
         shift(g1s)
+        permute(w3p[1][:], w3raw[1][:], 8)
+        gather(g1w[0], t1w[0][:].bitcast(U32), list1)
         for t in range(4):
             slope_unit(0, t)
         cast_w2(1)
-        quantize(w2c[1], w2s[1], w2h[1][:])
+        quantize(w2c[1][:], w2s[1][:], w2h[1][:])
         permute(w1p[:], w1raw[:], 4)
-        permute(w1sp[:].bitcast(I32), w1sraw[:], 2)
-        permute(w3p[1][:], w3raw[1][:], 8)
         gather(g1w[1], t1w[1][:].bitcast(U32), list1)
-        h0 = sb("h0", [P, 4, 4 * P], BF16)
+        curve(0)
+        w1sp = keep.tile([P, 2, H], U8, name="w1sp", tag="slope0", align_bytes=64)
+        permute(w1sp[:].bitcast(I32), w1sraw[:], 2)
         for t in range(4):
             slope_unit(1, t)
-            level_unit(0, t, h0[:, t, :])
+        h0 = sb("h0", [P, 4, 4 * P], BF16)
+        for q in range(4):
+            level_unit(0, q, h0[:, q, :], w1sp)
+        curve(1)
+        quantize(hc[0][:], hs[0][:], h0[:].rearrange("p q c -> p (q c)"))
         for b in range(2):
             cast_wo(b)
+            quantize(woc[b][:], wos[b][:], woh[b][:])
+        accs = [psum.tile([P, 4 if q < 3 else 2, P], F32, name=f"acc{q}", tag="soil") for q in range(4)]
         for q in range(4):
-            quantize(hc[0, q], hs[0, q], h0[:, q, :])
-        for b in range(2):
-            quantize(woc[b], wos[b], woh[b][:])
-        for q in range(4):
-            out_pass(0, q)
+            out_pass(0, q, accs[q], 0)
         h1 = keep.tile([P, 4, 4 * P], BF16, name="h1", tag="half1", align_bytes=64)
-        level_unit(1, 0, h1[:, 0, :])
+        level_unit(1, 0, h1[:, 0, :], w1sp)
         for q in range(4):
             if q < 3:
-                level_unit(1, q + 1, h1[:, q + 1, :])
-            quantize(hc[1, q], hs[1, q], h1[:, q, :])
-            out_pass(1, q)
-            store(q)
+                level_unit(1, q + 1, h1[:, q + 1, :], w1sp)
+            else:
+                last = psum.tile([P, 2, P], F32, name="last", tag="wl")
+                out_pass(0, 3, last, 2)
+            quantize(hc[1][:, P * q : P * (q + 1)], hs[1][:, P * q : P * (q + 1)], h1[:, q, :])
+            out_pass(1, q, accs[q], 0)
+            store(q, accs[q], 0, nc.scalar.copy)
+        out_pass(1, 3, last, 2)
+        store(3, last, 2, nc.vector.tensor_copy)

@@ -141,15 +141,15 @@ def tile_list_wheat_reaction_norm_kernel(
             )
 
         def cast_w2(b):
-            dst = w2h[b][:].rearrange("p (t g u i j) -> p t g u j i", t=4, g=16, u=2, i=4)
-            src = w2raw[b][:].rearrange("p j (g t u i) -> p t g u j i", t=4, u=2, i=4)
+            dst = w2h[b][:].rearrange("p (t g u i j) -> p t g u j i", t=4, g=16, u=4, i=2)
+            src = w2raw[b][:].rearrange("p j (g t u i) -> p t g u j i", t=4, u=4, i=2)
             for t in range(4):
                 nc.scalar.copy(out=dst[:, t], in_=src[:, t])
 
         def cast_wo(b):
             nc.scalar.copy(
-                out=woh[b][:].rearrange("p (c i t) -> p c t i", i=4, t=4),
-                in_=woraw[b][:].rearrange("p t (c i) -> p c t i", i=4),
+                out=woh[b][:].rearrange("p (c i t) -> p c t i", i=2, t=4),
+                in_=woraw[b][:].rearrange("p t (c i) -> p c t i", i=2),
             )
 
         def quantize(codes, scales, values):
@@ -194,9 +194,9 @@ def tile_list_wheat_reaction_norm_kernel(
                         rhs=g1w[a][:, toks].bitcast(FP8X4), rhs_scale=g1s[a][:, toks], start=(a == 0), stop=(a == 1),
                     )
             nc.vector.tensor_tensor(
-                hh.rearrange("p (c i t) -> p c t i", i=4, t=4),
-                line[:].rearrange("p t (c i) -> p c t i", i=4),
-                curved[b][:, :, toks].rearrange("p t (c i) -> p c t i", i=4),
+                hh.rearrange("p (c i t) -> p c t i", i=2, t=4),
+                line[:].rearrange("p t (c i) -> p c t i", i=2),
+                curved[b][:, :, toks].rearrange("p t (c i) -> p c t i", i=2),
                 ADD,
             )
 

@@ -54,7 +54,7 @@ def tile_list_wheat_reaction_norm_kernel(
         w3p = [sb(f"w3p{b}", [P, 2, 512], I32) for b in range(2)]
         w3sraw = sb("w3sraw", [P, 2, H // 4], I32)
         w3sp = sb("w3sp", [P, 2, H], U8)
-        w2raw = [sb(f"w2raw{b}", [P, 4, 512], F32) for b in range(2)]
+        w2raw = [keep.tile([P, 4, 512], F32, name=f"w2raw{b}", tag=f"w2raw{b}", align_bytes=64) for b in range(2)]
         w2h = [sb(f"w2h{b}", [P, 2048], BF16) for b in range(2)]
         w2c = [sb(f"w2c{b}", [P, 512], U32) for b in range(2)]
         w2s = [sb(f"w2s{b}", [P, 512], U8) for b in range(2)]
@@ -64,7 +64,7 @@ def tile_list_wheat_reaction_norm_kernel(
         wos = [sb(f"wos{b}", [P, N], U8) for b in range(2)]
         cvrows = sb("cvrows", [P, P], F32)
         ident = sb("ident", [P, P], F32)
-        cv = sb("cv", [P, 8], F32)
+        make_identity(nc, ident[:])
         nc.gpsimd.memset(cvrows[:], 0.0)
 
         nc.vector.memset(t3s[:].bitcast(I32), 0)
@@ -77,11 +77,11 @@ def tile_list_wheat_reaction_norm_kernel(
         def words(dram, a):
             return dram[a].rearrange("p c i -> p (c i)").bitcast(I32)
 
-        def load_table_scales(tile, dram):
+        def load_table_scales(eng, tile, dram):
             passes = dram.shape[0]
             rows = dram.bitcast(I32).rearrange("a (q r) c -> r q a c", r=4)
             for r in range(4):
-                nc.scalar.dma_start(out=tile[r : P : 32 // passes, :].bitcast(I32), in_=rows[r])
+                eng.dma_start(out=tile[r : P : 32 // passes, :].bitcast(I32), in_=rows[r])
 
         def load_weight_scales(eng, tile, dram):
             rows = dram.bitcast(I32).rearrange("a (q r) c -> q r a c", r=4)
@@ -117,16 +117,14 @@ def tile_list_wheat_reaction_norm_kernel(
         load_wo(1)
         load_weight_scales(nc.scalar, t3s[:].bitcast(I32), tab3_scales)
         load_weight_scales(nc.scalar, w3sraw, w3_scales)
-        load_table_scales(t2s, tab2_scales)
+        load_table_scales(nc.scalar, t2s, tab2_scales)
 
         crows = curv.rearrange("(b g t i) -> b t g i", b=2, t=4, i=8)
         for b in range(2):
             nc.gpsimd.dma_start(out=cvrows[4 * b : 4 * b + 4, :].rearrange("t (g i) -> t g i", i=8), in_=crows[b])
-        make_identity(nc, ident[:])
-        load_weight_scales(nc.gpsimd, w1sraw, w1_scales)
+        load_table_scales(nc.gpsimd, t1s, tab_scales)
         cvt = psum.tile([P, P], F32, name="cvt", tag="wl")
         nc.tensor.transpose(cvt[:], cvrows[:], ident[:])
-        nc.scalar.copy(out=cv[:], in_=cvt[:, 0:8])
 
         def gather(dst, window, lst):
             nc.vector.tensor_copy(dst[:], window.indirect(lst[:]))
@@ -159,7 +157,7 @@ def tile_list_wheat_reaction_norm_kernel(
         slope = [keep.tile([P, 4, S], F32, name=f"slope{b}", tag=f"slope{b}", align_bytes=64) for b in range(2)]
         curved = [sb(f"curved{b}", [P, 4, S], F32) for b in range(2)]
 
-        def slope_unit(b, t):
+        def slope_unit(b, t, cv):
             cols = slice(P * t, P * (t + 1))
             hcols = slice(512 * b + P * t, 512 * b + P * (t + 1))
             weather = psum.tile([P, S], F32, name="weather", tag="wl")
@@ -176,8 +174,8 @@ def tile_list_wheat_reaction_norm_kernel(
             nc.scalar.copy(out=wsb[b][:, t, :], in_=weather[:])
             nc.vector.scalar_tensor_tensor(slope[b][:, t, :], wsb[b][:, t, :], cv[:, 4 * b + t : 4 * b + t + 1], soil[:], MULT, ADD)
 
-        def curve(b):
-            nc.vector.tensor_tensor(curved[b][:], slope[b][:], wsb[b][:], MULT)
+        def curve(eng, b, ts):
+            eng.tensor_tensor(curved[b][:, ts, :], slope[b][:, ts, :], wsb[b][:, ts, :], MULT)
 
         hc = [sb(f"hc{b}", [P, S], U32) for b in range(2)]
         hs = [sb(f"hs{b}", [P, S], U8) for b in range(2)]
@@ -225,7 +223,9 @@ def tile_list_wheat_reaction_norm_kernel(
         permute(w3sp[:].bitcast(I32), w3sraw[:], 2)
         permute(w3p[0][:], w3raw[0][:], 8)
         cast_w2(0)
-        load_table_scales(t1s, tab_scales)
+        cv = keep.tile([P, 8], F32, name="cv", tag="w2raw0", align_bytes=64)
+        nc.scalar.copy(out=cv[:], in_=cvt[:, 0:8])
+        load_weight_scales(nc.scalar, w1sraw, w1_scales)
         gather(g2s, t2s[:], list2)
         quantize(w2c[0][:], w2s[0][:], w2h[0][:])
         gather(g2w, t2w[:].bitcast(U32), list2)
@@ -234,20 +234,22 @@ def tile_list_wheat_reaction_norm_kernel(
         permute(w3p[1][:], w3raw[1][:], 8)
         gather(g1w[0], t1w[0][:].bitcast(U32), list1)
         for t in range(4):
-            slope_unit(0, t)
+            slope_unit(0, t, cv)
         cast_w2(1)
         quantize(w2c[1][:], w2s[1][:], w2h[1][:])
         permute(w1p[:], w1raw[:], 4)
         gather(g1w[1], t1w[1][:].bitcast(U32), list1)
-        curve(0)
+        curve(nc.vector, 0, slice(0, 4))
         w1sp = keep.tile([P, 2, H], U8, name="w1sp", tag="slope0", align_bytes=64)
         permute(w1sp[:].bitcast(I32), w1sraw[:], 2)
         for t in range(4):
-            slope_unit(1, t)
+            slope_unit(1, t, cv)
+            if t < 3:
+                curve(nc.gpsimd, 1, slice(t, t + 1))
         h0 = sb("h0", [P, 4, 4 * P], BF16)
         for q in range(4):
             level_unit(0, q, h0[:, q, :], w1sp)
-        curve(1)
+        curve(nc.vector, 1, slice(3, 4))
         quantize(hc[0][:], hs[0][:], h0[:].rearrange("p q c -> p (q c)"))
         for b in range(2):
             cast_wo(b)

@@ -36,10 +36,10 @@ def tile_list_wheat_reaction_norm_kernel(
         list2 = sb("list2", [P, S // 16], U16)
         list3 = sb("list3", [P, S // 16], U16)
         t1w = [sb(f"t1w{a}", [P, T], I32) for a in range(2)]
-        t2w = sb("t2w", [P, T2], I32)
+        t2w = keep.tile([P, T2], I32, name="t2w", tag="t2w", align_bytes=64)
         t3w = [sb(f"t3w{a}", [P, T3], U16) for a in range(2)]
         t1s = sb("t1s", [P, T], U8)
-        t2s = sb("t2s", [P, T2], U8)
+        t2s = keep.tile([P, T2], U8, name="t2s", tag="t2s", align_bytes=64)
         t3s = sb("t3s", [P, 2, T3], U8)
         g1w = [sb(f"g1w{a}", [P, S], U32) for a in range(2)]
         g2w = sb("g2w", [P, S], U32)
@@ -50,13 +50,13 @@ def tile_list_wheat_reaction_norm_kernel(
         w1raw = sb("w1raw", [P, 2, H // 2], I32)
         w1p = sb("w1p", [P, 2, H // 2], I32)
         w1sraw = sb("w1sraw", [P, 2, H // 4], I32)
-        w3raw = [sb(f"w3raw{b}", [P, 2, 512], I32) for b in range(2)]
-        w3p = [sb(f"w3p{b}", [P, 2, 512], I32) for b in range(2)]
+        w3raw = sb("w3raw", [P, 2, H], I32)
+        w3p = [keep.tile([P, 2, 512], I32, name=f"w3p{b}", tag=("w3p0", "t2w")[b], align_bytes=64) for b in range(2)]
         w3sraw = sb("w3sraw", [P, 2, H // 4], I32)
         w3sp = sb("w3sp", [P, 2, H], U8)
         w2raw = [keep.tile([P, 4, 512], F32, name=f"w2raw{b}", tag=f"w2raw{b}", align_bytes=64) for b in range(2)]
         w2h = [sb(f"w2h{b}", [P, 2048], BF16) for b in range(2)]
-        w2c = [sb(f"w2c{b}", [P, 512], U32) for b in range(2)]
+        w2c = [keep.tile([P, 512], U32, name=f"w2c{b}", tag=("t2s", "w2c1")[b], align_bytes=64) for b in range(2)]
         w2s = [sb(f"w2s{b}", [P, 512], U8) for b in range(2)]
         woraw = [sb(f"woraw{b}", [P, 4, N], F32) for b in range(2)]
         woh = [keep.tile([P, 4 * N], BF16, name=f"woh{b}", tag=f"half{b}", align_bytes=64) for b in range(2)]
@@ -64,10 +64,9 @@ def tile_list_wheat_reaction_norm_kernel(
         wos = [sb(f"wos{b}", [P, N], U8) for b in range(2)]
         cvrows = sb("cvrows", [P, P], F32)
         ident = sb("ident", [P, P], F32)
-        make_identity(nc, ident[:])
-        nc.gpsimd.memset(cvrows[:], 0.0)
 
         nc.vector.memset(t3s[:].bitcast(I32), 0)
+        nc.gpsimd.memset(cvrows[:], 0.0)
         nc.vector.memset(w3sraw[:], 0)
         nc.vector.memset(t2s[:].bitcast(I32), 0)
         nc.vector.memset(t1s[:].bitcast(I32), 0)
@@ -91,9 +90,6 @@ def tile_list_wheat_reaction_norm_kernel(
         def load_w2(b):
             nc.sync.dma_start(out=w2raw[b][:], in_=w2[:, 512 * b : 512 * (b + 1)].rearrange("(p j) c -> p j c", j=4))
 
-        def load_w3(b):
-            src = w3_words.rearrange("a p c i -> p a (c i)")[:, :, 2048 * b : 2048 * (b + 1)].bitcast(I32)
-            nc.sync.dma_start(out=w3raw[b][:], in_=src)
 
         def load_wo(b):
             rows = wo[512 * b : 512 * (b + 1), :].rearrange("(g t i) n -> t g i n", t=4, i=8)
@@ -103,26 +99,27 @@ def tile_list_wheat_reaction_norm_kernel(
         nc.sync.dma_start(list3[:], offs3)
         for a in range(2):
             nc.sync.dma_start(out=t3w[a][:].bitcast(I32), in_=tab3_words[a].bitcast(I32))
+        load_weight_scales(nc.sync, t3s[:].bitcast(I32), tab3_scales)
         load_w2(0)
-        load_w3(0)
+        load_weight_scales(nc.sync, w3sraw, w3_scales)
+        nc.sync.dma_start(out=w3raw[:], in_=w3_words.rearrange("a p c i -> p a (c i)").bitcast(I32))
         nc.sync.dma_start(list2[:], offs2)
+        load_table_scales(nc.sync, t2s, tab2_scales)
         nc.sync.dma_start(out=t2w[:], in_=words(tab2_words, 0))
         nc.sync.dma_start(list1[:], offs)
-        load_w3(1)
-        nc.sync.dma_start(out=t1w[0][:], in_=words(tab_words, 0))
+        load_table_scales(nc.sync, t1s, tab_scales)
         load_w2(1)
+        nc.sync.dma_start(out=t1w[0][:], in_=words(tab_words, 0))
+        load_weight_scales(nc.sync, w1sraw, w1_scales)
         nc.sync.dma_start(out=w1raw[:], in_=w1_words.rearrange("a p c -> p a c").bitcast(I32))
         nc.sync.dma_start(out=t1w[1][:], in_=words(tab_words, 1))
         load_wo(0)
         load_wo(1)
-        load_weight_scales(nc.scalar, t3s[:].bitcast(I32), tab3_scales)
-        load_weight_scales(nc.scalar, w3sraw, w3_scales)
-        load_table_scales(nc.scalar, t2s, tab2_scales)
 
         crows = curv.rearrange("(b g t i) -> b t g i", b=2, t=4, i=8)
         for b in range(2):
             nc.gpsimd.dma_start(out=cvrows[4 * b : 4 * b + 4, :].rearrange("t (g i) -> t g i", i=8), in_=crows[b])
-        load_table_scales(nc.gpsimd, t1s, tab_scales)
+        make_identity(nc, ident[:])
         cvt = psum.tile([P, P], F32, name="cvt", tag="wl")
         nc.tensor.transpose(cvt[:], cvrows[:], ident[:])
 
@@ -136,6 +133,12 @@ def tile_list_wheat_reaction_norm_kernel(
             nc.vector.tensor_copy(
                 out=dst.rearrange("p a (b t g i) -> p (a b) t g i", t=4, g=16, i=run),
                 in_=src.rearrange("p a (b g t i) -> p (a b) t g i", t=4, g=16, i=run),
+            )
+
+        def permute_w3(b):
+            nc.vector.tensor_copy(
+                out=w3p[b][:].rearrange("p a (t g i) -> p a t g i", t=4, i=8),
+                in_=w3raw[:, :, 512 * b : 512 * (b + 1)].rearrange("p a (g t i) -> p a t g i", t=4, i=8),
             )
 
         def cast_w2(b):
@@ -153,7 +156,7 @@ def tile_list_wheat_reaction_norm_kernel(
         def quantize(codes, scales, values):
             nc.vector.quantize_mx(out=codes.bitcast(FP8X4), scales=scales, in_=values)
 
-        wsb = [sb(f"wsb{b}", [P, 4, S], F32) for b in range(2)]
+        wsb = [keep.tile([P, 4, S], F32, name=f"wsb{b}", tag=("wsb0", "w2raw1")[b], align_bytes=64) for b in range(2)]
         slope = [keep.tile([P, 4, S], F32, name=f"slope{b}", tag=f"slope{b}", align_bytes=64) for b in range(2)]
         curved = [sb(f"curved{b}", [P, 4, S], F32) for b in range(2)]
 
@@ -183,13 +186,14 @@ def tile_list_wheat_reaction_norm_kernel(
         def level_unit(b, q, hh, w1sp):
             toks = slice(P * q, P * (q + 1))
             line = psum.tile([P, 4, P], F32, name="line", tag="wl")
-            for t in range(4):
-                c0 = 512 * b + P * t
-                for a in range(2):
+            for a in range(2):
+                for t in range(4):
+                    c0 = 512 * b + P * t
                     nc.tensor.matmul_mx(
                         out=line[:, t, :], lhsT=w1p[:, a, c0 // 2 : (c0 + P) // 2].bitcast(FP4X4),
                         lhsT_scale=w1sp[:, a, c0 : c0 + P],
-                        rhs=g1w[a][:, toks].bitcast(FP8X4), rhs_scale=g1s[a][:, toks], start=(a == 0), stop=(a == 1),
+                        rhs=g1w[a][:, toks].bitcast(FP8X4), rhs_scale=g1s[a][:, toks],
+                        start=(a == 0 and t == 0), stop=(a == 1 and t == 3),
                     )
             nc.vector.tensor_tensor(
                 hh.rearrange("p (c i t) -> p c t i", i=2, t=4),
@@ -217,43 +221,41 @@ def tile_list_wheat_reaction_norm_kernel(
             nc.sync.dma_start(out=out_rows[:, m0 : m0 + count, P * q : P * (q + 1)], in_=res[:])
 
         gather(g3w[0], t3w[0][:], list3)
-        gather(g3s[0], t3s[:, 0, :], list3)
         gather(g3w[1], t3w[1][:], list3)
+        gather(g3s[0], t3s[:, 0, :], list3)
         gather(g3s[1], t3s[:, 1, :], list3)
-        permute(w3sp[:].bitcast(I32), w3sraw[:], 2)
-        permute(w3p[0][:], w3raw[0][:], 8)
         cast_w2(0)
         cv = keep.tile([P, 8], F32, name="cv", tag="w2raw0", align_bytes=64)
         nc.scalar.copy(out=cv[:], in_=cvt[:, 0:8])
-        load_weight_scales(nc.scalar, w1sraw, w1_scales)
+        permute(w3sp[:].bitcast(I32), w3sraw[:], 2)
+        permute_w3(0)
         gather(g2s, t2s[:], list2)
         quantize(w2c[0][:], w2s[0][:], w2h[0][:])
         gather(g2w, t2w[:].bitcast(U32), list2)
-        gather(g1s[0], t1s[:], list1)
-        shift(g1s)
-        permute(w3p[1][:], w3raw[1][:], 8)
-        gather(g1w[0], t1w[0][:].bitcast(U32), list1)
+        permute_w3(1)
         for t in range(4):
             slope_unit(0, t, cv)
+            curve(nc.gpsimd, 0, slice(t, t + 1))
         cast_w2(1)
+        gather(g1s[0], t1s[:], list1)
+        shift(g1s)
         quantize(w2c[1][:], w2s[1][:], w2h[1][:])
-        permute(w1p[:], w1raw[:], 4)
-        gather(g1w[1], t1w[1][:].bitcast(U32), list1)
-        curve(nc.vector, 0, slice(0, 4))
-        w1sp = keep.tile([P, 2, H], U8, name="w1sp", tag="slope0", align_bytes=64)
-        permute(w1sp[:].bitcast(I32), w1sraw[:], 2)
         for t in range(4):
             slope_unit(1, t, cv)
-            if t < 3:
-                curve(nc.gpsimd, 1, slice(t, t + 1))
-        h0 = sb("h0", [P, 4, 4 * P], BF16)
+            curve(nc.gpsimd, 1, slice(t, t + 1))
+        gather(g1w[0], t1w[0][:].bitcast(U32), list1)
+        w1sp = sb("w1sp", [P, 2, H], U8)
+        permute(w1sp[:].bitcast(I32), w1sraw[:], 2)
+        permute(w1p[:], w1raw[:], 4)
+        gather(g1w[1], t1w[1][:].bitcast(U32), list1)
+        cast_wo(0)
+        quantize(woc[0][:], wos[0][:], woh[0][:])
+        h0 = keep.tile([P, 4, 4 * P], BF16, name="h0", tag="half0", align_bytes=64)
         for q in range(4):
             level_unit(0, q, h0[:, q, :], w1sp)
-        curve(nc.vector, 1, slice(3, 4))
         quantize(hc[0][:], hs[0][:], h0[:].rearrange("p q c -> p (q c)"))
-        for b in range(2):
-            cast_wo(b)
-            quantize(woc[b][:], wos[b][:], woh[b][:])
+        cast_wo(1)
+        quantize(woc[1][:], wos[1][:], woh[1][:])
         accs = [psum.tile([P, 4 if q < 3 else 2, P], F32, name=f"acc{q}", tag="soil") for q in range(4)]
         for q in range(4):
             out_pass(0, q, accs[q], 0)

@@ -35,10 +35,10 @@ def tile_list_wheat_reaction_norm_kernel(
         list1 = sb("list1", [P, S // 16], U16)
         list2 = sb("list2", [P, S // 16], U16)
         list3 = sb("list3", [P, S // 16], U16)
-        t1w = [sb(f"t1w{a}", [P, T], I32) for a in range(2)]
+        t1w = [keep.tile([P, T], I32, name=f"t1w{a}", tag=f"t1w{a}", align_bytes=64) for a in range(2)]
         t2w = keep.tile([P, T2], I32, name="t2w", tag="t2w", align_bytes=64)
         t3w = [sb(f"t3w{a}", [P, T3], U16) for a in range(2)]
-        t1s = sb("t1s", [P, T], U8)
+        t1s = keep.tile([P, T], U8, name="t1s", tag="t1s", align_bytes=64)
         t2s = keep.tile([P, T2], U8, name="t2s", tag="t2s", align_bytes=64)
         t3s = sb("t3s", [P, 2, T3], U8)
         g1w = [sb(f"g1w{a}", [P, S], U32) for a in range(2)]
@@ -60,7 +60,6 @@ def tile_list_wheat_reaction_norm_kernel(
         w2s = [sb(f"w2s{b}", [P, 512], U8) for b in range(2)]
         woraw = [sb(f"woraw{b}", [P, 4, N], F32) for b in range(2)]
         woh = [keep.tile([P, 4 * N], BF16, name=f"woh{b}", tag=f"half{b}", align_bytes=64) for b in range(2)]
-        woc = [sb(f"woc{b}", [P, N], U32) for b in range(2)]
         wos = [sb(f"wos{b}", [P, N], U8) for b in range(2)]
         cvrows = sb("cvrows", [P, P], F32)
         ident = sb("ident", [P, P], F32)
@@ -157,8 +156,8 @@ def tile_list_wheat_reaction_norm_kernel(
             nc.vector.quantize_mx(out=codes.bitcast(FP8X4), scales=scales, in_=values)
 
         wsb = [keep.tile([P, 4, S], F32, name=f"wsb{b}", tag=("wsb0", "w2raw1")[b], align_bytes=64) for b in range(2)]
-        slope = [keep.tile([P, 4, S], F32, name=f"slope{b}", tag=f"slope{b}", align_bytes=64) for b in range(2)]
-        curved = [sb(f"curved{b}", [P, 4, S], F32) for b in range(2)]
+        slope = [keep.tile([P, 4, S], F32, name=f"slope{b}", tag=("t1s", "t1w1")[b], align_bytes=64) for b in range(2)]
+        curved = [keep.tile([P, 4, S], F32, name=f"curved{b}", tag=f"curved{b}", align_bytes=64) for b in range(2)]
 
         def slope_unit(b, t, cv):
             cols = slice(P * t, P * (t + 1))
@@ -176,9 +175,16 @@ def tile_list_wheat_reaction_norm_kernel(
             )
             nc.scalar.copy(out=wsb[b][:, t, :], in_=weather[:])
             nc.vector.scalar_tensor_tensor(slope[b][:, t, :], wsb[b][:, t, :], cv[:, 4 * b + t : 4 * b + t + 1], soil[:], MULT, ADD)
+            return weather
 
-        def curve(eng, b, ts):
-            eng.tensor_tensor(curved[b][:, ts, :], slope[b][:, ts, :], wsb[b][:, ts, :], MULT)
+        def slopes(b, cv, shared):
+            banks = []
+            for t in range(4):
+                banks.append(slope_unit(b, t, cv))
+                if t < shared:
+                    nc.gpsimd.tensor_tensor(curved[b][:, t, :], slope[b][:, t, :], wsb[b][:, t, :], MULT)
+            for t in range(shared, 4):
+                nc.vector.tensor_tensor(curved[b][:, t, :], slope[b][:, t, :], banks[t][:], MULT)
 
         hc = [sb(f"hc{b}", [P, S], U32) for b in range(2)]
         hs = [sb(f"hs{b}", [P, S], U8) for b in range(2)]
@@ -233,29 +239,25 @@ def tile_list_wheat_reaction_norm_kernel(
         quantize(w2c[0][:], w2s[0][:], w2h[0][:])
         gather(g2w, t2w[:].bitcast(U32), list2)
         permute_w3(1)
-        for t in range(4):
-            slope_unit(0, t, cv)
-            curve(nc.gpsimd, 0, slice(t, t + 1))
-        cast_w2(1)
         gather(g1s[0], t1s[:], list1)
         shift(g1s)
+        slopes(0, cv, 2)
+        cast_w2(1)
         quantize(w2c[1][:], w2s[1][:], w2h[1][:])
-        for t in range(4):
-            slope_unit(1, t, cv)
-            curve(nc.gpsimd, 1, slice(t, t + 1))
         gather(g1w[0], t1w[0][:].bitcast(U32), list1)
         w1sp = sb("w1sp", [P, 2, H], U8)
         permute(w1sp[:].bitcast(I32), w1sraw[:], 2)
         permute(w1p[:], w1raw[:], 4)
         gather(g1w[1], t1w[1][:].bitcast(U32), list1)
-        cast_wo(0)
-        quantize(woc[0][:], wos[0][:], woh[0][:])
-        h0 = keep.tile([P, 4, 4 * P], BF16, name="h0", tag="half0", align_bytes=64)
+        slopes(1, cv, 3)
+        h0 = sb("h0", [P, 4, 4 * P], BF16)
         for q in range(4):
             level_unit(0, q, h0[:, q, :], w1sp)
         quantize(hc[0][:], hs[0][:], h0[:].rearrange("p q c -> p (q c)"))
-        cast_wo(1)
-        quantize(woc[1][:], wos[1][:], woh[1][:])
+        woc = [keep.tile([P, N], U32, name=f"woc{b}", tag=("curved0", "woc1")[b], align_bytes=64) for b in range(2)]
+        for b in range(2):
+            cast_wo(b)
+            quantize(woc[b][:], wos[b][:], woh[b][:])
         accs = [psum.tile([P, 4 if q < 3 else 2, P], F32, name=f"acc{q}", tag="soil") for q in range(4)]
         for q in range(4):
             out_pass(0, q, accs[q], 0)

@@ -50,8 +50,8 @@ def tile_list_wheat_reaction_norm_kernel(
         w1raw = sb("w1raw", [P, 2, H // 2], I32)
         w1p = sb("w1p", [P, 2, H // 2], I32)
         w1sraw = sb("w1sraw", [P, 2, H // 4], I32)
-        w3raw = sb("w3raw", [P, 2, H], I32)
-        w3p = [keep.tile([P, 2, 512], I32, name=f"w3p{b}", tag=("w3p0", "t2w")[b], align_bytes=64) for b in range(2)]
+        w3raw = [sb(f"w3raw{b}", [P, 2, 512], I32) for b in range(2)]
+        w3p = [keep.tile([P, 2, 512], I32, name=f"w3p{b}", tag=f"w3p{b}", align_bytes=64) for b in range(2)]
         w3sraw = sb("w3sraw", [P, 2, H // 4], I32)
         w3sp = sb("w3sp", [P, 2, H], U8)
         w2raw = [keep.tile([P, 4, 512], F32, name=f"w2raw{b}", tag=f"w2raw{b}", align_bytes=64) for b in range(2)]
@@ -82,13 +82,17 @@ def tile_list_wheat_reaction_norm_kernel(
                 eng.dma_start(out=tile[r : P : 32 // passes, :].bitcast(I32), in_=rows[r])
 
         def load_weight_scales(eng, tile, dram):
-            rows = dram.bitcast(I32).rearrange("a (q r) c -> q r a c", r=4)
-            for q in range(4):
-                eng.dma_start(out=tile[32 * q : 32 * q + 4, :, :], in_=rows[q])
+            rows = dram.bitcast(I32).rearrange("a (q r) c -> r q a c", r=4)
+            for r in range(4):
+                eng.dma_start(out=tile[r:P:32, :, :], in_=rows[r])
 
         def load_w2(b):
             nc.sync.dma_start(out=w2raw[b][:], in_=w2[:, 512 * b : 512 * (b + 1)].rearrange("(p j) c -> p j c", j=4))
 
+
+        def load_w3(b):
+            src = w3_words.rearrange("a p c i -> p a (c i)")[:, :, 2048 * b : 2048 * (b + 1)].bitcast(I32)
+            nc.sync.dma_start(out=w3raw[b][:], in_=src)
 
         def load_wo(b):
             rows = wo[512 * b : 512 * (b + 1), :].rearrange("(g t i) n -> t g i n", t=4, i=8)
@@ -101,13 +105,14 @@ def tile_list_wheat_reaction_norm_kernel(
         load_weight_scales(nc.sync, t3s[:].bitcast(I32), tab3_scales)
         load_w2(0)
         load_weight_scales(nc.sync, w3sraw, w3_scales)
-        nc.sync.dma_start(out=w3raw[:], in_=w3_words.rearrange("a p c i -> p a (c i)").bitcast(I32))
+        load_w3(0)
         nc.sync.dma_start(list2[:], offs2)
         load_table_scales(nc.sync, t2s, tab2_scales)
         nc.sync.dma_start(out=t2w[:], in_=words(tab2_words, 0))
         nc.sync.dma_start(list1[:], offs)
         load_table_scales(nc.sync, t1s, tab_scales)
         load_w2(1)
+        load_w3(1)
         nc.sync.dma_start(out=t1w[0][:], in_=words(tab_words, 0))
         load_weight_scales(nc.sync, w1sraw, w1_scales)
         nc.sync.dma_start(out=w1raw[:], in_=w1_words.rearrange("a p c -> p a c").bitcast(I32))
@@ -137,7 +142,7 @@ def tile_list_wheat_reaction_norm_kernel(
         def permute_w3(b):
             nc.vector.tensor_copy(
                 out=w3p[b][:].rearrange("p a (t g i) -> p a t g i", t=4, i=8),
-                in_=w3raw[:, :, 512 * b : 512 * (b + 1)].rearrange("p a (g t i) -> p a t g i", t=4, i=8),
+                in_=w3raw[b][:].rearrange("p a (g t i) -> p a t g i", t=4, i=8),
             )
 
         def cast_w2(b):
@@ -238,11 +243,11 @@ def tile_list_wheat_reaction_norm_kernel(
         gather(g2s, t2s[:], list2)
         quantize(w2c[0][:], w2s[0][:], w2h[0][:])
         gather(g2w, t2w[:].bitcast(U32), list2)
-        permute_w3(1)
         gather(g1s[0], t1s[:], list1)
         shift(g1s)
         slopes(0, cv, 2)
         cast_w2(1)
+        permute_w3(1)
         quantize(w2c[1][:], w2s[1][:], w2h[1][:])
         gather(g1w[0], t1w[0][:].bitcast(U32), list1)
         w1sp = sb("w1sp", [P, 2, H], U8)

@@ -64,8 +64,9 @@ def tile_list_wheat_reaction_norm_kernel(
         cvrows = sb("cvrows", [P, P], F32)
         ident = sb("ident", [P, P], F32)
 
-        nc.vector.memset(t3s[:].bitcast(I32), 0)
+        make_identity(nc, ident[:])
         nc.gpsimd.memset(cvrows[:], 0.0)
+        nc.vector.memset(t3s[:].bitcast(I32), 0)
         nc.vector.memset(w3sraw[:], 0)
         nc.vector.memset(t2s[:].bitcast(I32), 0)
         nc.vector.memset(t1s[:].bitcast(I32), 0)
@@ -123,7 +124,6 @@ def tile_list_wheat_reaction_norm_kernel(
         crows = curv.rearrange("(b g t i) -> b t g i", b=2, t=4, i=8)
         for b in range(2):
             nc.gpsimd.dma_start(out=cvrows[4 * b : 4 * b + 4, :].rearrange("t (g i) -> t g i", i=8), in_=crows[b])
-        make_identity(nc, ident[:])
         cvt = psum.tile([P, P], F32, name="cvt", tag="wl")
         nc.tensor.transpose(cvt[:], cvrows[:], ident[:])
 
@@ -151,10 +151,10 @@ def tile_list_wheat_reaction_norm_kernel(
             for t in range(4):
                 nc.scalar.copy(out=dst[:, t], in_=src[:, t])
 
-        def cast_wo(b):
+        def cast_wo(b, c0, c1):
             nc.scalar.copy(
-                out=woh[b][:].rearrange("p (c i t) -> p c t i", i=2, t=4),
-                in_=woraw[b][:].rearrange("p t (c i) -> p c t i", i=2),
+                out=woh[b][:, 4 * c0 : 4 * c1].rearrange("p (c i t) -> p c t i", i=2, t=4),
+                in_=woraw[b][:, :, c0:c1].rearrange("p t (c i) -> p c t i", i=2),
             )
 
         def quantize(codes, scales, values):
@@ -213,23 +213,12 @@ def tile_list_wheat_reaction_norm_kernel(
                 ADD,
             )
 
-        def out_pass(b, q, acc, m0):
-            count = acc.shape[1]
-            for m in range(count):
-                cols = slice(P * (m0 + m), P * (m0 + m + 1))
-                nc.tensor.matmul_mx(
-                    out=acc[:, m, :], lhsT=woc[b][:, cols].bitcast(FP8X4), lhsT_scale=wos[b][:, cols],
-                    rhs=hc[b][:, P * q : P * (q + 1)].bitcast(FP8X4), rhs_scale=hs[b][:, P * q : P * (q + 1)],
-                    start=(b == 0 and m == 0), stop=(b == 1 and m == count - 1),
-                )
-
-        out_rows = out.rearrange("(m p) j -> p m j", p=P)
-
-        def store(q, acc, m0, copy):
-            count = acc.shape[1]
-            res = sb(f"res{q}{m0}", [P, count, P], F32)
-            copy(out=res[:], in_=acc[:])
-            nc.sync.dma_start(out=out_rows[:, m0 : m0 + count, P * q : P * (q + 1)], in_=res[:])
+        def out_pass(b, m, acc):
+            cols = slice(P * m, P * (m + 1))
+            nc.tensor.matmul_mx(
+                out=acc[:], lhsT=woc[b][:, cols].bitcast(FP8X4), lhsT_scale=wos[b][:, cols],
+                rhs=hc[b][:].bitcast(FP8X4), rhs_scale=hs[b][:], start=(b == 0), stop=(b == 1),
+            )
 
         gather(g3w[0], t3w[0][:], list3)
         gather(g3w[1], t3w[1][:], list3)
@@ -260,22 +249,21 @@ def tile_list_wheat_reaction_norm_kernel(
             level_unit(0, q, h0[:, q, :], w1sp)
         quantize(hc[0][:], hs[0][:], h0[:].rearrange("p q c -> p (q c)"))
         woc = [keep.tile([P, N], U32, name=f"woc{b}", tag=("curved0", "woc1")[b], align_bytes=64) for b in range(2)]
-        for b in range(2):
-            cast_wo(b)
-            quantize(woc[b][:], wos[b][:], woh[b][:])
-        accs = [psum.tile([P, 4 if q < 3 else 2, P], F32, name=f"acc{q}", tag="soil") for q in range(4)]
+        cast_wo(0, 0, N)
+        quantize(woc[0][:], wos[0][:], woh[0][:])
+        accs = [psum.tile([P, S], F32, name=f"acc{m}", tag="soil") for m in range(4)]
+        for m in range(4):
+            out_pass(0, m, accs[m])
+        h1 = sb("h1", [P, 4, 4 * P], BF16)
         for q in range(4):
-            out_pass(0, q, accs[q], 0)
-        h1 = keep.tile([P, 4, 4 * P], BF16, name="h1", tag="half1", align_bytes=64)
-        level_unit(1, 0, h1[:, 0, :], w1sp)
-        for q in range(4):
-            if q < 3:
-                level_unit(1, q + 1, h1[:, q + 1, :], w1sp)
-            else:
-                last = psum.tile([P, 2, P], F32, name="last", tag="wl")
-                out_pass(0, 3, last, 2)
-            quantize(hc[1][:, P * q : P * (q + 1)], hs[1][:, P * q : P * (q + 1)], h1[:, q, :])
-            out_pass(1, q, accs[q], 0)
-            store(q, accs[q], 0, nc.scalar.copy)
-        out_pass(1, 3, last, 2)
-        store(3, last, 2, nc.vector.tensor_copy)
+            level_unit(1, q, h1[:, q, :], w1sp)
+        quantize(hc[1][:], hs[1][:], h1[:].rearrange("p q c -> p (q c)"))
+        for m in range(4):
+            cols = slice(P * m, P * (m + 1))
+            cast_wo(1, P * m, P * (m + 1))
+            quantize(woc[1][:, cols], wos[1][:, cols], woh[1][:, 4 * P * m : 4 * P * (m + 1)])
+            out_pass(1, m, accs[m])
+        for m in range(4):
+            res = sb(f"res{m}", [P, S], F32)
+            (nc.vector.tensor_copy, nc.scalar.copy)[m % 2](out=res[:], in_=accs[m][:])
+            nc.sync.dma_start(out=out[P * m : P * (m + 1), :], in_=res[:])

@@ -47,11 +47,11 @@ def tile_list_wheat_reaction_norm_kernel(
         g1s = [sb(f"g1s{a}", [P, S], U8) for a in range(2)]
         g2s = sb("g2s", [P, S], U8)
         g3s = [sb(f"g3s{a}", [P, S], U8) for a in range(2)]
-        w1raw = sb("w1raw", [P, 2, H // 2], I32)
+        w1raw = keep.tile([P, 2, H // 2], I32, name="w1raw", tag="w1raw", align_bytes=64)
         w1p = sb("w1p", [P, 2, H // 2], I32)
         w1sraw = sb("w1sraw", [P, 2, H // 4], I32)
-        w3raw = [sb(f"w3raw{b}", [P, 2, 512], I32) for b in range(2)]
-        w3p = [keep.tile([P, 2, 512], I32, name=f"w3p{b}", tag=f"w3p{b}", align_bytes=64) for b in range(2)]
+        w3raw = sb("w3raw", [P, 2, H], I32)
+        w3p = [keep.tile([P, 2, 512], I32, name=f"w3p{b}", tag=("w3p0", "t2w")[b], align_bytes=64) for b in range(2)]
         w3sraw = sb("w3sraw", [P, 2, H // 4], I32)
         w3sp = sb("w3sp", [P, 2, H], U8)
         w2raw = [keep.tile([P, 4, 512], F32, name=f"w2raw{b}", tag=f"w2raw{b}", align_bytes=64) for b in range(2)]
@@ -91,10 +91,6 @@ def tile_list_wheat_reaction_norm_kernel(
             nc.sync.dma_start(out=w2raw[b][:], in_=w2[:, 512 * b : 512 * (b + 1)].rearrange("(p j) c -> p j c", j=4))
 
 
-        def load_w3(b):
-            src = w3_words.rearrange("a p c i -> p a (c i)")[:, :, 2048 * b : 2048 * (b + 1)].bitcast(I32)
-            nc.sync.dma_start(out=w3raw[b][:], in_=src)
-
         def load_wo(b):
             rows = wo[512 * b : 512 * (b + 1), :].rearrange("(g t i) n -> t g i n", t=4, i=8)
             for t in range(4):
@@ -106,14 +102,13 @@ def tile_list_wheat_reaction_norm_kernel(
         load_weight_scales(nc.sync, t3s[:].bitcast(I32), tab3_scales)
         load_w2(0)
         load_weight_scales(nc.sync, w3sraw, w3_scales)
-        load_w3(0)
+        nc.sync.dma_start(out=w3raw[:], in_=w3_words.rearrange("a p c i -> p a (c i)").bitcast(I32))
         nc.sync.dma_start(list2[:], offs2)
         load_table_scales(nc.sync, t2s, tab2_scales)
         nc.sync.dma_start(out=t2w[:], in_=words(tab2_words, 0))
         nc.sync.dma_start(list1[:], offs)
         load_table_scales(nc.sync, t1s, tab_scales)
         load_w2(1)
-        load_w3(1)
         nc.sync.dma_start(out=t1w[0][:], in_=words(tab_words, 0))
         load_weight_scales(nc.sync, w1sraw, w1_scales)
         nc.sync.dma_start(out=w1raw[:], in_=w1_words.rearrange("a p c -> p a c").bitcast(I32))
@@ -142,7 +137,7 @@ def tile_list_wheat_reaction_norm_kernel(
         def permute_w3(b):
             nc.vector.tensor_copy(
                 out=w3p[b][:].rearrange("p a (t g i) -> p a t g i", t=4, i=8),
-                in_=w3raw[b][:].rearrange("p a (g t i) -> p a t g i", t=4, i=8),
+                in_=w3raw[:, :, 512 * b : 512 * (b + 1)].rearrange("p a (g t i) -> p a t g i", t=4, i=8),
             )
 
         def cast_w2(b):
@@ -161,7 +156,7 @@ def tile_list_wheat_reaction_norm_kernel(
             nc.vector.quantize_mx(out=codes.bitcast(FP8X4), scales=scales, in_=values)
 
         wsb = [keep.tile([P, 4, S], F32, name=f"wsb{b}", tag=("wsb0", "w2raw1")[b], align_bytes=64) for b in range(2)]
-        slope = [keep.tile([P, 4, S], F32, name=f"slope{b}", tag=("t1s", "t1w1")[b], align_bytes=64) for b in range(2)]
+        slope = [keep.tile([P, 4, S], F32, name=f"slope{b}", tag=("t1s", "w1raw")[b], align_bytes=64) for b in range(2)]
         curved = [keep.tile([P, 4, S], F32, name=f"curved{b}", tag=f"curved{b}", align_bytes=64) for b in range(2)]
 
         def slope_unit(b, t, cv):
@@ -180,16 +175,11 @@ def tile_list_wheat_reaction_norm_kernel(
             )
             nc.scalar.copy(out=wsb[b][:, t, :], in_=weather[:])
             nc.vector.scalar_tensor_tensor(slope[b][:, t, :], wsb[b][:, t, :], cv[:, 4 * b + t : 4 * b + t + 1], soil[:], MULT, ADD)
-            return weather
 
-        def slopes(b, cv, shared):
-            banks = []
+        def slopes(b, cv):
             for t in range(4):
-                banks.append(slope_unit(b, t, cv))
-                if t < shared:
-                    nc.gpsimd.tensor_tensor(curved[b][:, t, :], slope[b][:, t, :], wsb[b][:, t, :], MULT)
-            for t in range(shared, 4):
-                nc.vector.tensor_tensor(curved[b][:, t, :], slope[b][:, t, :], banks[t][:], MULT)
+                slope_unit(b, t, cv)
+                nc.gpsimd.tensor_tensor(curved[b][:, t, :], slope[b][:, t, :], wsb[b][:, t, :], MULT)
 
         hc = [sb(f"hc{b}", [P, S], U32) for b in range(2)]
         hs = [sb(f"hs{b}", [P, S], U8) for b in range(2)]
@@ -232,23 +222,23 @@ def tile_list_wheat_reaction_norm_kernel(
         gather(g2s, t2s[:], list2)
         quantize(w2c[0][:], w2s[0][:], w2h[0][:])
         gather(g2w, t2w[:].bitcast(U32), list2)
+        permute_w3(1)
         gather(g1s[0], t1s[:], list1)
         shift(g1s)
-        slopes(0, cv, 2)
+        slopes(0, cv)
         cast_w2(1)
-        permute_w3(1)
         quantize(w2c[1][:], w2s[1][:], w2h[1][:])
         gather(g1w[0], t1w[0][:].bitcast(U32), list1)
         w1sp = sb("w1sp", [P, 2, H], U8)
         permute(w1sp[:].bitcast(I32), w1sraw[:], 2)
         permute(w1p[:], w1raw[:], 4)
+        slopes(1, cv)
         gather(g1w[1], t1w[1][:].bitcast(U32), list1)
-        slopes(1, cv, 3)
         h0 = sb("h0", [P, 4, 4 * P], BF16)
         for q in range(4):
             level_unit(0, q, h0[:, q, :], w1sp)
         quantize(hc[0][:], hs[0][:], h0[:].rearrange("p q c -> p (q c)"))
-        woc = [keep.tile([P, N], U32, name=f"woc{b}", tag=("curved0", "woc1")[b], align_bytes=64) for b in range(2)]
+        woc = [keep.tile([P, N], U32, name=f"woc{b}", tag=f"woc{b}", align_bytes=64) for b in range(2)]
         cast_wo(0, 0, N)
         quantize(woc[0][:], wos[0][:], woh[0][:])
         accs = [psum.tile([P, S], F32, name=f"acc{m}", tag="soil") for m in range(4)]

@@ -18,6 +18,10 @@ MULT = mybir.AluOpType.mult
 ADD = mybir.AluOpType.add
 
 P = 128
+SHARED = 2
+WEATHER_BANKS = ((0, 1, 2, 3), (0, 1, 4, 5))
+SOIL_BANKS = ((4, 5, 6, 7), (6, 7, 2, 3))
+LINE_BANKS = ((0, 1, 6, 7), (2, 3, 4, 5))
 
 
 def tile_list_wheat_reaction_norm_kernel(
@@ -27,10 +31,13 @@ def tile_list_wheat_reaction_norm_kernel(
     nc = tc.nc
     with ExitStack() as ctx:
         keep = ctx.enter_context(tc.tile_pool(name="keep", bufs=1))
-        psum = ctx.enter_context(tc.psum_pool(name="psum", bufs=4))
+        psum = ctx.enter_context(tc.psum_pool(name="psum", bufs=1))
 
         def sb(name, shape, dtype):
             return keep.tile(shape, dtype, name=name, align_bytes=64)
+
+        def bank(name, shape, index):
+            return psum.tile(shape, F32, name=name, tag=f"bank{index}")
 
         list1 = sb("list1", [P, S // 16], U16)
         list2 = sb("list2", [P, S // 16], U16)
@@ -50,8 +57,8 @@ def tile_list_wheat_reaction_norm_kernel(
         w1raw = keep.tile([P, 2, H // 2], I32, name="w1raw", tag="w1raw", align_bytes=64)
         w1p = sb("w1p", [P, 2, H // 2], I32)
         w1sraw = sb("w1sraw", [P, 2, H // 4], I32)
-        w3raw = sb("w3raw", [P, 2, H], I32)
-        w3p = [keep.tile([P, 2, 512], I32, name=f"w3p{b}", tag=("w3p0", "t2w")[b], align_bytes=64) for b in range(2)]
+        w3raw = [sb(f"w3raw{b}", [P, 2, 512], I32) for b in range(2)]
+        w3p = [keep.tile([P, 2, 512], I32, name=f"w3p{b}", tag=f"w3p{b}", align_bytes=64) for b in range(2)]
         w3sraw = sb("w3sraw", [P, 2, H // 4], I32)
         w3sp = sb("w3sp", [P, 2, H], U8)
         w2raw = [keep.tile([P, 4, 512], F32, name=f"w2raw{b}", tag=f"w2raw{b}", align_bytes=64) for b in range(2)]
@@ -91,6 +98,10 @@ def tile_list_wheat_reaction_norm_kernel(
             nc.sync.dma_start(out=w2raw[b][:], in_=w2[:, 512 * b : 512 * (b + 1)].rearrange("(p j) c -> p j c", j=4))
 
 
+        def load_w3(b):
+            src = w3_words.rearrange("a p c i -> p a (c i)")[:, :, 2048 * b : 2048 * (b + 1)].bitcast(I32)
+            nc.sync.dma_start(out=w3raw[b][:], in_=src)
+
         def load_wo(b):
             rows = wo[512 * b : 512 * (b + 1), :].rearrange("(g t i) n -> t g i n", t=4, i=8)
             for t in range(4):
@@ -102,10 +113,11 @@ def tile_list_wheat_reaction_norm_kernel(
         load_weight_scales(nc.sync, t3s[:].bitcast(I32), tab3_scales)
         load_w2(0)
         load_weight_scales(nc.sync, w3sraw, w3_scales)
-        nc.sync.dma_start(out=w3raw[:], in_=w3_words.rearrange("a p c i -> p a (c i)").bitcast(I32))
+        load_w3(0)
         nc.sync.dma_start(list2[:], offs2)
         load_table_scales(nc.sync, t2s, tab2_scales)
         nc.sync.dma_start(out=t2w[:], in_=words(tab2_words, 0))
+        load_w3(1)
         nc.sync.dma_start(list1[:], offs)
         load_table_scales(nc.sync, t1s, tab_scales)
         load_w2(1)
@@ -119,7 +131,7 @@ def tile_list_wheat_reaction_norm_kernel(
         crows = curv.rearrange("(b g t i) -> b t g i", b=2, t=4, i=8)
         for b in range(2):
             nc.gpsimd.dma_start(out=cvrows[4 * b : 4 * b + 4, :].rearrange("t (g i) -> t g i", i=8), in_=crows[b])
-        cvt = psum.tile([P, P], F32, name="cvt", tag="wl")
+        cvt = bank("cvt", [P, P], 7)
         nc.tensor.transpose(cvt[:], cvrows[:], ident[:])
 
         def gather(dst, window, lst):
@@ -137,7 +149,7 @@ def tile_list_wheat_reaction_norm_kernel(
         def permute_w3(b):
             nc.vector.tensor_copy(
                 out=w3p[b][:].rearrange("p a (t g i) -> p a t g i", t=4, i=8),
-                in_=w3raw[:, :, 512 * b : 512 * (b + 1)].rearrange("p a (g t i) -> p a t g i", t=4, i=8),
+                in_=w3raw[b][:].rearrange("p a (g t i) -> p a t g i", t=4, i=8),
             )
 
         def cast_w2(b):
@@ -162,31 +174,36 @@ def tile_list_wheat_reaction_norm_kernel(
         def slope_unit(b, t, cv):
             cols = slice(P * t, P * (t + 1))
             hcols = slice(512 * b + P * t, 512 * b + P * (t + 1))
-            weather = psum.tile([P, S], F32, name="weather", tag="wl")
+            weather = bank("weather", [P, S], WEATHER_BANKS[b][t])
             for a in range(2):
                 nc.tensor.matmul_mx(
                     out=weather[:], lhsT=w3p[b][:, a, cols].bitcast(FP8X4), lhsT_scale=w3sp[:, a, hcols],
                     rhs=g3w[a][:].bitcast(FP4X4), rhs_scale=g3s[a][:], start=(a == 0), stop=(a == 1),
                 )
-            soil = psum.tile([P, S], F32, name="soil", tag="soil")
+            soil = bank("soil", [P, S], SOIL_BANKS[b][t])
             nc.tensor.matmul_mx(
                 out=soil[:], lhsT=w2c[b][:, cols].bitcast(FP8X4), lhsT_scale=w2s[b][:, cols],
                 rhs=g2w[:].bitcast(FP8X4), rhs_scale=g2s[:], start=True, stop=True,
             )
             nc.scalar.copy(out=wsb[b][:, t, :], in_=weather[:])
             nc.vector.scalar_tensor_tensor(slope[b][:, t, :], wsb[b][:, t, :], cv[:, 4 * b + t : 4 * b + t + 1], soil[:], MULT, ADD)
+            return weather
 
         def slopes(b, cv):
+            banks = []
             for t in range(4):
-                slope_unit(b, t, cv)
-                nc.gpsimd.tensor_tensor(curved[b][:, t, :], slope[b][:, t, :], wsb[b][:, t, :], MULT)
+                banks.append(slope_unit(b, t, cv))
+                if t < SHARED:
+                    nc.gpsimd.tensor_tensor(curved[b][:, t, :], slope[b][:, t, :], wsb[b][:, t, :], MULT)
+            for t in range(SHARED, 4):
+                nc.vector.tensor_tensor(curved[b][:, t, :], slope[b][:, t, :], banks[t][:], MULT)
 
         hc = [sb(f"hc{b}", [P, S], U32) for b in range(2)]
         hs = [sb(f"hs{b}", [P, S], U8) for b in range(2)]
 
         def level_unit(b, q, hh, w1sp):
             toks = slice(P * q, P * (q + 1))
-            line = psum.tile([P, 4, P], F32, name="line", tag="wl")
+            line = bank("line", [P, 4, P], LINE_BANKS[b][q])
             for a in range(2):
                 for t in range(4):
                     c0 = 512 * b + P * t
@@ -241,7 +258,7 @@ def tile_list_wheat_reaction_norm_kernel(
         woc = [keep.tile([P, N], U32, name=f"woc{b}", tag=f"woc{b}", align_bytes=64) for b in range(2)]
         cast_wo(0, 0, N)
         quantize(woc[0][:], wos[0][:], woh[0][:])
-        accs = [psum.tile([P, S], F32, name=f"acc{m}", tag="soil") for m in range(4)]
+        accs = [bank(f"acc{m}", [P, S], LINE_BANKS[0][m]) for m in range(4)]
         for m in range(4):
             out_pass(0, m, accs[m])
         h1 = sb("h1", [P, 4, 4 * P], BF16)

@@ -18,10 +18,10 @@ MULT = mybir.AluOpType.mult
 ADD = mybir.AluOpType.add
 
 P = 128
-SHARED = 2
+HALF = 256
 WEATHER_BANKS = ((0, 1, 2, 3), (0, 1, 4, 5))
 SOIL_BANKS = ((4, 5, 6, 7), (6, 7, 2, 3))
-LINE_BANKS = ((0, 1, 6, 7), (2, 3, 4, 5))
+LINE_BANKS = ((0, 4, 5, 6), (7, 1, 2, 3))
 
 
 def tile_list_wheat_reaction_norm_kernel(
@@ -57,8 +57,8 @@ def tile_list_wheat_reaction_norm_kernel(
         w1raw = keep.tile([P, 2, H // 2], I32, name="w1raw", tag="w1raw", align_bytes=64)
         w1p = sb("w1p", [P, 2, H // 2], I32)
         w1sraw = sb("w1sraw", [P, 2, H // 4], I32)
-        w3raw = [sb(f"w3raw{b}", [P, 2, 512], I32) for b in range(2)]
-        w3p = [keep.tile([P, 2, 512], I32, name=f"w3p{b}", tag=f"w3p{b}", align_bytes=64) for b in range(2)]
+        w3raw = [keep.tile([P, 2, 512], I32, name=f"w3raw{b}", tag=f"w3raw{b}", align_bytes=64) for b in range(2)]
+        w3p = [sb(f"w3p{b}", [P, 2, 512], I32) for b in range(2)]
         w3sraw = sb("w3sraw", [P, 2, H // 4], I32)
         w3sp = sb("w3sp", [P, 2, H], U8)
         w2raw = [keep.tile([P, 4, 512], F32, name=f"w2raw{b}", tag=f"w2raw{b}", align_bytes=64) for b in range(2)]
@@ -168,7 +168,9 @@ def tile_list_wheat_reaction_norm_kernel(
             nc.vector.quantize_mx(out=codes.bitcast(FP8X4), scales=scales, in_=values)
 
         wsb = [keep.tile([P, 4, S], F32, name=f"wsb{b}", tag=("wsb0", "w2raw1")[b], align_bytes=64) for b in range(2)]
-        slope = [keep.tile([P, 4, S], F32, name=f"slope{b}", tag=("t1s", "w1raw")[b], align_bytes=64) for b in range(2)]
+        slope0 = keep.tile([P, 4, S], F32, name="slope0", tag="t1s", align_bytes=64)
+        slope1 = [keep.tile([P, 2, S], F32, name=f"slope1{u}", tag=("w1raw", "t1w1")[u], align_bytes=64) for u in range(2)]
+        slope = [[slope0[:, t, :] for t in range(4)], [slope1[t // 2][:, t % 2, :] for t in range(4)]]
         curved = [keep.tile([P, 4, S], F32, name=f"curved{b}", tag=f"curved{b}", align_bytes=64) for b in range(2)]
 
         def slope_unit(b, t, cv):
@@ -186,17 +188,18 @@ def tile_list_wheat_reaction_norm_kernel(
                 rhs=g2w[:].bitcast(FP8X4), rhs_scale=g2s[:], start=True, stop=True,
             )
             nc.scalar.copy(out=wsb[b][:, t, :], in_=weather[:])
-            nc.vector.scalar_tensor_tensor(slope[b][:, t, :], wsb[b][:, t, :], cv[:, 4 * b + t : 4 * b + t + 1], soil[:], MULT, ADD)
+            nc.vector.scalar_tensor_tensor(slope[b][t], wsb[b][:, t, :], cv[:, 4 * b + t : 4 * b + t + 1], soil[:], MULT, ADD)
             return weather
 
-        def slopes(b, cv):
-            banks = []
-            for t in range(4):
-                banks.append(slope_unit(b, t, cv))
-                if t < SHARED:
-                    nc.gpsimd.tensor_tensor(curved[b][:, t, :], slope[b][:, t, :], wsb[b][:, t, :], MULT)
-            for t in range(SHARED, 4):
-                nc.vector.tensor_tensor(curved[b][:, t, :], slope[b][:, t, :], banks[t][:], MULT)
+        def slopes(b, ts, shared, cv):
+            banks = {}
+            for t in ts:
+                banks[t] = slope_unit(b, t, cv)
+                if t in shared:
+                    nc.gpsimd.tensor_tensor(curved[b][:, t, :], slope[b][t], wsb[b][:, t, :], MULT)
+            for t in ts:
+                if t not in shared:
+                    nc.vector.tensor_tensor(curved[b][:, t, :], slope[b][t], banks[t][:], MULT)
 
         hc = [sb(f"hc{b}", [P, S], U32) for b in range(2)]
         hs = [sb(f"hs{b}", [P, S], U8) for b in range(2)]
@@ -220,12 +223,28 @@ def tile_list_wheat_reaction_norm_kernel(
                 ADD,
             )
 
-        def out_pass(b, m, acc):
-            cols = slice(P * m, P * (m + 1))
-            nc.tensor.matmul_mx(
-                out=acc[:], lhsT=woc[b][:, cols].bitcast(FP8X4), lhsT_scale=wos[b][:, cols],
-                rhs=hc[b][:].bitcast(FP8X4), rhs_scale=hs[b][:], start=(b == 0), stop=(b == 1),
-            )
+        def out_passes(b, half, pair, acc):
+            toks = slice(HALF * half, HALF * (half + 1))
+            for k in range(2):
+                cols = slice(P * (2 * pair + k), P * (2 * pair + k + 1))
+                nc.tensor.matmul_mx(
+                    out=acc[:, k, :], lhsT=woc[b][:, cols].bitcast(FP8X4), lhsT_scale=wos[b][:, cols],
+                    rhs=hc[b][:, toks].bitcast(FP8X4), rhs_scale=hs[b][:, toks],
+                    start=(b == 0 and k == 0), stop=(b == 1 and k == 1),
+                )
+
+        out_rows = out.rearrange("(m p) j -> p m j", p=P)
+
+        def finish(half):
+            toks = slice(HALF * half, HALF * (half + 1))
+            quantize(hc[1][:, toks], hs[1][:, toks], h1[:, 2 * half : 2 * half + 2, :].rearrange("p q c -> p (q c)"))
+            for pair in range(2):
+                out_passes(1, half, pair, accs[half][pair])
+            for pair in range(2):
+                res = sb(f"res{half}{pair}", [P, 2, HALF], F32)
+                copy = nc.vector.tensor_copy if (half, pair) == (1, 0) else nc.scalar.copy
+                copy(out=res[:], in_=accs[half][pair][:])
+                nc.sync.dma_start(out=out_rows[:, 2 * pair : 2 * pair + 2, toks], in_=res[:])
 
         gather(g3w[0], t3w[0][:], list3)
         gather(g3w[1], t3w[1][:], list3)
@@ -242,15 +261,16 @@ def tile_list_wheat_reaction_norm_kernel(
         permute_w3(1)
         gather(g1s[0], t1s[:], list1)
         shift(g1s)
-        slopes(0, cv)
+        slopes(0, (0, 1, 2, 3), (0, 1), cv)
         cast_w2(1)
         quantize(w2c[1][:], w2s[1][:], w2h[1][:])
         gather(g1w[0], t1w[0][:].bitcast(U32), list1)
         w1sp = sb("w1sp", [P, 2, H], U8)
         permute(w1sp[:].bitcast(I32), w1sraw[:], 2)
         permute(w1p[:], w1raw[:], 4)
-        slopes(1, cv)
+        slopes(1, (0, 1), (0,), cv)
         gather(g1w[1], t1w[1][:].bitcast(U32), list1)
+        slopes(1, (2, 3), (2, 3), cv)
         h0 = sb("h0", [P, 4, 4 * P], BF16)
         for q in range(4):
             level_unit(0, q, h0[:, q, :], w1sp)
@@ -258,19 +278,17 @@ def tile_list_wheat_reaction_norm_kernel(
         woc = [keep.tile([P, N], U32, name=f"woc{b}", tag=f"woc{b}", align_bytes=64) for b in range(2)]
         cast_wo(0, 0, N)
         quantize(woc[0][:], wos[0][:], woh[0][:])
-        accs = [bank(f"acc{m}", [P, S], LINE_BANKS[0][m]) for m in range(4)]
-        for m in range(4):
-            out_pass(0, m, accs[m])
+        accs = [[bank(f"acc{u}{v}", [P, 2, HALF], LINE_BANKS[0][2 * u + v]) for v in range(2)] for u in range(2)]
+        for half in range(2):
+            for pair in range(2):
+                out_passes(0, half, pair, accs[half][pair])
+        for pair in range(2):
+            cols = slice(HALF * pair, HALF * (pair + 1))
+            cast_wo(1, HALF * pair, HALF * (pair + 1))
+            quantize(woc[1][:, cols], wos[1][:, cols], woh[1][:, 4 * HALF * pair : 4 * HALF * (pair + 1)])
         h1 = sb("h1", [P, 4, 4 * P], BF16)
-        for q in range(4):
+        for q in range(3):
             level_unit(1, q, h1[:, q, :], w1sp)
-        quantize(hc[1][:], hs[1][:], h1[:].rearrange("p q c -> p (q c)"))
-        for m in range(4):
-            cols = slice(P * m, P * (m + 1))
-            cast_wo(1, P * m, P * (m + 1))
-            quantize(woc[1][:, cols], wos[1][:, cols], woh[1][:, 4 * P * m : 4 * P * (m + 1)])
-            out_pass(1, m, accs[m])
-        for m in range(4):
-            res = sb(f"res{m}", [P, S], F32)
-            (nc.vector.tensor_copy, nc.scalar.copy)[m % 2](out=res[:], in_=accs[m][:])
-            nc.sync.dma_start(out=out[P * m : P * (m + 1), :], in_=res[:])
+        finish(0)
+        level_unit(1, 3, h1[:, 3, :], w1sp)
+        finish(1)

@@ -19,6 +19,8 @@ ADD = mybir.AluOpType.add
 
 P = 128
 HALF = 256
+SOIL_PLANE = 4
+WO_PIECES = ((0, 0, N), (1, 0, HALF), (1, HALF, N))
 WEATHER_BANKS = ((0, 1, 2, 3), (0, 1, 4, 5))
 SOIL_BANKS = ((4, 5, 6, 7), (6, 7, 2, 3))
 LINE_BANKS = ((0, 4, 5, 6), (7, 1, 2, 3))
@@ -56,16 +58,15 @@ def tile_list_wheat_reaction_norm_kernel(
         g3s = [sb(f"g3s{a}", [P, S], U8) for a in range(2)]
         w1raw = keep.tile([P, 2, H // 2], I32, name="w1raw", tag="w1raw", align_bytes=64)
         w1p = sb("w1p", [P, 2, H // 2], I32)
-        w1sraw = sb("w1sraw", [P, 2, H // 4], I32)
         w3raw = [keep.tile([P, 2, 512], I32, name=f"w3raw{b}", tag=f"w3raw{b}", align_bytes=64) for b in range(2)]
         w3p = [sb(f"w3p{b}", [P, 2, 512], I32) for b in range(2)]
-        w3sraw = sb("w3sraw", [P, 2, H // 4], I32)
+        wsraw = sb("wsraw", [P, 2, H // 4], I32)
         w3sp = sb("w3sp", [P, 2, H], U8)
         w2raw = [keep.tile([P, 4, 512], F32, name=f"w2raw{b}", tag=f"w2raw{b}", align_bytes=64) for b in range(2)]
         w2h = [sb(f"w2h{b}", [P, 2048], BF16) for b in range(2)]
         w2c = [keep.tile([P, 512], U32, name=f"w2c{b}", tag=("t2s", "w2c1")[b], align_bytes=64) for b in range(2)]
         w2s = [sb(f"w2s{b}", [P, 512], U8) for b in range(2)]
-        woraw = [sb(f"woraw{b}", [P, 4, N], F32) for b in range(2)]
+        woraw = {(b, c0): sb(f"woraw{b}_{c0}", [P, 4, c1 - c0], F32) for b, c0, c1 in WO_PIECES}
         woh = [keep.tile([P, 4 * N], BF16, name=f"woh{b}", tag=f"half{b}", align_bytes=64) for b in range(2)]
         wos = [sb(f"wos{b}", [P, N], U8) for b in range(2)]
         cvrows = sb("cvrows", [P, P], F32)
@@ -74,20 +75,18 @@ def tile_list_wheat_reaction_norm_kernel(
         make_identity(nc, ident[:])
         nc.gpsimd.memset(cvrows[:], 0.0)
         nc.vector.memset(t3s[:].bitcast(I32), 0)
-        nc.vector.memset(w3sraw[:], 0)
+        nc.vector.memset(wsraw[:], 0)
         nc.vector.memset(t2s[:].bitcast(I32), 0)
         nc.vector.memset(t1s[:].bitcast(I32), 0)
-        nc.vector.memset(g1s[1][:].bitcast(I32), 0)
-        nc.vector.memset(w1sraw[:], 0)
 
         def words(dram, a):
             return dram[a].rearrange("p c i -> p (c i)").bitcast(I32)
 
-        def load_table_scales(eng, tile, dram):
+        def load_table_scales(eng, tile, dram, first=0):
             passes = dram.shape[0]
             rows = dram.bitcast(I32).rearrange("a (q r) c -> r q a c", r=4)
             for r in range(4):
-                eng.dma_start(out=tile[r : P : 32 // passes, :].bitcast(I32), in_=rows[r])
+                eng.dma_start(out=tile[first + r : P : 32 // passes, :].bitcast(I32), in_=rows[r])
 
         def load_weight_scales(eng, tile, dram):
             rows = dram.bitcast(I32).rearrange("a (q r) c -> r q a c", r=4)
@@ -102,31 +101,38 @@ def tile_list_wheat_reaction_norm_kernel(
             src = w3_words.rearrange("a p c i -> p a (c i)")[:, :, 2048 * b : 2048 * (b + 1)].bitcast(I32)
             nc.sync.dma_start(out=w3raw[b][:], in_=src)
 
-        def load_wo(b):
-            rows = wo[512 * b : 512 * (b + 1), :].rearrange("(g t i) n -> t g i n", t=4, i=8)
+        def load_wo(b, c0, c1):
+            rows = wo[512 * b : 512 * (b + 1), c0:c1].rearrange("(g t i) n -> t g i n", t=4, i=8)
             for t in range(4):
-                nc.sync.dma_start(out=woraw[b][:, t, :], in_=rows[t])
+                nc.sync.dma_start(out=woraw[b, c0][:, t, :], in_=rows[t])
+
+        def permute(dst, src, run):
+            nc.vector.tensor_copy(
+                out=dst.rearrange("p a (b t g i) -> p (a b) t g i", t=4, g=16, i=run),
+                in_=src.rearrange("p a (b g t i) -> p (a b) t g i", t=4, g=16, i=run),
+            )
 
         nc.sync.dma_start(list3[:], offs3)
         for a in range(2):
             nc.sync.dma_start(out=t3w[a][:].bitcast(I32), in_=tab3_words[a].bitcast(I32))
         load_weight_scales(nc.sync, t3s[:].bitcast(I32), tab3_scales)
         load_w2(0)
-        load_weight_scales(nc.sync, w3sraw, w3_scales)
+        load_weight_scales(nc.sync, wsraw, w3_scales)
         load_w3(0)
         nc.sync.dma_start(list2[:], offs2)
-        load_table_scales(nc.sync, t2s, tab2_scales)
+        load_table_scales(nc.sync, t2s, tab2_scales, SOIL_PLANE)
         nc.sync.dma_start(out=t2w[:], in_=words(tab2_words, 0))
         load_w3(1)
         nc.sync.dma_start(list1[:], offs)
         load_table_scales(nc.sync, t1s, tab_scales)
         load_w2(1)
         nc.sync.dma_start(out=t1w[0][:], in_=words(tab_words, 0))
-        load_weight_scales(nc.sync, w1sraw, w1_scales)
+        permute(w3sp[:].bitcast(I32), wsraw[:], 2)
+        load_weight_scales(nc.sync, wsraw, w1_scales)
         nc.sync.dma_start(out=w1raw[:], in_=w1_words.rearrange("a p c -> p a c").bitcast(I32))
         nc.sync.dma_start(out=t1w[1][:], in_=words(tab_words, 1))
-        load_wo(0)
-        load_wo(1)
+        for piece in WO_PIECES:
+            load_wo(*piece)
 
         crows = curv.rearrange("(b g t i) -> b t g i", b=2, t=4, i=8)
         for b in range(2):
@@ -139,12 +145,6 @@ def tile_list_wheat_reaction_norm_kernel(
 
         def shift(g):
             nc.gpsimd.dma_start(out=g[1][0:112, :].bitcast(I32), in_=g[0][16:128, :].bitcast(I32))
-
-        def permute(dst, src, run):
-            nc.vector.tensor_copy(
-                out=dst.rearrange("p a (b t g i) -> p (a b) t g i", t=4, g=16, i=run),
-                in_=src.rearrange("p a (b g t i) -> p (a b) t g i", t=4, g=16, i=run),
-            )
 
         def permute_w3(b):
             nc.vector.tensor_copy(
@@ -161,7 +161,7 @@ def tile_list_wheat_reaction_norm_kernel(
         def cast_wo(b, c0, c1):
             nc.scalar.copy(
                 out=woh[b][:, 4 * c0 : 4 * c1].rearrange("p (c i t) -> p c t i", i=2, t=4),
-                in_=woraw[b][:, :, c0:c1].rearrange("p t (c i) -> p c t i", i=2),
+                in_=woraw[b, c0][:].rearrange("p t (c i) -> p c t i", i=2),
             )
 
         def quantize(codes, scales, values):
@@ -185,7 +185,7 @@ def tile_list_wheat_reaction_norm_kernel(
             soil = bank("soil", [P, S], SOIL_BANKS[b][t])
             nc.tensor.matmul_mx(
                 out=soil[:], lhsT=w2c[b][:, cols].bitcast(FP8X4), lhsT_scale=w2s[b][:, cols],
-                rhs=g2w[:].bitcast(FP8X4), rhs_scale=g2s[:], start=True, stop=True,
+                rhs=g2w[:].bitcast(FP8X4), rhs_scale=g2s[SOIL_PLANE:P, :], start=True, stop=True,
             )
             nc.scalar.copy(out=wsb[b][:, t, :], in_=weather[:])
             nc.vector.scalar_tensor_tensor(slope[b][t], wsb[b][:, t, :], cv[:, 4 * b + t : 4 * b + t + 1], soil[:], MULT, ADD)
@@ -253,7 +253,6 @@ def tile_list_wheat_reaction_norm_kernel(
         cast_w2(0)
         cv = keep.tile([P, 8], F32, name="cv", tag="w2raw0", align_bytes=64)
         nc.scalar.copy(out=cv[:], in_=cvt[:, 0:8])
-        permute(w3sp[:].bitcast(I32), w3sraw[:], 2)
         permute_w3(0)
         gather(g2s, t2s[:], list2)
         quantize(w2c[0][:], w2s[0][:], w2h[0][:])
@@ -266,7 +265,7 @@ def tile_list_wheat_reaction_norm_kernel(
         quantize(w2c[1][:], w2s[1][:], w2h[1][:])
         gather(g1w[0], t1w[0][:].bitcast(U32), list1)
         w1sp = sb("w1sp", [P, 2, H], U8)
-        permute(w1sp[:].bitcast(I32), w1sraw[:], 2)
+        permute(w1sp[:].bitcast(I32), wsraw[:], 2)
         permute(w1p[:], w1raw[:], 4)
         slopes(1, (0, 1), (0,), cv)
         gather(g1w[1], t1w[1][:].bitcast(U32), list1)

@@ -20,10 +20,10 @@ ADD = mybir.AluOpType.add
 P = 128
 HALF = 256
 SOIL_PLANE = 4
-WO_PIECES = ((0, 0, N), (1, 0, HALF), (1, HALF, N))
 WEATHER_BANKS = ((0, 1, 2, 3), (0, 1, 4, 5))
-SOIL_BANKS = ((4, 5, 6, 7), (6, 7, 2, 3))
-LINE_BANKS = ((0, 4, 5, 6), (7, 1, 2, 3))
+SOIL_BANKS = ((4, 5, 6, 7), (0, 1, 4, 5))
+LINE_BANKS = ((2, 3, 6, 7), (2, 3, 6, 7))
+OUT_BANKS = (0, 1, 4, 5)
 
 
 def tile_list_wheat_reaction_norm_kernel(
@@ -66,7 +66,7 @@ def tile_list_wheat_reaction_norm_kernel(
         w2h = [sb(f"w2h{b}", [P, 2048], BF16) for b in range(2)]
         w2c = [keep.tile([P, 512], U32, name=f"w2c{b}", tag=("t2s", "w2c1")[b], align_bytes=64) for b in range(2)]
         w2s = [sb(f"w2s{b}", [P, 512], U8) for b in range(2)]
-        woraw = {(b, c0): sb(f"woraw{b}_{c0}", [P, 4, c1 - c0], F32) for b, c0, c1 in WO_PIECES}
+        woraw = [sb(f"woraw{b}", [P, 4, N], F32) for b in range(2)]
         woh = [keep.tile([P, 4 * N], BF16, name=f"woh{b}", tag=f"half{b}", align_bytes=64) for b in range(2)]
         wos = [sb(f"wos{b}", [P, N], U8) for b in range(2)]
         cvrows = sb("cvrows", [P, P], F32)
@@ -101,10 +101,10 @@ def tile_list_wheat_reaction_norm_kernel(
             src = w3_words.rearrange("a p c i -> p a (c i)")[:, :, 2048 * b : 2048 * (b + 1)].bitcast(I32)
             nc.sync.dma_start(out=w3raw[b][:], in_=src)
 
-        def load_wo(b, c0, c1):
-            rows = wo[512 * b : 512 * (b + 1), c0:c1].rearrange("(g t i) n -> t g i n", t=4, i=8)
+        def load_wo(b):
+            rows = wo[512 * b : 512 * (b + 1), :].rearrange("(g t i) n -> t g i n", t=4, i=8)
             for t in range(4):
-                nc.sync.dma_start(out=woraw[b, c0][:, t, :], in_=rows[t])
+                nc.sync.dma_start(out=woraw[b][:, t, :], in_=rows[t])
 
         def permute(dst, src, run):
             nc.vector.tensor_copy(
@@ -131,8 +131,8 @@ def tile_list_wheat_reaction_norm_kernel(
         load_weight_scales(nc.sync, wsraw, w1_scales)
         nc.sync.dma_start(out=w1raw[:], in_=w1_words.rearrange("a p c -> p a c").bitcast(I32))
         nc.sync.dma_start(out=t1w[1][:], in_=words(tab_words, 1))
-        for piece in WO_PIECES:
-            load_wo(*piece)
+        load_wo(0)
+        load_wo(1)
 
         crows = curv.rearrange("(b g t i) -> b t g i", b=2, t=4, i=8)
         for b in range(2):
@@ -161,7 +161,7 @@ def tile_list_wheat_reaction_norm_kernel(
         def cast_wo(b, c0, c1):
             nc.scalar.copy(
                 out=woh[b][:, 4 * c0 : 4 * c1].rearrange("p (c i t) -> p c t i", i=2, t=4),
-                in_=woraw[b, c0][:].rearrange("p t (c i) -> p c t i", i=2),
+                in_=woraw[b][:, :, c0:c1].rearrange("p t (c i) -> p c t i", i=2),
             )
 
         def quantize(codes, scales, values):
@@ -169,8 +169,8 @@ def tile_list_wheat_reaction_norm_kernel(
 
         wsb = [keep.tile([P, 4, S], F32, name=f"wsb{b}", tag=("wsb0", "w2raw1")[b], align_bytes=64) for b in range(2)]
         slope0 = keep.tile([P, 4, S], F32, name="slope0", tag="t1s", align_bytes=64)
-        slope1 = [keep.tile([P, 2, S], F32, name=f"slope1{u}", tag=("w1raw", "t1w1")[u], align_bytes=64) for u in range(2)]
-        slope = [[slope0[:, t, :] for t in range(4)], [slope1[t // 2][:, t % 2, :] for t in range(4)]]
+        slope1 = keep.tile([P, 4, S], F32, name="slope1", tag="w1raw", align_bytes=64)
+        slope = [[tile[:, t, :] for t in range(4)] for tile in (slope0, slope1)]
         curved = [keep.tile([P, 4, S], F32, name=f"curved{b}", tag=f"curved{b}", align_bytes=64) for b in range(2)]
 
         def slope_unit(b, t, cv):
@@ -267,9 +267,12 @@ def tile_list_wheat_reaction_norm_kernel(
         w1sp = sb("w1sp", [P, 2, H], U8)
         permute(w1sp[:].bitcast(I32), wsraw[:], 2)
         permute(w1p[:], w1raw[:], 4)
-        slopes(1, (0, 1), (0,), cv)
-        gather(g1w[1], t1w[1][:].bitcast(U32), list1)
-        slopes(1, (2, 3), (2, 3), cv)
+        slopes(1, (0, 1, 2, 3), (0, 1, 2, 3), cv)
+        for half in range(2):
+            nc.vector.tensor_copy(
+                g1w[1][:, HALF * half : HALF * (half + 1)],
+                t1w[1][:].bitcast(U32).indirect(list1[:, 16 * half : 16 * (half + 1)]),
+            )
         h0 = sb("h0", [P, 4, 4 * P], BF16)
         for q in range(4):
             level_unit(0, q, h0[:, q, :], w1sp)
@@ -277,7 +280,7 @@ def tile_list_wheat_reaction_norm_kernel(
         woc = [keep.tile([P, N], U32, name=f"woc{b}", tag=f"woc{b}", align_bytes=64) for b in range(2)]
         cast_wo(0, 0, N)
         quantize(woc[0][:], wos[0][:], woh[0][:])
-        accs = [[bank(f"acc{u}{v}", [P, 2, HALF], LINE_BANKS[0][2 * u + v]) for v in range(2)] for u in range(2)]
+        accs = [[bank(f"acc{u}{v}", [P, 2, HALF], OUT_BANKS[2 * u + v]) for v in range(2)] for u in range(2)]
         for half in range(2):
             for pair in range(2):
                 out_passes(0, half, pair, accs[half][pair])

@@ -64,7 +64,7 @@ def tile_list_wheat_reaction_norm_kernel(
         w3sp = sb("w3sp", [P, 2, H], U8)
         w2raw = [keep.tile([P, 4, 512], F32, name=f"w2raw{b}", tag=f"w2raw{b}", align_bytes=64) for b in range(2)]
         w2h = [sb(f"w2h{b}", [P, 2048], BF16) for b in range(2)]
-        w2c = [keep.tile([P, 512], U32, name=f"w2c{b}", tag=("t2s", "w2c1")[b], align_bytes=64) for b in range(2)]
+        w2c = [keep.tile([P, 512], U32, name=f"w2c{b}", tag=("t2w", "w2c1")[b], align_bytes=64) for b in range(2)]
         w2s = [sb(f"w2s{b}", [P, 512], U8) for b in range(2)]
         woraw = [sb(f"woraw{b}", [P, 4, N], F32) for b in range(2)]
         woh = [keep.tile([P, 4 * N], BF16, name=f"woh{b}", tag=f"half{b}", align_bytes=64) for b in range(2)]
@@ -72,9 +72,9 @@ def tile_list_wheat_reaction_norm_kernel(
         cvrows = sb("cvrows", [P, P], F32)
         ident = sb("ident", [P, P], F32)
 
+        nc.gpsimd.memset(t3s[:].bitcast(I32), 0)
         make_identity(nc, ident[:])
         nc.gpsimd.memset(cvrows[:], 0.0)
-        nc.vector.memset(t3s[:].bitcast(I32), 0)
         nc.vector.memset(wsraw[:], 0)
         nc.vector.memset(t2s[:].bitcast(I32), 0)
         nc.vector.memset(t1s[:].bitcast(I32), 0)
@@ -82,10 +82,10 @@ def tile_list_wheat_reaction_norm_kernel(
         def words(dram, a):
             return dram[a].rearrange("p c i -> p (c i)").bitcast(I32)
 
-        def load_table_scales(eng, tile, dram, first=0):
+        def load_table_scales(eng, tile, dram, first=0, which=range(4)):
             passes = dram.shape[0]
             rows = dram.bitcast(I32).rearrange("a (q r) c -> r q a c", r=4)
-            for r in range(4):
+            for r in which:
                 eng.dma_start(out=tile[first + r : P : 32 // passes, :].bitcast(I32), in_=rows[r])
 
         def load_weight_scales(eng, tile, dram):
@@ -113,19 +113,20 @@ def tile_list_wheat_reaction_norm_kernel(
             )
 
         nc.sync.dma_start(list3[:], offs3)
-        for a in range(2):
-            nc.sync.dma_start(out=t3w[a][:].bitcast(I32), in_=tab3_words[a].bitcast(I32))
+        nc.sync.dma_start(out=t3w[0][:].bitcast(I32), in_=tab3_words[0].bitcast(I32))
         load_weight_scales(nc.sync, t3s[:].bitcast(I32), tab3_scales)
-        load_w2(0)
-        load_weight_scales(nc.sync, wsraw, w3_scales)
         load_w3(0)
+        load_weight_scales(nc.sync, wsraw, w3_scales)
+        nc.sync.dma_start(out=t3w[1][:].bitcast(I32), in_=tab3_words[1].bitcast(I32))
+        load_w2(0)
         nc.sync.dma_start(list2[:], offs2)
         load_table_scales(nc.sync, t2s, tab2_scales, SOIL_PLANE)
         nc.sync.dma_start(out=t2w[:], in_=words(tab2_words, 0))
         load_w3(1)
         nc.sync.dma_start(list1[:], offs)
-        load_table_scales(nc.sync, t1s, tab_scales)
+        load_table_scales(nc.sync, t1s, tab_scales, which=range(1))
         load_w2(1)
+        load_table_scales(nc.sync, t1s, tab_scales, which=range(1, 4))
         nc.sync.dma_start(out=t1w[0][:], in_=words(tab_words, 0))
         permute(w3sp[:].bitcast(I32), wsraw[:], 2)
         load_weight_scales(nc.sync, wsraw, w1_scales)
@@ -137,8 +138,6 @@ def tile_list_wheat_reaction_norm_kernel(
         crows = curv.rearrange("(b g t i) -> b t g i", b=2, t=4, i=8)
         for b in range(2):
             nc.gpsimd.dma_start(out=cvrows[4 * b : 4 * b + 4, :].rearrange("t (g i) -> t g i", i=8), in_=crows[b])
-        cvt = bank("cvt", [P, P], 7)
-        nc.tensor.transpose(cvt[:], cvrows[:], ident[:])
 
         def gather(dst, window, lst):
             nc.vector.tensor_copy(dst[:], window.indirect(lst[:]))
@@ -167,13 +166,18 @@ def tile_list_wheat_reaction_norm_kernel(
         def quantize(codes, scales, values):
             nc.vector.quantize_mx(out=codes.bitcast(FP8X4), scales=scales, in_=values)
 
-        wsb = [keep.tile([P, 4, S], F32, name=f"wsb{b}", tag=("wsb0", "w2raw1")[b], align_bytes=64) for b in range(2)]
-        slope0 = keep.tile([P, 4, S], F32, name="slope0", tag="t1s", align_bytes=64)
+        wflat = [keep.tile([P, 4 * S + 8], F32, name=f"wsb{b}", tag=f"w2raw{b}", align_bytes=64) for b in range(2)]
+        wsb = [tile[:, 0 : 4 * S].rearrange("p (t j) -> p t j", t=4) for tile in wflat]
+        slope0 = keep.tile([P, 4, S], F32, name="slope0", tag="slope0", align_bytes=64)
         slope1 = keep.tile([P, 4, S], F32, name="slope1", tag="w1raw", align_bytes=64)
         slope = [[tile[:, t, :] for t in range(4)] for tile in (slope0, slope1)]
-        curved = [keep.tile([P, 4, S], F32, name=f"curved{b}", tag=f"curved{b}", align_bytes=64) for b in range(2)]
+        curved0 = sb("curved0", [P, 4, S], F32)
+        curved1 = [keep.tile([P, 4, HALF], F32, name=f"curved1{u}", tag=("curved10", "t1w1")[u], align_bytes=64) for u in range(2)]
+        curved = [[curved0[:, :, 0:HALF], curved0[:, :, HALF:S]], [tile[:] for tile in curved1]]
 
-        def slope_unit(b, t, cv):
+        cv = wflat[0][:, 4 * S : 4 * S + 8]
+
+        def weather_unit(b, t):
             cols = slice(P * t, P * (t + 1))
             hcols = slice(512 * b + P * t, 512 * b + P * (t + 1))
             weather = bank("weather", [P, S], WEATHER_BANKS[b][t])
@@ -182,24 +186,18 @@ def tile_list_wheat_reaction_norm_kernel(
                     out=weather[:], lhsT=w3p[b][:, a, cols].bitcast(FP8X4), lhsT_scale=w3sp[:, a, hcols],
                     rhs=g3w[a][:].bitcast(FP4X4), rhs_scale=g3s[a][:], start=(a == 0), stop=(a == 1),
                 )
+            nc.scalar.copy(out=wsb[b][:, t, :], in_=weather[:])
+            return weather
+
+        def slope_unit(b, t):
+            cols = slice(P * t, P * (t + 1))
             soil = bank("soil", [P, S], SOIL_BANKS[b][t])
             nc.tensor.matmul_mx(
                 out=soil[:], lhsT=w2c[b][:, cols].bitcast(FP8X4), lhsT_scale=w2s[b][:, cols],
                 rhs=g2w[:].bitcast(FP8X4), rhs_scale=g2s[SOIL_PLANE:P, :], start=True, stop=True,
             )
-            nc.scalar.copy(out=wsb[b][:, t, :], in_=weather[:])
             nc.vector.scalar_tensor_tensor(slope[b][t], wsb[b][:, t, :], cv[:, 4 * b + t : 4 * b + t + 1], soil[:], MULT, ADD)
-            return weather
 
-        def slopes(b, ts, shared, cv):
-            banks = {}
-            for t in ts:
-                banks[t] = slope_unit(b, t, cv)
-                if t in shared:
-                    nc.gpsimd.tensor_tensor(curved[b][:, t, :], slope[b][t], wsb[b][:, t, :], MULT)
-            for t in ts:
-                if t not in shared:
-                    nc.vector.tensor_tensor(curved[b][:, t, :], slope[b][t], banks[t][:], MULT)
 
         hc = [sb(f"hc{b}", [P, S], U32) for b in range(2)]
         hs = [sb(f"hs{b}", [P, S], U8) for b in range(2)]
@@ -219,7 +217,7 @@ def tile_list_wheat_reaction_norm_kernel(
             nc.vector.tensor_tensor(
                 hh.rearrange("p (c i t) -> p c t i", i=2, t=4),
                 line[:].rearrange("p t (c i) -> p c t i", i=2),
-                curved[b][:, :, toks].rearrange("p t (c i) -> p c t i", i=2),
+                curved[b][q // 2][:, :, P * (q % 2) : P * (q % 2 + 1)].rearrange("p t (c i) -> p c t i", i=2),
                 ADD,
             )
 
@@ -235,62 +233,84 @@ def tile_list_wheat_reaction_norm_kernel(
 
         out_rows = out.rearrange("(m p) j -> p m j", p=P)
 
-        def finish(half):
-            toks = slice(HALF * half, HALF * (half + 1))
-            quantize(hc[1][:, toks], hs[1][:, toks], h1[:, 2 * half : 2 * half + 2, :].rearrange("p q c -> p (q c)"))
-            for pair in range(2):
-                out_passes(1, half, pair, accs[half][pair])
-            for pair in range(2):
-                res = sb(f"res{half}{pair}", [P, 2, HALF], F32)
-                copy = nc.vector.tensor_copy if (half, pair) == (1, 0) else nc.scalar.copy
-                copy(out=res[:], in_=accs[half][pair][:])
-                nc.sync.dma_start(out=out_rows[:, 2 * pair : 2 * pair + 2, toks], in_=res[:])
-
         gather(g3w[0], t3w[0][:], list3)
-        gather(g3w[1], t3w[1][:], list3)
         gather(g3s[0], t3s[:, 0, :], list3)
         gather(g3s[1], t3s[:, 1, :], list3)
-        cast_w2(0)
-        cv = keep.tile([P, 8], F32, name="cv", tag="w2raw0", align_bytes=64)
-        nc.scalar.copy(out=cv[:], in_=cvt[:, 0:8])
         permute_w3(0)
+        gather(g3w[1], t3w[1][:], list3)
+        cast_w2(0)
         gather(g2s, t2s[:], list2)
-        quantize(w2c[0][:], w2s[0][:], w2h[0][:])
         gather(g2w, t2w[:].bitcast(U32), list2)
+        quantize(w2c[0][:], w2s[0][:], w2h[0][:])
         permute_w3(1)
+        weather_unit(0, 0)
+        cvt = bank("cvt", [P, P], WEATHER_BANKS[0][0])
+        nc.tensor.transpose(cvt[:], cvrows[:], ident[:])
+        weather_unit(0, 1)
+        nc.scalar.copy(out=cv, in_=cvt[:, 0:8])
+        kept = weather_unit(0, 2)
+        weather_unit(0, 3)
+        for t in range(4):
+            slope_unit(0, t)
+            if t != 2:
+                nc.gpsimd.tensor_tensor(curved0[:, t, :], slope[0][t], wsb[0][:, t, :], MULT)
+        nc.vector.tensor_tensor(curved0[:, 2, :], slope[0][2], kept[:], MULT)
         gather(g1s[0], t1s[:], list1)
         shift(g1s)
-        slopes(0, (0, 1, 2, 3), (0, 1), cv)
         cast_w2(1)
         quantize(w2c[1][:], w2s[1][:], w2h[1][:])
         gather(g1w[0], t1w[0][:].bitcast(U32), list1)
         w1sp = sb("w1sp", [P, 2, H], U8)
         permute(w1sp[:].bitcast(I32), wsraw[:], 2)
         permute(w1p[:], w1raw[:], 4)
-        slopes(1, (0, 1, 2, 3), (0, 1, 2, 3), cv)
+        for t in range(4):
+            weather_unit(1, t)
+            slope_unit(1, t)
+            nc.gpsimd.tensor_tensor(curved1[0][:, t, :], slope[1][t][:, 0:HALF], wsb[1][:, t, 0:HALF], MULT)
         for half in range(2):
             nc.vector.tensor_copy(
                 g1w[1][:, HALF * half : HALF * (half + 1)],
                 t1w[1][:].bitcast(U32).indirect(list1[:, 16 * half : 16 * (half + 1)]),
             )
+        for t in range(4):
+            nc.gpsimd.tensor_tensor(curved1[1][:, t, :], slope[1][t][:, HALF:S], wsb[1][:, t, HALF:S], MULT)
         h0 = sb("h0", [P, 4, 4 * P], BF16)
-        for q in range(4):
-            level_unit(0, q, h0[:, q, :], w1sp)
-        quantize(hc[0][:], hs[0][:], h0[:].rearrange("p q c -> p (q c)"))
+        h1 = sb("h1", [P, 4, 4 * P], BF16)
         woc = [keep.tile([P, N], U32, name=f"woc{b}", tag=f"woc{b}", align_bytes=64) for b in range(2)]
-        cast_wo(0, 0, N)
-        quantize(woc[0][:], wos[0][:], woh[0][:])
         accs = [[bank(f"acc{u}{v}", [P, 2, HALF], OUT_BANKS[2 * u + v]) for v in range(2)] for u in range(2)]
-        for half in range(2):
-            for pair in range(2):
-                out_passes(0, half, pair, accs[half][pair])
-        for pair in range(2):
+
+        def quantize_h1(half):
+            toks = slice(HALF * half, HALF * (half + 1))
+            quantize(hc[1][:, toks], hs[1][:, toks], h1[:, 2 * half : 2 * half + 2, :].rearrange("p q c -> p (q c)"))
+
+        def quantize_wo1(pair):
             cols = slice(HALF * pair, HALF * (pair + 1))
             cast_wo(1, HALF * pair, HALF * (pair + 1))
             quantize(woc[1][:, cols], wos[1][:, cols], woh[1][:, 4 * HALF * pair : 4 * HALF * (pair + 1)])
-        h1 = sb("h1", [P, 4, 4 * P], BF16)
-        for q in range(3):
-            level_unit(1, q, h1[:, q, :], w1sp)
-        finish(0)
+
+        def finish(half, pair, copy):
+            out_passes(1, half, pair, accs[half][pair])
+            res = sb(f"res{half}{pair}", [P, 2, HALF], F32)
+            copy(out=res[:], in_=accs[half][pair][:])
+            nc.sync.dma_start(out=out_rows[:, 2 * pair : 2 * pair + 2, HALF * half : HALF * (half + 1)], in_=res[:])
+
+        for q in range(4):
+            level_unit(0, q, h0[:, q, :], w1sp)
+        level_unit(1, 0, h1[:, 0, :], w1sp)
+        quantize(hc[0][:], hs[0][:], h0[:].rearrange("p q c -> p (q c)"))
+        level_unit(1, 1, h1[:, 1, :], w1sp)
+        cast_wo(0, 0, N)
+        quantize(woc[0][:], wos[0][:], woh[0][:])
+        for half in range(2):
+            for pair in range(2):
+                out_passes(0, half, pair, accs[half][pair])
+        level_unit(1, 2, h1[:, 2, :], w1sp)
+        quantize_h1(0)
+        quantize_wo1(0)
+        finish(0, 0, nc.scalar.copy)
         level_unit(1, 3, h1[:, 3, :], w1sp)
-        finish(1)
+        quantize_wo1(1)
+        finish(0, 1, nc.scalar.copy)
+        quantize_h1(1)
+        finish(1, 0, nc.vector.tensor_copy)
+        finish(1, 1, nc.scalar.copy)

@@ -72,9 +72,9 @@ def tile_list_wheat_reaction_norm_kernel(
         cvrows = sb("cvrows", [P, P], F32)
         ident = sb("ident", [P, P], F32)
 
-        nc.gpsimd.memset(t3s[:].bitcast(I32), 0)
         make_identity(nc, ident[:])
         nc.gpsimd.memset(cvrows[:], 0.0)
+        nc.vector.memset(t3s[:].bitcast(I32), 0)
         nc.vector.memset(wsraw[:], 0)
         nc.vector.memset(t2s[:].bitcast(I32), 0)
         nc.vector.memset(t1s[:].bitcast(I32), 0)

@@ -64,7 +64,7 @@ def tile_list_wheat_reaction_norm_kernel(
         w3sp = sb("w3sp", [P, 2, H], U8)
         w2raw = [keep.tile([P, 4, 512], F32, name=f"w2raw{b}", tag=f"w2raw{b}", align_bytes=64) for b in range(2)]
         w2h = [sb(f"w2h{b}", [P, 2048], BF16) for b in range(2)]
-        w2c = [keep.tile([P, 512], U32, name=f"w2c{b}", tag=("t2w", "w2c1")[b], align_bytes=64) for b in range(2)]
+        w2c = [keep.tile([P, 512], U32, name=f"w2c{b}", tag=("t2w", "t1w0")[b], align_bytes=64) for b in range(2)]
         w2s = [sb(f"w2s{b}", [P, 512], U8) for b in range(2)]
         woraw = [sb(f"woraw{b}", [P, 4, N], F32) for b in range(2)]
         woh = [keep.tile([P, 4 * N], BF16, name=f"woh{b}", tag=f"half{b}", align_bytes=64) for b in range(2)]
@@ -101,13 +101,13 @@ def tile_list_wheat_reaction_norm_kernel(
             src = w3_words.rearrange("a p c i -> p a (c i)")[:, :, 2048 * b : 2048 * (b + 1)].bitcast(I32)
             nc.sync.dma_start(out=w3raw[b][:], in_=src)
 
-        def load_wo(b):
+        def load_wo(b, ts):
             rows = wo[512 * b : 512 * (b + 1), :].rearrange("(g t i) n -> t g i n", t=4, i=8)
-            for t in range(4):
+            for t in ts:
                 nc.sync.dma_start(out=woraw[b][:, t, :], in_=rows[t])
 
-        def permute(dst, src, run):
-            nc.vector.tensor_copy(
+        def permute(eng, dst, src, run):
+            eng.tensor_copy(
                 out=dst.rearrange("p a (b t g i) -> p (a b) t g i", t=4, g=16, i=run),
                 in_=src.rearrange("p a (b g t i) -> p (a b) t g i", t=4, g=16, i=run),
             )
@@ -128,12 +128,11 @@ def tile_list_wheat_reaction_norm_kernel(
         load_w2(1)
         load_table_scales(nc.sync, t1s, tab_scales, which=range(1, 4))
         nc.sync.dma_start(out=t1w[0][:], in_=words(tab_words, 0))
-        permute(w3sp[:].bitcast(I32), wsraw[:], 2)
+        permute(nc.gpsimd, w3sp[:].bitcast(I32), wsraw[:], 2)
         load_weight_scales(nc.sync, wsraw, w1_scales)
         nc.sync.dma_start(out=w1raw[:], in_=w1_words.rearrange("a p c -> p a c").bitcast(I32))
         nc.sync.dma_start(out=t1w[1][:], in_=words(tab_words, 1))
-        load_wo(0)
-        load_wo(1)
+        load_wo(0, (0, 1))
 
         crows = curv.rearrange("(b g t i) -> b t g i", b=2, t=4, i=8)
         for b in range(2):
@@ -143,10 +142,10 @@ def tile_list_wheat_reaction_norm_kernel(
             nc.vector.tensor_copy(dst[:], window.indirect(lst[:]))
 
         def shift(g):
-            nc.gpsimd.dma_start(out=g[1][0:112, :].bitcast(I32), in_=g[0][16:128, :].bitcast(I32))
+            nc.sync.dma_start(out=g[1][0:112, :].bitcast(I32), in_=g[0][16:128, :].bitcast(I32))
 
         def permute_w3(b):
-            nc.vector.tensor_copy(
+            (nc.gpsimd, nc.vector)[b].tensor_copy(
                 out=w3p[b][:].rearrange("p a (t g i) -> p a t g i", t=4, i=8),
                 in_=w3raw[b][:].rearrange("p a (g t i) -> p a t g i", t=4, i=8),
             )
@@ -257,12 +256,14 @@ def tile_list_wheat_reaction_norm_kernel(
         nc.vector.tensor_tensor(curved0[:, 2, :], slope[0][2], kept[:], MULT)
         gather(g1s[0], t1s[:], list1)
         shift(g1s)
+        load_wo(0, (2, 3))
+        load_wo(1, range(4))
         cast_w2(1)
         quantize(w2c[1][:], w2s[1][:], w2h[1][:])
         gather(g1w[0], t1w[0][:].bitcast(U32), list1)
         w1sp = sb("w1sp", [P, 2, H], U8)
-        permute(w1sp[:].bitcast(I32), wsraw[:], 2)
-        permute(w1p[:], w1raw[:], 4)
+        permute(nc.vector, w1sp[:].bitcast(I32), wsraw[:], 2)
+        permute(nc.vector, w1p[:], w1raw[:], 4)
         for t in range(4):
             weather_unit(1, t)
             slope_unit(1, t)

@@ -20,10 +20,6 @@ ADD = mybir.AluOpType.add
 P = 128
 HALF = 256
 SOIL_PLANE = 4
-WEATHER_BANKS = ((0, 1, 2, 3), (0, 1, 4, 5))
-SOIL_BANKS = ((4, 5, 6, 7), (0, 1, 4, 5))
-LINE_BANKS = ((2, 3, 6, 7), (2, 3, 6, 7))
-OUT_BANKS = (0, 1, 4, 5)
 
 
 def tile_list_wheat_reaction_norm_kernel(
@@ -38,116 +34,107 @@ def tile_list_wheat_reaction_norm_kernel(
         def sb(name, shape, dtype):
             return keep.tile(shape, dtype, name=name, align_bytes=64)
 
+        def pair(name, shape, dtype):
+            return [sb(f"{name}{k}", shape, dtype) for k in range(2)]
+
         def bank(name, shape, index):
             return psum.tile(shape, F32, name=name, tag=f"bank{index}")
 
         list1 = sb("list1", [P, S // 16], U16)
         list2 = sb("list2", [P, S // 16], U16)
         list3 = sb("list3", [P, S // 16], U16)
-        t1w = [keep.tile([P, T], I32, name=f"t1w{a}", tag=f"t1w{a}", align_bytes=64) for a in range(2)]
-        t2w = keep.tile([P, T2], I32, name="t2w", tag="t2w", align_bytes=64)
-        t3w = [sb(f"t3w{a}", [P, T3], U16) for a in range(2)]
-        t1s = keep.tile([P, T], U8, name="t1s", tag="t1s", align_bytes=64)
-        t2s = keep.tile([P, T2], U8, name="t2s", tag="t2s", align_bytes=64)
+        t1w = pair("t1w", [P, T], U32)
+        t2w = keep.tile([P, T2], U32, name="t2w", tag="t2w", align_bytes=64)
+        t3w = pair("t3w", [P, T3], U16)
+        t1s = sb("t1s", [P, T], U8)
+        t2s = sb("t2s", [P, T2], U8)
         t3s = sb("t3s", [P, 2, T3], U8)
-        g1w = [sb(f"g1w{a}", [P, S], U32) for a in range(2)]
+        g1w = pair("g1w", [P, S], U32)
         g2w = sb("g2w", [P, S], U32)
-        g3w = [sb(f"g3w{a}", [P, S], U16) for a in range(2)]
-        g1s = [sb(f"g1s{a}", [P, S], U8) for a in range(2)]
+        g3w = pair("g3w", [P, S], U16)
+        g1s = pair("g1s", [P, S], U8)
         g2s = sb("g2s", [P, S], U8)
-        g3s = [sb(f"g3s{a}", [P, S], U8) for a in range(2)]
-        w1raw = keep.tile([P, 2, H // 2], I32, name="w1raw", tag="w1raw", align_bytes=64)
-        w1p = sb("w1p", [P, 2, H // 2], I32)
-        w3raw = [keep.tile([P, 2, 512], I32, name=f"w3raw{b}", tag=f"w3raw{b}", align_bytes=64) for b in range(2)]
-        w3p = [sb(f"w3p{b}", [P, 2, 512], I32) for b in range(2)]
-        wsraw = sb("wsraw", [P, 2, H // 4], I32)
-        w3sp = sb("w3sp", [P, 2, H], U8)
+        g3s = pair("g3s", [P, S], U8)
+        w1raw = sb("w1raw", [P, 2, H // 2], U32)
+        w1p = pair("w1p", [P, 2, 256], U32)
+        w1sp = pair("w1sp", [P, 2, 128], U32)
+        w3raw = pair("w3raw", [P, 2, 512], U32)
+        w3p = pair("w3p", [P, 2, 512], U32)
+        wsraw = sb("wsraw", [P, 2, H // 4], U32)
+        w3sp = pair("w3sp", [P, 2, 128], U32)
         w2raw = [keep.tile([P, 4, 512], F32, name=f"w2raw{b}", tag=f"w2raw{b}", align_bytes=64) for b in range(2)]
-        w2h = [sb(f"w2h{b}", [P, 2048], BF16) for b in range(2)]
-        w2c = [keep.tile([P, 512], U32, name=f"w2c{b}", tag=("t2w", "t1w0")[b], align_bytes=64) for b in range(2)]
-        w2s = [sb(f"w2s{b}", [P, 512], U8) for b in range(2)]
-        woraw = [sb(f"woraw{b}", [P, 4, N], F32) for b in range(2)]
-        woh = [keep.tile([P, 4 * N], BF16, name=f"woh{b}", tag=f"half{b}", align_bytes=64) for b in range(2)]
-        wos = [sb(f"wos{b}", [P, N], U8) for b in range(2)]
+        w2h = pair("w2h", [P, 2048], BF16)
+        w2c = [keep.tile([P, 512], U32, name=f"w2c{b}", tag=("t2w", "w2c1")[b], align_bytes=64) for b in range(2)]
+        w2s = pair("w2s", [P, 512], U8)
+        woraw = pair("woraw", [P, 4, N], F32)
+        woh = [keep.tile([P, 4 * N], BF16, name=f"woh{b}", tag=f"woh{b}", align_bytes=64) for b in range(2)]
+        woc = pair("woc", [P, N], U32)
+        wos = pair("wos", [P, N], U8)
         cvrows = sb("cvrows", [P, P], F32)
         ident = sb("ident", [P, P], F32)
+        cv = sb("cv", [P, 8], F32)
+        wsb = [keep.tile([P, 4, S], F32, name=f"wsb{b}", tag=f"w2raw{b}", align_bytes=64) for b in range(2)]
+        slope = pair("slope", [P, 4, S], F32)
+        curved0 = sb("curved0", [P, 4, S], F32)
+        curved1 = pair("curved1", [P, 4, HALF], F32)
+        curved = [[curved0[:, :, 0:HALF], curved0[:, :, HALF:S]], [tile[:] for tile in curved1]]
+        h0 = sb("h0", [P, 4 * S], BF16)
+        hc = pair("hc", [P, S], U32)
+        hs = pair("hs", [P, S], U8)
 
-        make_identity(nc, ident[:])
-        nc.gpsimd.memset(cvrows[:], 0.0)
         nc.vector.memset(t3s[:].bitcast(I32), 0)
-        nc.vector.memset(wsraw[:], 0)
+        nc.vector.memset(wsraw[:].bitcast(I32), 0)
         nc.vector.memset(t2s[:].bitcast(I32), 0)
         nc.vector.memset(t1s[:].bitcast(I32), 0)
+        nc.gpsimd.memset(cvrows[:], 0.0)
+        crows = curv.rearrange("(b g t i) -> b t g i", b=2, t=4, i=8)
+        for b in range(2):
+            nc.gpsimd.dma_start(out=cvrows[4 * b : 4 * b + 4, :].rearrange("t (g i) -> t g i", i=8), in_=crows[b])
+        make_identity(nc, ident[:])
+
+        def load(tile, src):
+            nc.sync.dma_start(out=tile.bitcast(I32), in_=src.bitcast(I32))
 
         def words(dram, a):
-            return dram[a].rearrange("p c i -> p (c i)").bitcast(I32)
+            return dram[a].rearrange("p c i -> p (c i)")
 
-        def load_table_scales(eng, tile, dram, first=0, which=range(4)):
-            passes = dram.shape[0]
-            rows = dram.bitcast(I32).rearrange("a (q r) c -> r q a c", r=4)
-            for r in which:
-                eng.dma_start(out=tile[first + r : P : 32 // passes, :].bitcast(I32), in_=rows[r])
+        def scale_rows(dram):
+            return dram.bitcast(I32).rearrange("a (q r) c -> r q a c", r=4)
 
-        def load_weight_scales(eng, tile, dram):
-            rows = dram.bitcast(I32).rearrange("a (q r) c -> r q a c", r=4)
+        def load_stacked_scales(tile, dram, first=0):
+            rows = scale_rows(dram)
             for r in range(4):
-                eng.dma_start(out=tile[r:P:32, :, :], in_=rows[r])
+                nc.sync.dma_start(out=tile[first + r : P : 32 // dram.shape[0], :].bitcast(I32), in_=rows[r])
+
+        def load_scales(tile, dram):
+            rows = scale_rows(dram)
+            for r in range(4):
+                nc.sync.dma_start(out=tile[r:P:32, :, :].bitcast(I32), in_=rows[r])
 
         def load_w2(b):
             nc.sync.dma_start(out=w2raw[b][:], in_=w2[:, 512 * b : 512 * (b + 1)].rearrange("(p j) c -> p j c", j=4))
 
-
         def load_w3(b):
-            src = w3_words.rearrange("a p c i -> p a (c i)")[:, :, 2048 * b : 2048 * (b + 1)].bitcast(I32)
-            nc.sync.dma_start(out=w3raw[b][:], in_=src)
+            load(w3raw[b][:], w3_words.rearrange("a p c i -> p a (c i)")[:, :, 2048 * b : 2048 * (b + 1)])
 
-        def load_wo(b, ts):
+        def load_wo(b):
             rows = wo[512 * b : 512 * (b + 1), :].rearrange("(g t i) n -> t g i n", t=4, i=8)
-            for t in ts:
+            for t in range(4):
                 nc.sync.dma_start(out=woraw[b][:, t, :], in_=rows[t])
 
-        def permute(eng, dst, src, run):
-            eng.tensor_copy(
-                out=dst.rearrange("p a (b t g i) -> p (a b) t g i", t=4, g=16, i=run),
-                in_=src.rearrange("p a (b g t i) -> p (a b) t g i", t=4, g=16, i=run),
+        def gather(dst, window, lst):
+            nc.vector.tensor_copy(dst, window.indirect(lst))
+
+        def reorder(dst, src, copy=nc.scalar.copy):
+            copy(
+                out=dst.rearrange("p a (t g i) -> p a t g i", t=4, g=16),
+                in_=src.rearrange("p a (g t i) -> p a t g i", t=4, g=16),
             )
 
-        nc.sync.dma_start(list3[:], offs3)
-        nc.sync.dma_start(out=t3w[0][:].bitcast(I32), in_=tab3_words[0].bitcast(I32))
-        load_weight_scales(nc.sync, t3s[:].bitcast(I32), tab3_scales)
-        load_w3(0)
-        load_weight_scales(nc.sync, wsraw, w3_scales)
-        nc.sync.dma_start(out=t3w[1][:].bitcast(I32), in_=tab3_words[1].bitcast(I32))
-        load_w2(0)
-        nc.sync.dma_start(list2[:], offs2)
-        load_table_scales(nc.sync, t2s, tab2_scales, SOIL_PLANE)
-        nc.sync.dma_start(out=t2w[:], in_=words(tab2_words, 0))
-        load_w3(1)
-        nc.sync.dma_start(list1[:], offs)
-        load_table_scales(nc.sync, t1s, tab_scales, which=range(1))
-        load_w2(1)
-        load_table_scales(nc.sync, t1s, tab_scales, which=range(1, 4))
-        nc.sync.dma_start(out=t1w[0][:], in_=words(tab_words, 0))
-        permute(nc.gpsimd, w3sp[:].bitcast(I32), wsraw[:], 2)
-        load_weight_scales(nc.sync, wsraw, w1_scales)
-        nc.sync.dma_start(out=w1raw[:], in_=w1_words.rearrange("a p c -> p a c").bitcast(I32))
-        nc.sync.dma_start(out=t1w[1][:], in_=words(tab_words, 1))
-        load_wo(0, (0, 1))
-
-        crows = curv.rearrange("(b g t i) -> b t g i", b=2, t=4, i=8)
-        for b in range(2):
-            nc.gpsimd.dma_start(out=cvrows[4 * b : 4 * b + 4, :].rearrange("t (g i) -> t g i", i=8), in_=crows[b])
-
-        def gather(dst, window, lst):
-            nc.vector.tensor_copy(dst[:], window.indirect(lst[:]))
-
-        def shift(g):
-            nc.sync.dma_start(out=g[1][0:112, :].bitcast(I32), in_=g[0][16:128, :].bitcast(I32))
-
-        def permute_w3(b):
-            (nc.gpsimd, nc.vector)[b].tensor_copy(
-                out=w3p[b][:].rearrange("p a (t g i) -> p a t g i", t=4, i=8),
-                in_=w3raw[b][:].rearrange("p a (g t i) -> p a t g i", t=4, i=8),
+        def reorder_w3_slot(b, t):
+            nc.scalar.copy(
+                out=w3p[b][:, :, P * t : P * (t + 1)].rearrange("p a (g i) -> p a g i", g=16),
+                in_=w3raw[b][:].rearrange("p a (g t i) -> p a t g i", t=4, g=16)[:, :, t],
             )
 
         def cast_w2(b):
@@ -162,156 +149,149 @@ def tile_list_wheat_reaction_norm_kernel(
                 in_=woraw[b][:, :, c0:c1].rearrange("p t (c i) -> p c t i", i=2),
             )
 
-        def quantize(codes, scales, values):
-            nc.vector.quantize_mx(out=codes.bitcast(FP8X4), scales=scales, in_=values)
+        def quantize(codes, scales, values, c0, c1):
+            nc.vector.quantize_mx(out=codes[:, c0:c1].bitcast(FP8X4), scales=scales[:, c0:c1], in_=values[:, 4 * c0 : 4 * c1])
 
-        wflat = [keep.tile([P, 4 * S + 8], F32, name=f"wsb{b}", tag=f"w2raw{b}", align_bytes=64) for b in range(2)]
-        wsb = [tile[:, 0 : 4 * S].rearrange("p (t j) -> p t j", t=4) for tile in wflat]
-        slope0 = keep.tile([P, 4, S], F32, name="slope0", tag="slope0", align_bytes=64)
-        slope1 = keep.tile([P, 4, S], F32, name="slope1", tag="w1raw", align_bytes=64)
-        slope = [[tile[:, t, :] for t in range(4)] for tile in (slope0, slope1)]
-        curved0 = sb("curved0", [P, 4, S], F32)
-        curved1 = [keep.tile([P, 4, HALF], F32, name=f"curved1{u}", tag=("curved10", "t1w1")[u], align_bytes=64) for u in range(2)]
-        curved = [[curved0[:, :, 0:HALF], curved0[:, :, HALF:S]], [tile[:] for tile in curved1]]
-
-        cv = wflat[0][:, 4 * S : 4 * S + 8]
-
-        def weather_unit(b, t):
+        def weather_sum(b, t):
             cols = slice(P * t, P * (t + 1))
-            hcols = slice(512 * b + P * t, 512 * b + P * (t + 1))
-            weather = bank("weather", [P, S], WEATHER_BANKS[b][t])
+            weather = bank("weather", [P, S], t)
             for a in range(2):
                 nc.tensor.matmul_mx(
-                    out=weather[:], lhsT=w3p[b][:, a, cols].bitcast(FP8X4), lhsT_scale=w3sp[:, a, hcols],
+                    out=weather[:], lhsT=w3p[b][:, a, cols].bitcast(FP8X4), lhsT_scale=w3sp[b][:, a, :].bitcast(U8)[:, cols],
                     rhs=g3w[a][:].bitcast(FP4X4), rhs_scale=g3s[a][:], start=(a == 0), stop=(a == 1),
                 )
             nc.scalar.copy(out=wsb[b][:, t, :], in_=weather[:])
-            return weather
 
-        def slope_unit(b, t):
+        def slope_sum(b, t):
             cols = slice(P * t, P * (t + 1))
-            soil = bank("soil", [P, S], SOIL_BANKS[b][t])
+            soil = bank("soil", [P, S], 4 + t)
             nc.tensor.matmul_mx(
                 out=soil[:], lhsT=w2c[b][:, cols].bitcast(FP8X4), lhsT_scale=w2s[b][:, cols],
                 rhs=g2w[:].bitcast(FP8X4), rhs_scale=g2s[SOIL_PLANE:P, :], start=True, stop=True,
             )
-            nc.vector.scalar_tensor_tensor(slope[b][t], wsb[b][:, t, :], cv[:, 4 * b + t : 4 * b + t + 1], soil[:], MULT, ADD)
+            nc.vector.scalar_tensor_tensor(slope[b][:, t, :], wsb[b][:, t, :], cv[:, 4 * b + t : 4 * b + t + 1], soil[:], MULT, ADD)
 
+        def product(t, half):
+            toks = slice(HALF * half, HALF * (half + 1))
+            nc.gpsimd.tensor_tensor(curved1[half][:, t, :], slope[1][:, t, toks], wsb[1][:, t, toks], MULT)
 
-        hc = [sb(f"hc{b}", [P, S], U32) for b in range(2)]
-        hs = [sb(f"hs{b}", [P, S], U8) for b in range(2)]
-
-        def level_unit(b, q, hh, w1sp):
+        def level_sum(b, q, dst):
             toks = slice(P * q, P * (q + 1))
-            line = bank("line", [P, 4, P], LINE_BANKS[b][q])
+            line = bank("line", [P, 4, P], q)
             for a in range(2):
                 for t in range(4):
-                    c0 = 512 * b + P * t
                     nc.tensor.matmul_mx(
-                        out=line[:, t, :], lhsT=w1p[:, a, c0 // 2 : (c0 + P) // 2].bitcast(FP4X4),
-                        lhsT_scale=w1sp[:, a, c0 : c0 + P],
+                        out=line[:, t, :], lhsT=w1p[b][:, a, 64 * t : 64 * (t + 1)].bitcast(FP4X4),
+                        lhsT_scale=w1sp[b][:, a, :].bitcast(U8)[:, P * t : P * (t + 1)],
                         rhs=g1w[a][:, toks].bitcast(FP8X4), rhs_scale=g1s[a][:, toks],
                         start=(a == 0 and t == 0), stop=(a == 1 and t == 3),
                     )
             nc.vector.tensor_tensor(
-                hh.rearrange("p (c i t) -> p c t i", i=2, t=4),
+                dst.rearrange("p (c i t) -> p c t i", i=2, t=4),
                 line[:].rearrange("p t (c i) -> p c t i", i=2),
                 curved[b][q // 2][:, :, P * (q % 2) : P * (q % 2 + 1)].rearrange("p t (c i) -> p c t i", i=2),
                 ADD,
             )
 
-        def out_passes(b, half, pair, acc):
+        def out_passes(b, half, side, acc):
             toks = slice(HALF * half, HALF * (half + 1))
             for k in range(2):
-                cols = slice(P * (2 * pair + k), P * (2 * pair + k + 1))
+                cols = slice(P * (2 * side + k), P * (2 * side + k + 1))
                 nc.tensor.matmul_mx(
                     out=acc[:, k, :], lhsT=woc[b][:, cols].bitcast(FP8X4), lhsT_scale=wos[b][:, cols],
                     rhs=hc[b][:, toks].bitcast(FP8X4), rhs_scale=hs[b][:, toks],
                     start=(b == 0 and k == 0), stop=(b == 1 and k == 1),
                 )
 
+        nc.sync.dma_start(list3[:], offs3)
+        load(t3w[0][:], tab3_words[0])
+        load_scales(t3s, tab3_scales)
+        load(t3w[1][:], tab3_words[1])
+        load_w3(0)
+        load_scales(wsraw, w3_scales)
+        load_w2(0)
+        nc.sync.dma_start(list2[:], offs2)
+        load_stacked_scales(t2s, tab2_scales, SOIL_PLANE)
+        load(t2w[:], words(tab2_words, 0))
+        load_w3(1)
+        nc.sync.dma_start(list1[:], offs)
+        load_stacked_scales(t1s, tab_scales)
+        load_w2(1)
+        load(t1w[0][:], words(tab_words, 0))
+        for b in range(2):
+            reorder(w3sp[b][:], wsraw[:, :, 128 * b : 128 * (b + 1)])
+        load_scales(wsraw, w1_scales)
+        load(w1raw[:], w1_words.rearrange("a p c -> p a c"))
+        load(t1w[1][:], words(tab_words, 1))
+
+        gather(g3w[0][:], t3w[0][:], list3[:])
+        for a in range(2):
+            gather(g3s[a][:], t3s[:, a, :], list3[:])
+        gather(g3w[1][:], t3w[1][:], list3[:])
+        for t in range(4):
+            reorder_w3_slot(0, t)
+        cast_w2(0)
+        gather(g2s[:], t2s[:], list2[:])
+        gather(g2w[:], t2w[:], list2[:])
+        quantize(w2c[0], w2s[0], w2h[0], 0, 512)
+        reorder(w3p[1][:], w3raw[1][:], nc.gpsimd.tensor_copy)
+        weather_sum(0, 0)
+        cvt = bank("cvt", [P, P], 0)
+        nc.tensor.transpose(cvt[:], cvrows[:], ident[:])
+        nc.scalar.copy(out=cv[:], in_=cvt[:, 0:8])
+        for t in range(1, 4):
+            weather_sum(0, t)
+        for t in range(4):
+            slope_sum(0, t)
+            nc.gpsimd.tensor_tensor(curved0[:, t, :], slope[0][:, t, :], wsb[0][:, t, :], MULT)
+        gather(g1s[0][:], t1s[:], list1[:])
+        nc.sync.dma_start(out=g1s[1][0:112, :].bitcast(I32), in_=g1s[0][16:128, :].bitcast(I32))
+        load_wo(0)
+        load_wo(1)
+        cast_w2(1)
+        for u in range(2):
+            quantize(w2c[1], w2s[1], w2h[1], HALF * u, HALF * (u + 1))
+        gather(g1w[0][:], t1w[0][:], list1[:])
+        for t in range(4):
+            weather_sum(1, t)
+        for t in range(4):
+            slope_sum(1, t)
+            product(t, 0)
+        for b in range(2):
+            reorder(w1sp[b][:], wsraw[:, :, 128 * b : 128 * (b + 1)])
+            reorder(w1p[b][:], w1raw[:, :, 256 * b : 256 * (b + 1)])
+        for half in range(2):
+            gather(g1w[1][:, HALF * half : HALF * (half + 1)], t1w[1][:], list1[:, 16 * half : 16 * (half + 1)])
+        for t in range(4):
+            product(t, 1)
+
         out_rows = out.rearrange("(m p) j -> p m j", p=P)
 
-        gather(g3w[0], t3w[0][:], list3)
-        gather(g3s[0], t3s[:, 0, :], list3)
-        gather(g3s[1], t3s[:, 1, :], list3)
-        permute_w3(0)
-        gather(g3w[1], t3w[1][:], list3)
-        cast_w2(0)
-        gather(g2s, t2s[:], list2)
-        gather(g2w, t2w[:].bitcast(U32), list2)
-        quantize(w2c[0][:], w2s[0][:], w2h[0][:])
-        permute_w3(1)
-        weather_unit(0, 0)
-        cvt = bank("cvt", [P, P], WEATHER_BANKS[0][0])
-        nc.tensor.transpose(cvt[:], cvrows[:], ident[:])
-        weather_unit(0, 1)
-        nc.scalar.copy(out=cv, in_=cvt[:, 0:8])
-        kept = weather_unit(0, 2)
-        weather_unit(0, 3)
-        for t in range(4):
-            slope_unit(0, t)
-            if t != 2:
-                nc.gpsimd.tensor_tensor(curved0[:, t, :], slope[0][t], wsb[0][:, t, :], MULT)
-        nc.vector.tensor_tensor(curved0[:, 2, :], slope[0][2], kept[:], MULT)
-        gather(g1s[0], t1s[:], list1)
-        shift(g1s)
-        load_wo(0, (2, 3))
-        load_wo(1, range(4))
-        cast_w2(1)
-        quantize(w2c[1][:], w2s[1][:], w2h[1][:])
-        gather(g1w[0], t1w[0][:].bitcast(U32), list1)
-        w1sp = sb("w1sp", [P, 2, H], U8)
-        permute(nc.vector, w1sp[:].bitcast(I32), wsraw[:], 2)
-        permute(nc.vector, w1p[:], w1raw[:], 4)
-        for t in range(4):
-            weather_unit(1, t)
-            slope_unit(1, t)
-            nc.gpsimd.tensor_tensor(curved1[0][:, t, :], slope[1][t][:, 0:HALF], wsb[1][:, t, 0:HALF], MULT)
-        for half in range(2):
-            nc.vector.tensor_copy(
-                g1w[1][:, HALF * half : HALF * (half + 1)],
-                t1w[1][:].bitcast(U32).indirect(list1[:, 16 * half : 16 * (half + 1)]),
-            )
-        for t in range(4):
-            nc.gpsimd.tensor_tensor(curved1[1][:, t, :], slope[1][t][:, HALF:S], wsb[1][:, t, HALF:S], MULT)
-        h0 = sb("h0", [P, 4, 4 * P], BF16)
-        h1 = sb("h1", [P, 4, 4 * P], BF16)
-        woc = [keep.tile([P, N], U32, name=f"woc{b}", tag=f"woc{b}", align_bytes=64) for b in range(2)]
-        accs = [[bank(f"acc{u}{v}", [P, 2, HALF], OUT_BANKS[2 * u + v]) for v in range(2)] for u in range(2)]
-
-        def quantize_h1(half):
-            toks = slice(HALF * half, HALF * (half + 1))
-            quantize(hc[1][:, toks], hs[1][:, toks], h1[:, 2 * half : 2 * half + 2, :].rearrange("p q c -> p (q c)"))
-
-        def quantize_wo1(pair):
-            cols = slice(HALF * pair, HALF * (pair + 1))
-            cast_wo(1, HALF * pair, HALF * (pair + 1))
-            quantize(woc[1][:, cols], wos[1][:, cols], woh[1][:, 4 * HALF * pair : 4 * HALF * (pair + 1)])
-
-        def finish(half, pair, copy):
-            out_passes(1, half, pair, accs[half][pair])
-            res = sb(f"res{half}{pair}", [P, 2, HALF], F32)
-            copy(out=res[:], in_=accs[half][pair][:])
-            nc.sync.dma_start(out=out_rows[:, 2 * pair : 2 * pair + 2, HALF * half : HALF * (half + 1)], in_=res[:])
+        def finish(half, side, copy):
+            out_passes(1, half, side, accs[half][side])
+            res = sb(f"res{half}{side}", [P, 2, HALF], F32)
+            copy(out=res[:], in_=accs[half][side][:])
+            nc.sync.dma_start(out=out_rows[:, 2 * side : 2 * side + 2, HALF * half : HALF * (half + 1)], in_=res[:])
 
         for q in range(4):
-            level_unit(0, q, h0[:, q, :], w1sp)
-        level_unit(1, 0, h1[:, 0, :], w1sp)
-        quantize(hc[0][:], hs[0][:], h0[:].rearrange("p q c -> p (q c)"))
-        level_unit(1, 1, h1[:, 1, :], w1sp)
+            level_sum(0, q, h0[:, 4 * P * q : 4 * P * (q + 1)])
         cast_wo(0, 0, N)
-        quantize(woc[0][:], wos[0][:], woh[0][:])
+        quantize(woc[0], wos[0], woh[0], 0, N)
+        h1 = keep.tile([P, 4 * S], BF16, name="h1", tag="woh0", align_bytes=64)
+        level_sum(1, 0, h1[:, 0 : 4 * P])
+        quantize(hc[0], hs[0], h0, 0, S)
+        accs = [[bank(f"acc{u}{v}", [P, 2, HALF], 4 + 2 * u + v) for v in range(2)] for u in range(2)]
         for half in range(2):
-            for pair in range(2):
-                out_passes(0, half, pair, accs[half][pair])
-        level_unit(1, 2, h1[:, 2, :], w1sp)
-        quantize_h1(0)
-        quantize_wo1(0)
-        finish(0, 0, nc.scalar.copy)
-        level_unit(1, 3, h1[:, 3, :], w1sp)
-        quantize_wo1(1)
-        finish(0, 1, nc.scalar.copy)
-        quantize_h1(1)
-        finish(1, 0, nc.vector.tensor_copy)
-        finish(1, 1, nc.scalar.copy)
+            for side in range(2):
+                out_passes(0, half, side, accs[half][side])
+        for q in range(1, 4):
+            level_sum(1, q, h1[:, 4 * P * q : 4 * P * (q + 1)])
+            if q == 2:
+                quantize(hc[1], hs[1], h1, 0, HALF)
+        for side in range(2):
+            cast_wo(1, HALF * side, HALF * (side + 1))
+            quantize(woc[1], wos[1], woh[1], HALF * side, HALF * (side + 1))
+            if side == 0:
+                quantize(hc[1], hs[1], h1, HALF, S)
+            finish(0, side, nc.scalar.copy)
+            finish(1, side, nc.vector.tensor_copy)

@@ -55,7 +55,7 @@ def tile_list_wheat_reaction_norm_kernel(
         g1s = pair("g1s", [P, S], U8)
         g2s = sb("g2s", [P, S], U8)
         g3s = pair("g3s", [P, S], U8)
-        w1raw = sb("w1raw", [P, 2, H // 2], U32)
+        w1raw = pair("w1raw", [P, 2, 256], U32)
         w1p = pair("w1p", [P, 2, 256], U32)
         w1sp = pair("w1sp", [P, 2, 128], U32)
         w3raw = pair("w3raw", [P, 2, 512], U32)
@@ -101,10 +101,10 @@ def tile_list_wheat_reaction_norm_kernel(
         def scale_rows(dram):
             return dram.bitcast(I32).rearrange("a (q r) c -> r q a c", r=4)
 
-        def load_stacked_scales(tile, dram, first=0):
+        def load_stacked_scales(queue, tile, dram, first=0):
             rows = scale_rows(dram)
             for r in range(4):
-                nc.sync.dma_start(out=tile[first + r : P : 32 // dram.shape[0], :].bitcast(I32), in_=rows[r])
+                queue.dma_start(out=tile[first + r : P : 32 // dram.shape[0], :].bitcast(I32), in_=rows[r])
 
         def load_scales(tile, dram):
             rows = scale_rows(dram)
@@ -117,6 +117,9 @@ def tile_list_wheat_reaction_norm_kernel(
         def load_w3(b):
             load(w3raw[b][:], w3_words.rearrange("a p c i -> p a (c i)")[:, :, 2048 * b : 2048 * (b + 1)])
 
+        def load_w1(b):
+            load(w1raw[b][:], w1_words.rearrange("a p c -> p a c")[:, :, 1024 * b : 1024 * (b + 1)])
+
         def load_wo(b):
             rows = wo[512 * b : 512 * (b + 1), :].rearrange("(g t i) n -> t g i n", t=4, i=8)
             for t in range(4):
@@ -125,8 +128,8 @@ def tile_list_wheat_reaction_norm_kernel(
         def gather(dst, window, lst):
             nc.vector.tensor_copy(dst, window.indirect(lst))
 
-        def reorder(dst, src, copy=nc.scalar.copy):
-            copy(
+        def reorder(dst, src):
+            nc.scalar.copy(
                 out=dst.rearrange("p a (t g i) -> p a t g i", t=4, g=16),
                 in_=src.rearrange("p a (g t i) -> p a t g i", t=4, g=16),
             )
@@ -211,18 +214,17 @@ def tile_list_wheat_reaction_norm_kernel(
         load_scales(wsraw, w3_scales)
         load_w2(0)
         nc.sync.dma_start(list2[:], offs2)
-        load_stacked_scales(t2s, tab2_scales, SOIL_PLANE)
+        load_stacked_scales(nc.sync, t2s, tab2_scales, SOIL_PLANE)
         load(t2w[:], words(tab2_words, 0))
         load_w3(1)
-        nc.sync.dma_start(list1[:], offs)
-        load_stacked_scales(t1s, tab_scales)
         load_w2(1)
+        nc.sync.dma_start(list1[:], offs)
         load(t1w[0][:], words(tab_words, 0))
         for b in range(2):
             reorder(w3sp[b][:], wsraw[:, :, 128 * b : 128 * (b + 1)])
         load_scales(wsraw, w1_scales)
-        load(w1raw[:], w1_words.rearrange("a p c -> p a c"))
-        load(t1w[1][:], words(tab_words, 1))
+        load_w1(0)
+        load_stacked_scales(nc.gpsimd, t1s, tab_scales)
 
         gather(g3w[0][:], t3w[0][:], list3[:])
         for a in range(2):
@@ -234,7 +236,6 @@ def tile_list_wheat_reaction_norm_kernel(
         gather(g2s[:], t2s[:], list2[:])
         gather(g2w[:], t2w[:], list2[:])
         quantize(w2c[0], w2s[0], w2h[0], 0, 512)
-        reorder(w3p[1][:], w3raw[1][:], nc.gpsimd.tensor_copy)
         weather_sum(0, 0)
         cvt = bank("cvt", [P, P], 0)
         nc.tensor.transpose(cvt[:], cvrows[:], ident[:])
@@ -244,8 +245,11 @@ def tile_list_wheat_reaction_norm_kernel(
         for t in range(4):
             slope_sum(0, t)
             nc.gpsimd.tensor_tensor(curved0[:, t, :], slope[0][:, t, :], wsb[0][:, t, :], MULT)
+        reorder(w3p[1][:], w3raw[1][:])
         gather(g1s[0][:], t1s[:], list1[:])
+        load(t1w[1][:], words(tab_words, 1))
         nc.sync.dma_start(out=g1s[1][0:112, :].bitcast(I32), in_=g1s[0][16:128, :].bitcast(I32))
+        load_w1(1)
         load_wo(0)
         load_wo(1)
         cast_w2(1)
@@ -259,9 +263,9 @@ def tile_list_wheat_reaction_norm_kernel(
             product(t, 0)
         for b in range(2):
             reorder(w1sp[b][:], wsraw[:, :, 128 * b : 128 * (b + 1)])
-            reorder(w1p[b][:], w1raw[:, :, 256 * b : 256 * (b + 1)])
-        for half in range(2):
-            gather(g1w[1][:, HALF * half : HALF * (half + 1)], t1w[1][:], list1[:, 16 * half : 16 * (half + 1)])
+            reorder(w1p[b][:], w1raw[b][:])
+        gather(g1w[1][:, 0:P], t1w[1][:], list1[:, 0:8])
+        gather(g1w[1][:, P:S], t1w[1][:], list1[:, 8:32])
         for t in range(4):
             product(t, 1)
 
@@ -275,23 +279,24 @@ def tile_list_wheat_reaction_norm_kernel(
 
         for q in range(4):
             level_sum(0, q, h0[:, 4 * P * q : 4 * P * (q + 1)])
+        h1a = sb("h1a", [P, 4 * HALF], BF16)
+        level_sum(1, 0, h1a[:, 0 : 4 * P])
+        quantize(hc[0], hs[0], h0, 0, S)
+        level_sum(1, 1, h1a[:, 4 * P : 8 * P])
         cast_wo(0, 0, N)
         quantize(woc[0], wos[0], woh[0], 0, N)
-        h1 = keep.tile([P, 4 * S], BF16, name="h1", tag="woh0", align_bytes=64)
-        level_sum(1, 0, h1[:, 0 : 4 * P])
-        quantize(hc[0], hs[0], h0, 0, S)
         accs = [[bank(f"acc{u}{v}", [P, 2, HALF], 4 + 2 * u + v) for v in range(2)] for u in range(2)]
         for half in range(2):
             for side in range(2):
                 out_passes(0, half, side, accs[half][side])
-        for q in range(1, 4):
-            level_sum(1, q, h1[:, 4 * P * q : 4 * P * (q + 1)])
-            if q == 2:
-                quantize(hc[1], hs[1], h1, 0, HALF)
+        h1b = keep.tile([P, 4 * N], BF16, name="h1b", tag="woh0", align_bytes=64)
+        level_sum(1, 2, h1b[:, 0 : 4 * P])
+        quantize(hc[1], hs[1], h1a, 0, HALF)
+        level_sum(1, 3, h1b[:, 4 * P : 8 * P])
         for side in range(2):
             cast_wo(1, HALF * side, HALF * (side + 1))
             quantize(woc[1], wos[1], woh[1], HALF * side, HALF * (side + 1))
             if side == 0:
-                quantize(hc[1], hs[1], h1, HALF, S)
+                quantize(hc[1][:, HALF:S], hs[1][:, HALF:S], h1b, 0, HALF)
             finish(0, side, nc.scalar.copy)
             finish(1, side, nc.vector.tensor_copy)

@@ -70,9 +70,9 @@ def tile_list_wheat_reaction_norm_kernel(
         woh = [keep.tile([P, 4 * N], BF16, name=f"woh{b}", tag=f"woh{b}", align_bytes=64) for b in range(2)]
         woc = pair("woc", [P, N], U32)
         wos = pair("wos", [P, N], U8)
-        cvrows = sb("cvrows", [P, P], F32)
+        cvrows = sb("cvrows", [P, 2 * P], F32)
         ident = sb("ident", [P, P], F32)
-        cv = sb("cv", [P, 8], F32)
+        cv = sb("cv", [P, 2, 4], F32)
         wsb = [keep.tile([P, 4, S], F32, name=f"wsb{b}", tag=f"w2raw{b}", align_bytes=64) for b in range(2)]
         slope = pair("slope", [P, 4, S], F32)
         curved0 = sb("curved0", [P, 4, S], F32)
@@ -83,14 +83,10 @@ def tile_list_wheat_reaction_norm_kernel(
         hs = pair("hs", [P, S], U8)
 
         nc.vector.memset(t3s[:].bitcast(I32), 0)
+        nc.gpsimd.memset(cvrows[:], 0.0)
         nc.vector.memset(wsraw[:].bitcast(I32), 0)
         nc.vector.memset(t2s[:].bitcast(I32), 0)
         nc.vector.memset(t1s[:].bitcast(I32), 0)
-        nc.gpsimd.memset(cvrows[:], 0.0)
-        crows = curv.rearrange("(b g t i) -> b t g i", b=2, t=4, i=8)
-        for b in range(2):
-            nc.gpsimd.dma_start(out=cvrows[4 * b : 4 * b + 4, :].rearrange("t (g i) -> t g i", i=8), in_=crows[b])
-        make_identity(nc, ident[:])
 
         def load(tile, src):
             nc.sync.dma_start(out=tile.bitcast(I32), in_=src.bitcast(I32))
@@ -152,6 +148,12 @@ def tile_list_wheat_reaction_norm_kernel(
                 in_=woraw[b][:, :, c0:c1].rearrange("p t (c i) -> p c t i", i=2),
             )
 
+        def cast_wo_on_gpsimd(b, c0, c1):
+            nc.gpsimd.tensor_copy(
+                out=woh[b][:, 4 * c0 : 4 * c1].rearrange("p (c t) -> p c t", t=4),
+                in_=woraw[b][:, :, c0:c1].rearrange("p t c -> p c t"),
+            )
+
         def quantize(codes, scales, values, c0, c1):
             nc.vector.quantize_mx(out=codes[:, c0:c1].bitcast(FP8X4), scales=scales[:, c0:c1], in_=values[:, 4 * c0 : 4 * c1])
 
@@ -172,7 +174,7 @@ def tile_list_wheat_reaction_norm_kernel(
                 out=soil[:], lhsT=w2c[b][:, cols].bitcast(FP8X4), lhsT_scale=w2s[b][:, cols],
                 rhs=g2w[:].bitcast(FP8X4), rhs_scale=g2s[SOIL_PLANE:P, :], start=True, stop=True,
             )
-            nc.vector.scalar_tensor_tensor(slope[b][:, t, :], wsb[b][:, t, :], cv[:, 4 * b + t : 4 * b + t + 1], soil[:], MULT, ADD)
+            nc.vector.scalar_tensor_tensor(slope[b][:, t, :], wsb[b][:, t, :], cv[:, b, t : t + 1], soil[:], MULT, ADD)
 
         def product(t, half):
             toks = slice(HALF * half, HALF * (half + 1))
@@ -206,6 +208,10 @@ def tile_list_wheat_reaction_norm_kernel(
                     start=(b == 0 and k == 0), stop=(b == 1 and k == 1),
                 )
 
+        nc.gpsimd.dma_start(
+            out=cvrows[0:4, :].rearrange("t (g i) -> t g i", i=8), in_=curv.rearrange("(g t i) -> t g i", t=4, i=8)
+        )
+        make_identity(nc, ident[:])
         nc.sync.dma_start(list3[:], offs3)
         load(t3w[0][:], tab3_words[0])
         load_scales(t3s, tab3_scales)
@@ -217,14 +223,14 @@ def tile_list_wheat_reaction_norm_kernel(
         load_stacked_scales(nc.sync, t2s, tab2_scales, SOIL_PLANE)
         load(t2w[:], words(tab2_words, 0))
         load_w3(1)
-        load_w2(1)
         nc.sync.dma_start(list1[:], offs)
+        load_stacked_scales(nc.sync, t1s, tab_scales)
+        load_w2(1)
         load(t1w[0][:], words(tab_words, 0))
         for b in range(2):
             reorder(w3sp[b][:], wsraw[:, :, 128 * b : 128 * (b + 1)])
         load_scales(wsraw, w1_scales)
         load_w1(0)
-        load_stacked_scales(nc.gpsimd, t1s, tab_scales)
 
         gather(g3w[0][:], t3w[0][:], list3[:])
         for a in range(2):
@@ -237,9 +243,10 @@ def tile_list_wheat_reaction_norm_kernel(
         gather(g2w[:], t2w[:], list2[:])
         quantize(w2c[0], w2s[0], w2h[0], 0, 512)
         weather_sum(0, 0)
-        cvt = bank("cvt", [P, P], 0)
-        nc.tensor.transpose(cvt[:], cvrows[:], ident[:])
-        nc.scalar.copy(out=cv[:], in_=cvt[:, 0:8])
+        cvt = bank("cvt", [P, 2, P], 0)
+        for b in range(2):
+            nc.tensor.transpose(cvt[:, b, :], cvrows[:, P * b : P * (b + 1)], ident[:])
+        nc.scalar.copy(out=cv[:], in_=cvt[:, :, 0:4])
         for t in range(1, 4):
             weather_sum(0, t)
         for t in range(4):
@@ -289,14 +296,17 @@ def tile_list_wheat_reaction_norm_kernel(
         for half in range(2):
             for side in range(2):
                 out_passes(0, half, side, accs[half][side])
-        h1b = keep.tile([P, 4 * N], BF16, name="h1b", tag="woh0", align_bytes=64)
-        level_sum(1, 2, h1b[:, 0 : 4 * P])
+        h12 = sb("h12", [P, 4 * P], BF16)
+        level_sum(1, 2, h12[:])
         quantize(hc[1], hs[1], h1a, 0, HALF)
-        level_sum(1, 3, h1b[:, 4 * P : 8 * P])
+        quantize(hc[1][:, 2 * P : 3 * P], hs[1][:, 2 * P : 3 * P], h12, 0, P)
+        h13 = keep.tile([P, 4 * P], BF16, name="h13", tag="woh0", align_bytes=64)
+        level_sum(1, 3, h13[:])
+        cast_wo_on_gpsimd(1, 3 * P, N)
         for side in range(2):
-            cast_wo(1, HALF * side, HALF * (side + 1))
+            cast_wo(1, HALF * side, HALF * side + (HALF, P)[side])
             quantize(woc[1], wos[1], woh[1], HALF * side, HALF * (side + 1))
             if side == 0:
-                quantize(hc[1][:, HALF:S], hs[1][:, HALF:S], h1b, 0, HALF)
+                quantize(hc[1][:, 3 * P : S], hs[1][:, 3 * P : S], h13, 0, P)
             finish(0, side, nc.scalar.copy)
             finish(1, side, nc.vector.tensor_copy)

@@ -66,7 +66,7 @@ def tile_list_wheat_reaction_norm_kernel(
         w2h = pair("w2h", [P, 2048], BF16)
         w2c = [keep.tile([P, 512], U32, name=f"w2c{b}", tag=("t2w", "w2c1")[b], align_bytes=64) for b in range(2)]
         w2s = pair("w2s", [P, 512], U8)
-        woraw = pair("woraw", [P, 4, N], F32)
+        woraw = [keep.tile([P, 4, N], F32, name=f"woraw{b}", tag=f"woraw{b}", align_bytes=64) for b in range(2)]
         woh = [keep.tile([P, 4 * N], BF16, name=f"woh{b}", tag=f"woh{b}", align_bytes=64) for b in range(2)]
         woc = pair("woc", [P, N], U32)
         wos = pair("wos", [P, N], U8)
@@ -79,10 +79,10 @@ def tile_list_wheat_reaction_norm_kernel(
         curved1 = pair("curved1", [P, 4, HALF], F32)
         curved = [[curved0[:, :, 0:HALF], curved0[:, :, HALF:S]], [tile[:] for tile in curved1]]
         h0 = sb("h0", [P, 4 * S], BF16)
-        hc = pair("hc", [P, S], U32)
+        hc = [keep.tile([P, S], U32, name=f"hc{b}", tag=("hc0", "woraw0")[b], align_bytes=64) for b in range(2)]
         hs = pair("hs", [P, S], U8)
 
-        nc.vector.memset(t3s[:].bitcast(I32), 0)
+        nc.gpsimd.memset(t3s[:].bitcast(I32), 0)
         nc.gpsimd.memset(cvrows[:], 0.0)
         nc.vector.memset(wsraw[:].bitcast(I32), 0)
         nc.vector.memset(t2s[:].bitcast(I32), 0)
@@ -130,8 +130,8 @@ def tile_list_wheat_reaction_norm_kernel(
                 in_=src.rearrange("p a (g t i) -> p a t g i", t=4, g=16),
             )
 
-        def reorder_w3_slot(b, t):
-            nc.scalar.copy(
+        def reorder_w3_slot(b, t, copy):
+            copy(
                 out=w3p[b][:, :, P * t : P * (t + 1)].rearrange("p a (g i) -> p a g i", g=16),
                 in_=w3raw[b][:].rearrange("p a (g t i) -> p a t g i", t=4, g=16)[:, :, t],
             )
@@ -237,11 +237,14 @@ def tile_list_wheat_reaction_norm_kernel(
             gather(g3s[a][:], t3s[:, a, :], list3[:])
         gather(g3w[1][:], t3w[1][:], list3[:])
         for t in range(4):
-            reorder_w3_slot(0, t)
+            reorder_w3_slot(0, t, nc.scalar.copy)
         cast_w2(0)
         gather(g2s[:], t2s[:], list2[:])
         gather(g2w[:], t2w[:], list2[:])
-        quantize(w2c[0], w2s[0], w2h[0], 0, 512)
+        for u in range(2):
+            quantize(w2c[0], w2s[0], w2h[0], HALF * u, HALF * (u + 1))
+        for t in range(4):
+            reorder_w3_slot(1, t, nc.gpsimd.tensor_copy)
         weather_sum(0, 0)
         cvt = bank("cvt", [P, 2, P], 0)
         for b in range(2):
@@ -252,7 +255,6 @@ def tile_list_wheat_reaction_norm_kernel(
         for t in range(4):
             slope_sum(0, t)
             nc.gpsimd.tensor_tensor(curved0[:, t, :], slope[0][:, t, :], wsb[0][:, t, :], MULT)
-        reorder(w3p[1][:], w3raw[1][:])
         gather(g1s[0][:], t1s[:], list1[:])
         load(t1w[1][:], words(tab_words, 1))
         nc.sync.dma_start(out=g1s[1][0:112, :].bitcast(I32), in_=g1s[0][16:128, :].bitcast(I32))
@@ -296,17 +298,15 @@ def tile_list_wheat_reaction_norm_kernel(
         for half in range(2):
             for side in range(2):
                 out_passes(0, half, side, accs[half][side])
-        h12 = sb("h12", [P, 4 * P], BF16)
-        level_sum(1, 2, h12[:])
+        h1b = keep.tile([P, 4 * N], BF16, name="h1b", tag="woh0", align_bytes=64)
+        level_sum(1, 2, h1b[:, 0 : 4 * P])
         quantize(hc[1], hs[1], h1a, 0, HALF)
-        quantize(hc[1][:, 2 * P : 3 * P], hs[1][:, 2 * P : 3 * P], h12, 0, P)
-        h13 = keep.tile([P, 4 * P], BF16, name="h13", tag="woh0", align_bytes=64)
-        level_sum(1, 3, h13[:])
+        level_sum(1, 3, h1b[:, 4 * P : 8 * P])
         cast_wo_on_gpsimd(1, 3 * P, N)
         for side in range(2):
             cast_wo(1, HALF * side, HALF * side + (HALF, P)[side])
             quantize(woc[1], wos[1], woh[1], HALF * side, HALF * (side + 1))
             if side == 0:
-                quantize(hc[1][:, 3 * P : S], hs[1][:, 3 * P : S], h13, 0, P)
+                quantize(hc[1][:, HALF:S], hs[1][:, HALF:S], h1b, 0, HALF)
             finish(0, side, nc.scalar.copy)
             finish(1, side, nc.vector.tensor_copy)

@@ -182,7 +182,7 @@ def tile_list_wheat_reaction_norm_kernel(
 
         def level_sum(b, q, dst):
             toks = slice(P * q, P * (q + 1))
-            line = bank("line", [P, 4, P], q)
+            line = bank("line", [P, 4, P], q % (4, 2)[b])
             for a in range(2):
                 for t in range(4):
                     nc.tensor.matmul_mx(
@@ -292,21 +292,23 @@ def tile_list_wheat_reaction_norm_kernel(
         level_sum(1, 0, h1a[:, 0 : 4 * P])
         quantize(hc[0], hs[0], h0, 0, S)
         level_sum(1, 1, h1a[:, 4 * P : 8 * P])
+        h12 = sb("h12", [P, 4 * P], BF16)
+        level_sum(1, 2, h12[:])
         cast_wo(0, 0, N)
         quantize(woc[0], wos[0], woh[0], 0, N)
         accs = [[bank(f"acc{u}{v}", [P, 2, HALF], 4 + 2 * u + v) for v in range(2)] for u in range(2)]
         for half in range(2):
             for side in range(2):
                 out_passes(0, half, side, accs[half][side])
-        h1b = keep.tile([P, 4 * N], BF16, name="h1b", tag="woh0", align_bytes=64)
-        level_sum(1, 2, h1b[:, 0 : 4 * P])
         quantize(hc[1], hs[1], h1a, 0, HALF)
-        level_sum(1, 3, h1b[:, 4 * P : 8 * P])
+        quantize(hc[1][:, 2 * P : 3 * P], hs[1][:, 2 * P : 3 * P], h12, 0, P)
+        h13 = keep.tile([P, 4 * P], BF16, name="h13", tag="woh0", align_bytes=64)
+        level_sum(1, 3, h13[:])
         cast_wo_on_gpsimd(1, 3 * P, N)
         for side in range(2):
             cast_wo(1, HALF * side, HALF * side + (HALF, P)[side])
             quantize(woc[1], wos[1], woh[1], HALF * side, HALF * (side + 1))
             if side == 0:
-                quantize(hc[1][:, HALF:S], hs[1][:, HALF:S], h1b, 0, HALF)
+                quantize(hc[1][:, 3 * P : S], hs[1][:, 3 * P : S], h13, 0, P)
             finish(0, side, nc.scalar.copy)
             finish(1, side, nc.vector.tensor_copy)

from contextlib import ExitStack

import concourse.mybir as mybir
from concourse.masks import make_identity

K, K2, K3, H, N, T, T2, T3, S = 1024, 512, 1024, 1024, 512, 2048, 1024, 1024, 512
FLOPS = 2 * S * (H * (K + K2 + K3) + N * H)

F32 = mybir.dt.float32
BF16 = mybir.dt.bfloat16
I32 = mybir.dt.int32
U32 = mybir.dt.uint32
U16 = mybir.dt.uint16
U8 = mybir.dt.uint8
FP8X4 = mybir.dt.float8_e4m3fn_x4
FP4X4 = mybir.dt.float4_e2m1fn_x4
MULT = mybir.AluOpType.mult
ADD = mybir.AluOpType.add

P = 128
HALF = 256
SOIL_PLANE = 4


def tile_list_wheat_reaction_norm_kernel(
    tc, tab_words, tab_scales, tab2_words, tab2_scales, tab3_words, tab3_scales, offs, offs2, offs3,
    w1_words, w1_scales, w2, w3_words, w3_scales, curv, wo, out,
):
    nc = tc.nc
    with ExitStack() as ctx:
        keep = ctx.enter_context(tc.tile_pool(name="keep", bufs=1))
        psum = ctx.enter_context(tc.psum_pool(name="psum", bufs=1))

        def sb(name, shape, dtype):
            return keep.tile(shape, dtype, name=name, align_bytes=64)

        def pair(name, shape, dtype):
            return [sb(f"{name}{k}", shape, dtype) for k in range(2)]

        def bank(name, shape, index):
            return psum.tile(shape, F32, name=name, tag=f"bank{index}")

        list1 = sb("list1", [P, S // 16], U16)
        list2 = sb("list2", [P, S // 16], U16)
        list3 = sb("list3", [P, S // 16], U16)
        t1w = pair("t1w", [P, T], U32)
        t2w = keep.tile([P, T2], U32, name="t2w", tag="t2w", align_bytes=64)
        t3w = pair("t3w", [P, T3], U16)
        t1s = sb("t1s", [P, T], U8)
        t2s = sb("t2s", [P, T2], U8)
        t3s = sb("t3s", [P, 2, T3], U8)
        g1w = pair("g1w", [P, S], U32)
        g2w = sb("g2w", [P, S], U32)
        g3w = pair("g3w", [P, S], U16)
        g1s = pair("g1s", [P, S], U8)
        g2s = sb("g2s", [P, S], U8)
        g3s = pair("g3s", [P, S], U8)
        w1raw = pair("w1raw", [P, 2, 256], U32)
        w1p = pair("w1p", [P, 2, 256], U32)
        w1sp = pair("w1sp", [P, 2, 128], U32)
        w3raw = pair("w3raw", [P, 2, 512], U32)
        w3p = pair("w3p", [P, 2, 512], U32)
        wsraw = sb("wsraw", [P, 2, H // 4], U32)
        w3sp = pair("w3sp", [P, 2, 128], U32)
        w2raw = [keep.tile([P, 4, 512], F32, name=f"w2raw{b}", tag=f"w2raw{b}", align_bytes=64) for b in range(2)]
        w2h = pair("w2h", [P, 2048], BF16)
        w2c = [keep.tile([P, 512], U32, name=f"w2c{b}", tag=("t2w", "w2c1")[b], align_bytes=64) for b in range(2)]
        w2s = pair("w2s", [P, 512], U8)
        woraw = [keep.tile([P, 4, N], F32, name=f"woraw{b}", tag=f"woraw{b}", align_bytes=64) for b in range(2)]
        woh = [keep.tile([P, 4 * N], BF16, name=f"woh{b}", tag=f"woh{b}", align_bytes=64) for b in range(2)]
        woc = pair("woc", [P, N], U32)
        wos = pair("wos", [P, N], U8)
        cvrows = sb("cvrows", [P, 2 * P], F32)
        ident = sb("ident", [P, P], F32)
        cv = sb("cv", [P, 2, 4], F32)
        wsb = [keep.tile([P, 4, S], F32, name=f"wsb{b}", tag=f"w2raw{b}", align_bytes=64) for b in range(2)]
        slope = pair("slope", [P, 4, S], F32)
        curved0 = sb("curved0", [P, 4, S], F32)
        curved1 = pair("curved1", [P, 4, HALF], F32)
        curved = [[curved0[:, :, 0:HALF], curved0[:, :, HALF:S]], [tile[:] for tile in curved1]]
        h0 = sb("h0", [P, 4 * S], BF16)
        hc = [keep.tile([P, S], U32, name=f"hc{b}", tag=("hc0", "woraw0")[b], align_bytes=64) for b in range(2)]
        hs = pair("hs", [P, S], U8)

        nc.gpsimd.memset(t3s[:].bitcast(I32), 0)
        nc.gpsimd.memset(cvrows[:], 0.0)
        nc.vector.memset(wsraw[:].bitcast(I32), 0)
        nc.vector.memset(t2s[:].bitcast(I32), 0)
        nc.vector.memset(t1s[:].bitcast(I32), 0)

        def load(tile, src):
            nc.sync.dma_start(out=tile.bitcast(I32), in_=src.bitcast(I32))

        def words(dram, a):
            return dram[a].rearrange("p c i -> p (c i)")

        def scale_rows(dram):
            return dram.bitcast(I32).rearrange("a (q r) c -> r q a c", r=4)

        def load_stacked_scales(queue, tile, dram, first=0):
            rows = scale_rows(dram)
            for r in range(4):
                queue.dma_start(out=tile[first + r : P : 32 // dram.shape[0], :].bitcast(I32), in_=rows[r])

        def load_scales(tile, dram):
            rows = scale_rows(dram)
            for r in range(4):
                nc.sync.dma_start(out=tile[r:P:32, :, :].bitcast(I32), in_=rows[r])

        def load_w2(b):
            nc.sync.dma_start(out=w2raw[b][:], in_=w2[:, 512 * b : 512 * (b + 1)].rearrange("(p j) c -> p j c", j=4))

        def load_w3(b):
            load(w3raw[b][:], w3_words.rearrange("a p c i -> p a (c i)")[:, :, 2048 * b : 2048 * (b + 1)])

        def load_w1(b):
            load(w1raw[b][:], w1_words.rearrange("a p c -> p a c")[:, :, 1024 * b : 1024 * (b + 1)])

        def load_wo(b):
            rows = wo[512 * b : 512 * (b + 1), :].rearrange("(g t i) n -> t g i n", t=4, i=8)
            for t in range(4):
                nc.sync.dma_start(out=woraw[b][:, t, :], in_=rows[t])

        def gather(dst, window, lst):
            nc.vector.tensor_copy(dst, window.indirect(lst))

        def reorder(dst, src):
            nc.scalar.copy(
                out=dst.rearrange("p a (t g i) -> p a t g i", t=4, g=16),
                in_=src.rearrange("p a (g t i) -> p a t g i", t=4, g=16),
            )

        def reorder_w3_slot(b, t, copy):
            copy(
                out=w3p[b][:, :, P * t : P * (t + 1)].rearrange("p a (g i) -> p a g i", g=16),
                in_=w3raw[b][:].rearrange("p a (g t i) -> p a t g i", t=4, g=16)[:, :, t],
            )

        def cast_w2(b):
            dst = w2h[b][:].rearrange("p (t g u i j) -> p t g u j i", t=4, g=16, u=4, i=2)
            src = w2raw[b][:].rearrange("p j (g t u i) -> p t g u j i", t=4, u=4, i=2)
            for t in range(4):
                nc.scalar.copy(out=dst[:, t], in_=src[:, t])

        def cast_wo(b, c0, c1):
            nc.scalar.copy(
                out=woh[b][:, 4 * c0 : 4 * c1].rearrange("p (c i t) -> p c t i", i=2, t=4),
                in_=woraw[b][:, :, c0:c1].rearrange("p t (c i) -> p c t i", i=2),
            )

        def cast_wo_on_gpsimd(b, c0, c1):
            nc.gpsimd.tensor_copy(
                out=woh[b][:, 4 * c0 : 4 * c1].rearrange("p (c t) -> p c t", t=4),
                in_=woraw[b][:, :, c0:c1].rearrange("p t c -> p c t"),
            )

        def quantize(codes, scales, values, c0, c1):
            nc.vector.quantize_mx(out=codes[:, c0:c1].bitcast(FP8X4), scales=scales[:, c0:c1], in_=values[:, 4 * c0 : 4 * c1])

        def weather_sum(b, t):
            cols = slice(P * t, P * (t + 1))
            weather = bank("weather", [P, S], t)
            for a in range(2):
                nc.tensor.matmul_mx(
                    out=weather[:], lhsT=w3p[b][:, a, cols].bitcast(FP8X4), lhsT_scale=w3sp[b][:, a, :].bitcast(U8)[:, cols],
                    rhs=g3w[a][:].bitcast(FP4X4), rhs_scale=g3s[a][:], start=(a == 0), stop=(a == 1),
                )
            nc.scalar.copy(out=wsb[b][:, t, :], in_=weather[:])

        def slope_sum(b, t):
            cols = slice(P * t, P * (t + 1))
            soil = bank("soil", [P, S], 4 + t)
            nc.tensor.matmul_mx(
                out=soil[:], lhsT=w2c[b][:, cols].bitcast(FP8X4), lhsT_scale=w2s[b][:, cols],
                rhs=g2w[:].bitcast(FP8X4), rhs_scale=g2s[SOIL_PLANE:P, :], start=True, stop=True,
            )
            nc.vector.scalar_tensor_tensor(slope[b][:, t, :], wsb[b][:, t, :], cv[:, b, t : t + 1], soil[:], MULT, ADD)

        def product(t, half):
            toks = slice(HALF * half, HALF * (half + 1))
            nc.gpsimd.tensor_tensor(curved1[half][:, t, :], slope[1][:, t, toks], wsb[1][:, t, toks], MULT)

        def level_sum(b, q, dst):
            toks = slice(P * q, P * (q + 1))
            line = bank("line", [P, 4, P], q % (4, 2)[b])
            for a in range(2):
                for t in range(4):
                    nc.tensor.matmul_mx(
                        out=line[:, t, :], lhsT=w1p[b][:, a, 64 * t : 64 * (t + 1)].bitcast(FP4X4),
                        lhsT_scale=w1sp[b][:, a, :].bitcast(U8)[:, P * t : P * (t + 1)],
                        rhs=g1w[a][:, toks].bitcast(FP8X4), rhs_scale=g1s[a][:, toks],
                        start=(a == 0 and t == 0), stop=(a == 1 and t == 3),
                    )
            nc.vector.tensor_tensor(
                dst.rearrange("p (c i t) -> p c t i", i=2, t=4),
                line[:].rearrange("p t (c i) -> p c t i", i=2),
                curved[b][q // 2][:, :, P * (q % 2) : P * (q % 2 + 1)].rearrange("p t (c i) -> p c t i", i=2),
                ADD,
            )

        def out_passes(b, half, side, acc):
            toks = slice(HALF * half, HALF * (half + 1))
            for k in range(2):
                cols = slice(P * (2 * side + k), P * (2 * side + k + 1))
                nc.tensor.matmul_mx(
                    out=acc[:, k, :], lhsT=woc[b][:, cols].bitcast(FP8X4), lhsT_scale=wos[b][:, cols],
                    rhs=hc[b][:, toks].bitcast(FP8X4), rhs_scale=hs[b][:, toks],
                    start=(b == 0 and k == 0), stop=(b == 1 and k == 1),
                )

        nc.gpsimd.dma_start(
            out=cvrows[0:4, :].rearrange("t (g i) -> t g i", i=8), in_=curv.rearrange("(g t i) -> t g i", t=4, i=8)
        )
        make_identity(nc, ident[:])
        nc.sync.dma_start(list3[:], offs3)
        load(t3w[0][:], tab3_words[0])
        load_scales(t3s, tab3_scales)
        load(t3w[1][:], tab3_words[1])
        load_w3(0)
        load_scales(wsraw, w3_scales)
        load_w2(0)
        nc.sync.dma_start(list2[:], offs2)
        load_stacked_scales(nc.sync, t2s, tab2_scales, SOIL_PLANE)
        load(t2w[:], words(tab2_words, 0))
        load_w3(1)
        nc.sync.dma_start(list1[:], offs)
        load_stacked_scales(nc.sync, t1s, tab_scales)
        load_w2(1)
        load(t1w[0][:], words(tab_words, 0))
        for b in range(2):
            reorder(w3sp[b][:], wsraw[:, :, 128 * b : 128 * (b + 1)])
        load_scales(wsraw, w1_scales)
        load_w1(0)

        gather(g3w[0][:], t3w[0][:], list3[:])
        for a in range(2):
            gather(g3s[a][:], t3s[:, a, :], list3[:])
        gather(g3w[1][:], t3w[1][:], list3[:])
        for t in range(4):
            reorder_w3_slot(0, t, nc.scalar.copy)
        cast_w2(0)
        gather(g2s[:], t2s[:], list2[:])
        gather(g2w[:], t2w[:], list2[:])
        for u in range(2):
            quantize(w2c[0], w2s[0], w2h[0], HALF * u, HALF * (u + 1))
        for t in range(4):
            reorder_w3_slot(1, t, nc.gpsimd.tensor_copy)
        weather_sum(0, 0)
        cvt = bank("cvt", [P, 2, P], 0)
        for b in range(2):
            nc.tensor.transpose(cvt[:, b, :], cvrows[:, P * b : P * (b + 1)], ident[:])
        nc.scalar.copy(out=cv[:], in_=cvt[:, :, 0:4])
        for t in range(1, 4):
            weather_sum(0, t)
        for t in range(4):
            slope_sum(0, t)
            nc.gpsimd.tensor_tensor(curved0[:, t, :], slope[0][:, t, :], wsb[0][:, t, :], MULT)
        gather(g1s[0][:], t1s[:], list1[:])
        load(t1w[1][:], words(tab_words, 1))
        nc.sync.dma_start(out=g1s[1][0:112, :].bitcast(I32), in_=g1s[0][16:128, :].bitcast(I32))
        load_w1(1)
        load_wo(0)
        load_wo(1)
        cast_w2(1)
        for u in range(2):
            quantize(w2c[1], w2s[1], w2h[1], HALF * u, HALF * (u + 1))
        gather(g1w[0][:], t1w[0][:], list1[:])
        for t in range(4):
            weather_sum(1, t)
        for t in range(4):
            slope_sum(1, t)
            product(t, 0)
        for b in range(2):
            reorder(w1sp[b][:], wsraw[:, :, 128 * b : 128 * (b + 1)])
            reorder(w1p[b][:], w1raw[b][:])
        gather(g1w[1][:, 0:P], t1w[1][:], list1[:, 0:8])
        gather(g1w[1][:, P:S], t1w[1][:], list1[:, 8:32])
        for t in range(4):
            product(t, 1)

        out_rows = out.rearrange("(m p) j -> p m j", p=P)

        def finish(half, side, copy):
            out_passes(1, half, side, accs[half][side])
            res = sb(f"res{half}{side}", [P, 2, HALF], F32)
            copy(out=res[:], in_=accs[half][side][:])
            nc.sync.dma_start(out=out_rows[:, 2 * side : 2 * side + 2, HALF * half : HALF * (half + 1)], in_=res[:])

        for q in range(4):
            level_sum(0, q, h0[:, 4 * P * q : 4 * P * (q + 1)])
        h1a = sb("h1a", [P, 4 * HALF], BF16)
        level_sum(1, 0, h1a[:, 0 : 4 * P])
        quantize(hc[0], hs[0], h0, 0, S)
        level_sum(1, 1, h1a[:, 4 * P : 8 * P])
        h12 = sb("h12", [P, 4 * P], BF16)
        level_sum(1, 2, h12[:])
        cast_wo(0, 0, N)
        quantize(woc[0], wos[0], woh[0], 0, N)
        accs = [[bank(f"acc{u}{v}", [P, 2, HALF], 4 + 2 * u + v) for v in range(2)] for u in range(2)]
        for half in range(2):
            for side in range(2):
                out_passes(0, half, side, accs[half][side])
        quantize(hc[1], hs[1], h1a, 0, HALF)
        quantize(hc[1][:, 2 * P : 3 * P], hs[1][:, 2 * P : 3 * P], h12, 0, P)
        h13 = keep.tile([P, 4 * P], BF16, name="h13", tag="woh0", align_bytes=64)
        level_sum(1, 3, h13[:])
        cast_wo_on_gpsimd(1, 3 * P, N)
        for side in range(2):
            cast_wo(1, HALF * side, HALF * side + (HALF, P)[side])
            quantize(woc[1], wos[1], woh[1], HALF * side, HALF * (side + 1))
            if side == 0:
                quantize(hc[1][:, 3 * P : S], hs[1][:, 3 * P : S], h13, 0, P)
            finish(0, side, nc.scalar.copy)
            finish(1, side, nc.vector.tensor_copy)
